import numpy as np, ml_dtypes
CORES = [24,25,26,27,28,29,30,31]
N = 8
import mx_ref
BF = ml_dtypes.bfloat16
def gcols(t, e):
    v = np.concatenate([t.reshape(8, 16, -1, 4), np.zeros((8, 16, 1, 4), BF)], axis=2)
    return np.ascontiguousarray(np.stack([v[g][:, e[g]] for g in range(8)])).reshape(128, -1)
def tile(rs):
    return np.stack(rs, axis=2).reshape(128, -1).astype(BF)
def pick(q, e):
    c = np.concatenate([q[0].reshape(128, -1, 4), np.zeros((128, 1, 4), np.uint8)], axis=1); s = np.concatenate([q[1], np.ones((16, 1), np.uint8)], axis=1)
    return (np.ascontiguousarray(c[:, e].reshape(128, -1)), np.ascontiguousarray(s[:, e]))
def join(*qs):
    return (np.concatenate([q[0] for q in qs], axis=1), np.concatenate([q[1] for q in qs], axis=1))
def put(q, e, v):
    c, s = q[0].reshape(128, -1, 4).copy(), q[1].copy(); c[:, e] = v[0].reshape(128, -1, 4); s[:, e] = v[1]
    return (c.reshape(128, -1), s)
def pk(c, s):
    return (np.ascontiguousarray(c), mx_ref.live(s))
def emit(q):
    return q[0], q[1]
def packed(v, rng):
    q = [mx_ref.quantize(np.ascontiguousarray(v[r])) for r in range(N)]
    return np.stack([a for a, b in q]), np.stack([mx_ref.plane(b, rng) for a, b in q])
def values_of_codes():
    e, c = np.zeros((128, 128, 4), np.float32), np.zeros((128, 2, 4), np.uint8)
    e[np.arange(128), np.arange(128), 0] = 1
    c[:127, :, 0] = np.arange(256).reshape(2, 128).T[:127]
    return mx_ref.matmul(mx_ref.quantize(e.reshape(128, 512).astype(BF)), (c.reshape(128, 8), np.full((16, 2), 127, np.uint8))).T.reshape(-1).astype(np.float64)
CODE_VALUE, SCALE_VALUE = values_of_codes(), 2.0 ** (np.arange(256) - 127.0)
def decode(q):
    return (CODE_VALUE[q[0]].reshape(16, 8, -1, 4) * SCALE_VALUE[q[1]][:, None, :, None] + 0.0).reshape(128, -1).astype(np.float32)
def f(rng, *shape):
    return mx_ref.flush((rng.standard_normal(shape, dtype=np.float32) * np.exp2(rng.integers(-2, 3, shape[:-1] + (1,)))).astype(BF))
def wide(rng, *shape, cols=0):
    v = rng.standard_normal(shape, dtype=np.float32) * np.exp2(rng.integers(-12, 13, shape)).astype(np.float32)
    if cols: v *= np.repeat(np.exp2(rng.integers(-cols, cols + 1, shape[:-2] + (1, shape[-1] // 4))) * (rng.random(shape[:-2] + (1, shape[-1] // 4)) > 0.0625), 4, axis=-1).astype(np.float32)
    return mx_ref.flush(v.astype(BF))
J, K, R = 8, 4, 3
def cycle(t, o):
    i = np.arange(len(t))
    a, b = o[:, 0], o[:, 1]
    c = np.where(t[i, a, b] == o[:, 2], o[:, 3], o[:, 2])
    m = np.zeros((len(t), 16), bool)
    for k in range(6):
        m[i, c] = True
        c = t[i, a, c]
        m[i, c] = True
        c = t[i, b, c]
    return m
def switched(t, o):
    i = np.arange(len(t))
    a, b = o[:, 0], o[:, 1]
    m = cycle(t, o)
    inside = m[:, :, None] & m[:, None, :]
    aa, bb = a[:, None, None], b[:, None, None]
    new = np.where(inside & (t == aa), bb, np.where(inside & (t == bb), aa, t))
    ra, rb = np.where(m, t[i, b], t[i, a]), np.where(m, t[i, a], t[i, b])
    new[i, a] = ra
    new[i, :, a] = ra
    new[i, b] = rb
    new[i, :, b] = rb
    return new
def numbered(e):
    return (e.reshape(N, 8, 16, J).transpose(0, 1, 3, 2) + 16 * np.arange(16)).reshape(N, 8, 16 * J)
FIELD = (((np.arange(16) + 1) % 16)[:, None] ^ ((np.arange(16) + 1) % 16)[None, :]) + 15
FIELD = FIELD % 16
def orders(rng, n):
    return np.argsort(rng.random((n, 15)), axis=1)
def renamed(rng, t):
    n = len(t)
    s = np.concatenate([orders(rng, n), np.full((n, 1), 15)], axis=1)
    k = np.argsort(s, axis=1)
    i = np.arange(n)[:, None, None]
    return s[i, t[i, k[:, :, None], k[:, None, :]]]
def systems(rng):
    t = renamed(rng, np.stack([FIELD] * (N * 128)))
    for k in range(16): t = switched(t, orders(rng, N * 128))
    return t
def stored(t):
    return t.astype(np.int32).reshape(N, 128, 256)
def big(v):
    v = v.astype(np.float32)
    v[np.abs(v) < np.float32(2.0 ** -16)] = 0
    return v.astype(BF)
def odd(rng):
    s = (N, 8, 8, 16, 16, 4)
    k = rng.integers(8, 15, s)
    k[:, :, 1, :, :, 0] = 13 + k[:, :, 1, :, :, 0] % 2
    v = (1.0 + (2 * rng.integers(0, 64, s) + 1) * 2.0 ** -7) * 2.0 ** -k.astype(float)
    v[:, :, 0, :, :, 0] = 1.96875
    return (v * (rng.integers(0, 2, s) * 2.0 - 1.0)).astype(np.float32).astype(BF)
def numbers_of(rng):
    return {"x": big(f(rng, N, 128, 1024)), "u": np.array(f(rng, N, 128, 512)), "v": np.array(f(rng, N, 128, 512))}
def weights(rng, still=[]):
    w = big(f(rng, N, 128, 2048)).reshape(N, 8, 16, 4, 8, 16, 4)
    for i in still:
        w[:, :, i] = 0
        w[:, :, :, :, :, i] = 0
    c, p = packed(w.reshape(N, 128, 2048), rng)
    return {"wc": c, "ws": p}
def setup_inputs(rng):
    return {**numbers_of(rng), "tri": stored(systems(rng)), **weights(rng)}
def setup_inputs_ties(rng):
    d = numbers_of(rng)
    x = d["x"].reshape(N, 8, 16, 16, 16, 4)
    k = rng.integers(0, 3, (N, 8, 16, 16)) - 4 * rng.integers(0, 2, (N, 8, 16, 1))
    k = np.where(rng.random((N, 8, 16, 1)) < 0.25, k[:, :, :, :1], k)
    x[:, :, 0] = 0
    x[:, :, 0, :, :, 0] = k.astype(np.float32).astype(BF)
    x[:, :, 8:] = odd(rng)
    u = d["u"].reshape(N, 128, 128, 4)
    u[:, :, ::16] = 0
    o = rng.permutation(N)
    for r in range(N):
        e = 16 * rng.permutation(8)[:2]
        for h in range(0, 128, 16): u[r, h + 9 if h in e else h, h, 0] = 0.0 if r == o[0] else -1.0 if r == o[1] else 1.0
    return {"x": x.reshape(N, 128, 1024), "u": u.reshape(N, 128, 512), "v": d["v"], "tri": stored(systems(rng)), **weights(rng, [0])}
def setup_inputs_near(rng):
    d = numbers_of(rng)
    x = d["x"].astype(np.float32).reshape(N, 8, 16, 16, 16, 4)
    x[:, :, 0] = 0
    x[:, :, 8:] = 0
    x[:, :, 0, :, :, 0] = rng.integers(0, 2, (N, 8, 16, 1)) * 2.0 - 1.0
    s = rng.integers(0, 16, (N, 8, 16, 16))
    x[:, :, 8] = ((s[..., None] >> np.arange(4)) & 1) * np.exp2(np.arange(4) - 23.0)
    u = d["u"].reshape(N, 128, 128, 4)
    u[:, :, ::16] = 0
    o = rng.permutation(N) % 4
    for r in range(N):
        k = 1.0 if o[r] == 0 else 2.0 ** -30
        if o[r] < 2: x[r, :, 11, :, :, 0] = 2.0 ** -10
        if o[r] == 2:
            a = np.zeros((8, 16, 16), np.float32)
            e = np.argsort(rng.random((8, 16, 15)), axis=2)
            np.put_along_axis(a, e[:, :, :1], 1.0, axis=2)
            np.put_along_axis(a, e[:, :, 1:2], -1.0, axis=2)
            x[r, :, 0, :, :, 0] = a
        if o[r] == 3:
            x[r, :, 8] = 0
            x[r, :, 10, :, :, 0] = rng.integers(-7, 8, (8, 16, 16)) * 2.0 ** -27
        for h in range(0, 128, 16):
            if o[r] < 2:
                u[r, h, h, 0] = k
                u[r, h + 11, h, 0] = k
            if o[r] == 2: u[r, h, h, 0] = 1.0
            if o[r] < 3: u[r, h + 8, h] = k
            else: u[r, h + 10, h, 0] = k
    return {"x": x.reshape(N, 128, 1024).astype(BF), "u": u.reshape(N, 128, 512), "v": d["v"], "tri": stored(systems(rng)), **weights(rng, [0, 8, 9, 10, 11, 12, 13, 14, 15])}
def setup_inputs_late(rng):
    d = numbers_of(rng)
    n = N * 128
    o = rng.permutation(N)
    t = systems(rng)
    for r in o[:N // 2]: t[128 * r:128 * r + 128] = renamed(rng, np.stack([FIELD] * 128))
    best = orders(rng, n)
    most = np.count_nonzero(cycle(t, best), axis=1)
    for j in range(60):
        e = orders(rng, n)
        m = np.count_nonzero(cycle(t, e), axis=1)
        best[m > most] = e[m > most]
        most = np.maximum(most, m)
    i = np.arange(n)
    third = t[i, best[:, 0], best[:, 1]]
    c = np.where(third == best[:, 2], best[:, 3], best[:, 2])
    k = np.argsort(best, axis=1).astype(float)
    k[i, c] = 1.6
    k[i[::2], third[::2]] = 1.3
    p = np.argsort(np.argsort(k, axis=1), axis=1).reshape(N, 8, 16, 15)
    s = 15.0 - p
    s[o[::2]] -= 16.0
    x = d["x"].reshape(N, 8, 16, 16, 16, 4)
    x[:, :, 0, :, :15, 0] = s.astype(np.float32).astype(BF)
    x[:, :, 8:] = odd(rng)
    u = d["u"].reshape(N, 128, 128, 4)
    u[:, :, ::16] = 0
    for h in range(0, 128, 16): u[:, h, h, 0] = 1
    return {"x": x.reshape(N, 128, 1024), "u": u.reshape(N, 128, 512), "v": d["v"], "tri": stored(t), **weights(rng)}
def setup_inputs_huge(rng):
    d = numbers_of(rng)
    q = int(rng.integers(N))
    c = rng.integers(0, 2, (N, 1, 1, 16, 16, 1)) * 2.0 - 1.0
    c[:, :, :, ::2] = c[:, :, :, ::2, :1]
    x = (0.6 + 0.06 * rng.random((N, 8, 1, 16, 16, 1)) + 0.03 * rng.random((N, 8, 16, 16, 16, 4))) * c
    s = -np.ones((16, 16))
    np.put_along_axis(s, np.argsort(rng.random((16, 15)), axis=1)[:, :3], 1.0, axis=1)
    x[q] = 0.875 * s[None, None, :, :, None]
    h = rng.integers(0, 8, (1, 16, 16, 1))
    x[q, 0, :2] *= np.where(4 * np.arange(2)[:, None, None, None] + np.arange(4) < h, 0.5, 1.0)
    a = 2.0 ** 29 * (1.0 - 0.1 * rng.random((N, 8, 16, 8, 4)))
    for g in range(8): a[:, g, :, g] *= 2.0
    a *= rng.integers(0, 2, (N, 1, 1, 8, 1)) * 2.0 - 1.0
    a[q] = 2.0 ** 30
    u = d["u"].reshape(N, 128, 128, 4)
    u[:, :, ::16] = a.reshape(N, 128, 8, 4).astype(np.float32).astype(BF)
    w = np.zeros((N, 128, 4, 128, 4), np.float32)
    i = np.arange(128)
    for b in range(4): w[:, i, b, i, b] = -1
    wc, ws = packed(w.reshape(N, 128, 2048).astype(BF), rng)
    return {"x": (2.0 ** 30 * x).astype(np.float32).reshape(N, 128, 1024).astype(BF), "u": u.reshape(N, 128, 512), "v": d["v"], "tri": stored(systems(rng)), "wc": wc, "ws": ws}
def setup_inputs_spread(rng):
    d = setup_inputs(rng)
    d["x"] = big(wide(rng, N, 128, 1024, cols=6))
    return d
def check_inputs(d):
    b = []
    for k in ("x", "u", "v"):
        a = np.abs(d[k].astype(np.float32))
        if not (np.isfinite(a).all() and ((a == 0) | (a >= 2.0 ** -30) & (a <= 2.0 ** 30)).all()): b.append("a value of " + k)
    if not ((d["tri"] >= 0) & (d["tri"] <= 15)).all(): b.append("an entry of tri")
    t = np.clip(d["tri"], 0, 15).astype(np.int64).reshape(-1, 16, 16)
    i = np.arange(16)
    if (t != t.transpose(0, 2, 1)).any() or (t[:, i, i] != 15).any() or (t[:, :, 15] != i).any() or (np.take_along_axis(t, t, axis=2) != i).any(): b.append("a table of tri that isn't one of triples")
    none, least, most = [emit(mx_ref.quantize(np.full((128, 16), k, np.float32).astype(BF)))[1][0, 0] for k in (0.0, 2.0 ** -30, 2.0 ** 30)]
    for r in range(N):
        if ((d["wc"][r] & 0x7F) == 0x7F).any(): b.append("wc: a code that is no number")
        s = mx_ref.live(d["ws"][r])
        if ((s != none) & ((s < least) | (s > most))).any(): b.append("ws: a scale out of range")
    return b
def reference(x, u, v, tri, wc, ws):
    qu = [mx_ref.quantize(u[r]) for r in range(N)]
    lay = [pk(wc[r], ws[r]) for r in range(N)]
    now = [x[r] for r in range(N)]
    t = tri.astype(np.int64).reshape(N * 128, 16, 16)
    i = np.arange(N * 128)[:, None]
    for h in range(R):
        q = [mx_ref.quantize(now[r]) for r in range(N)]
        own = [decode(q[r]).astype(BF) for r in range(N)]
        s = np.concatenate([(mx_ref.matmul(qu[r], q[r])[::16] + np.float32(0.0)).reshape(128, 16)[:, :15] for r in range(N)])
        o = np.argsort(-s, axis=1, kind="stable")
        first, second = numbered(o[:, :J]), numbered(o[:, 1:J + 1])
        third = numbered(t[i, o[:, :J], o[:, 1:J + 1]])
        z = [((gcols(own[r], second[r]).astype(np.float32) + gcols(own[r], third[r]).astype(np.float32)) * np.float32(0.5)).astype(BF) for r in range(N)]
        zq = [mx_ref.quantize(z[r]) for r in range(N)]
        for r in range(N):
            w = join(pick(zq[(r - 1) % N], np.arange(16 * K)), pick(zq[r], np.arange(16 * K, 16 * J)))
            made = tile([mx_ref.matmul(pick(lay[r], np.arange(128 * b, 128 * b + 128)), w) * np.float32(0.03125) + z[r][:, b::4].astype(np.float32) for b in range(4)]).reshape(8, 16, 16 * J, 4)
            new = np.array(own[r]).reshape(8, 16, 256, 4)
            for g in range(8): new[g][:, first[r, g]] = made[g]
            now[r] = new.reshape(128, 1024)
        t = switched(t, o)
    y, ot = np.zeros((N, 128, 256), np.float32), t.reshape(N, 128, 256).astype(np.float32)
    oc, osc = np.zeros((N, 128, 1024), np.uint8), np.zeros((N, 16, 256), np.uint8)
    for r in range(N):
        q = mx_ref.quantize(now[r])
        y[r] = mx_ref.matmul(mx_ref.quantize(v[r]), q)
        oc[r], osc[r] = emit(q)
    return {"y": y, "ot": ot, "oc": oc, "osc": osc}

@@ -1,0 +1,515 @@
+import numpy as np
+from concourse.bass import DstId, RemoteDMATransfer
+from concourse.mybir import dt, AluOpType as ALU, ActivationFunctionType as ACT
+
+ROUNDS = 3
+CFG = {"send": "fused4", "iters": 24000, "xeng": "SSVVSSSV",
+       "ws": 60.0, "wx": 100.0, "lat": 2600.0, "f": 1.2, "gc": 1.56, "sfix": 30.0, "pe": 0.6}
+COSTS = [{}, {"ws": 30.0, "wx": 60.0, "lat": 2000.0, "f": 1.0, "gc": 1.1, "sfix": 0.0, "pe": 0.45},
+         {"ws": 130.0, "wx": 180.0, "lat": 3200.0, "f": 1.35, "gc": 1.9, "sfix": 60.0, "pe": 0.9}]
+
+BF, F32, I32, U16, MXC, U8 = "bfloat16", "float32", "int32", "uint16", "float8_e4m3fn_x4", "uint8"
+SB = {}
+for _d, _names in (
+        (BF, "xn1024 ut512 vt512 et516 xt1088 gg240 sc256 fh1024 wn1536 ee144 st144 gt128 ms128 ab512 zt512 zs512 tb256 "
+             "dm1280 da1280 db1280 rs512 sb8 ch192 ne256 nk256 cs256 cc16 rho16 dl16 er32 ev16 ey256 tt256 kf240 kd128 "
+             "kr256 jc144 ka16 kb16 kc16 ua32 ub32 uc32"),
+        (F32, "ts512 aa240 oa8 ob8 wv32 wt32 wu16 sm8 otf256 ys256 ct16 col8 gf2"),
+        (I32, "ti256 ia44 ib44 ic32 ij32 ie32 iw32 ig32 ih32 ik16 im16 iq16 ir16 ip2 it2"),
+        (U16, "oi8 oj8 ok8 il16 lm44 lab32 ly16 lx16 lc6 lt2"),
+        (MXC, "wq512 qn256 qu128 qv128 qe512 qf256"), (U8, "wp512 sn256 su128 sv128 se512 sf256")):
+    for _n in _names.split():
+        SB[_n.rstrip("0123456789")] = (int(_n.lstrip("abcdefghijklmnopqrstuvwxyz")), _d)
+for _h in range(ROUNDS):
+    for _n, _w, _d in (("qx", 272, MXC), ("sx", 272, U8), ("qa", 128, MXC), ("sa", 128, U8), ("qz", 196, MXC), ("sz", 224, U8)):
+        SB["%s%d" % (_n, _h)] = (_w, _d)
+PSUM = {"ps": 512, "pt": 512, "pd": 2048, "py": 1024}
+SCRATCH = {k: ("sbuf", [128, n], d) for k, (n, d) in SB.items()}
+SCRATCH.update({k: ("psum", [128, n], F32) for k, n in PSUM.items()})
+SEMAPHORES = ["cV", "cS", "cP", "cG", "sent", "arr0", "arr1", "arr2", "l0", "l1", "l2", "l3", "l4", "l5",
+              "soc", "ss0", "ss1", "ss2", "ss3", "sot", "sy0", "sy1"]
+
+
+def v(name, a=0, b=None, s=1, n=None):
+    if n is not None:
+        b = a + s * (n - 1) + 1
+    if b is None:
+        b = SB[name][0] if name in SB else PSUM[name]
+    return ("v", name, a, b, s)
+
+
+def ind(win, off):
+    return ("i", win, off)
+
+
+def words(x):
+    return ("w", x)
+
+
+def count(x):
+    return 16 * count(x[2]) if x[0] == "i" else count(x[1]) if x[0] == "w" else len(range(x[2], x[3], x[4]))
+
+
+def views(x):
+    if not isinstance(x, tuple):
+        return []
+    return views(x[1]) + views(x[2]) if x[0] == "i" else views(x[1]) if x[0] == "w" else [x]
+
+
+def ap(T, x):
+    if not isinstance(x, tuple):
+        return x
+    if x[0] == "i":
+        return ap(T, x[1]).indirect(ap(T, x[2]))
+    if x[0] == "w":
+        return ap(T, x[1]).bitcast(dt.uint32)
+    return T[x[1]][:, x[2]:x[3]] if x[4] == 1 else T[x[1]][:, x[2]:x[3]:x[4]]
+
+
+def build(cfg):
+    ops = []
+    cyc = 0.83 * cfg["f"]
+
+    def add(eng, kind, emit, reads, writes, cost, **kw):
+        o = {"eng": eng, "kind": kind, "emit": emit, "r": [w for x in reads for w in views(x)],
+             "w": [w for x in writes for w in views(x)], "cost": cost, "lat": 0.0, "id": len(ops), "after": []}
+        o.update(kw)
+        ops.append(o)
+        return o
+
+    def vec(call, out, ins, args, per=None):
+        if per is None:
+            per = 0.5 if all(w[1] in SB and SB[w[1]][1] in (BF, U16) for x in [out] + ins for w in views(x)) else 1
+        cost = 50 + count(out) * cfg["gc"] * cyc if ins and ins[0][0] == "i" else max(64, count(out) * per) * cyc
+        add("V", "c", lambda g, T: call(g.vector)(*[ap(T, x) for x in [out] + ins + args]), ins + args, [out], cost)
+
+    def copy(out, a):
+        vec(lambda q: q.tensor_copy, out, [a], [])
+
+    def tt(out, a, b, op):
+        vec(lambda q: q.tensor_tensor, out, [a, b], [op], 1 if a[1] in PSUM else 2)
+
+    def ts(out, a, s1, op0, s2=None, op1=None):
+        vec(lambda q: q.tensor_scalar, out, [a], [s1, None, op0] if op1 is None else [s1, s2, op0, op1])
+
+    def scan(out, a, b, op0=ALU.mult, op1=ALU.add):
+        vec(lambda q: q.tensor_tensor_scan, out, [a, b], [0.0, op0, op1])
+
+    def transpose(out, a):
+        vec(lambda q: q.transpose, out, [a], [])
+
+    def memset(out, c):
+        vec(lambda q: q.memset, out, [], [c])
+
+    def quant(q, s, a):
+        add("V", "c", lambda g, T: g.vector.quantize_mx(ap(T, q), ap(T, s), ap(T, a)), [a], [q, s],
+            (12 + 0.22 * count(a)) * cfg["f"])
+
+    def act(out, a, func=ACT.Identity, **kw):
+        n = count(out)
+        cost = 65 + n * cfg["gc"] * cyc if a[0] == "i" else cfg["sfix"] + max(64, n) * cyc
+        add("S", "c", lambda g, T: g.scalar.activation(ap(T, out), ap(T, a), func, **{k: ap(T, x) for k, x in kw.items()}),
+            [a] + list(kw.values()), [out], cost)
+
+    def mm(out, l, r):
+        add("P", "c", lambda g, T: g.tensor.matmul_mx(*[ap(T, x) for x in [out] + l + r], True, True),
+            l + r, [out], (count(r[0]) + 16) * cfg["pe"])
+
+    def pair(q, s, a, n):
+        return [v(q, a, n=n), v(s, a, n=n)]
+
+    def iota(out, pattern, base, cm):
+        kw = {} if SB[out[1]][1] == I32 else {"allow_small_or_imprecise_dtypes": True}
+        add("G", "c", lambda g, T: g.iota(ap(T, out), pattern, base, cm, **kw), [], [out], 130 + 2 * count(out) * cyc)
+
+    def select(out, pattern, val, base, cm):
+        add("G", "c", lambda g, T: g.affine_select(ap(T, out), ap(T, out), pattern, ALU.not_equal, val, base, cm),
+            [out], [out], 170 + 2 * count(out) * cyc)
+
+    def dma(q, sem, sides, reads, writes, kb):
+        add(q, "d", lambda g, T: (g.sync if q == "Y" else g.scalar).dma_start(*sides(T)), reads, writes, 60.0,
+            sem=sem, lat=1500.0 + 4.0 * kb)
+
+    dma("S", "l0", lambda T: (T.ut[:], T.u[:]), [], [v("ut")], 128)
+    dma("Y", "l1", lambda T: (T.xn[:], T.x[:]), [], [v("xn")], 384)
+    dma("Y", "l2", lambda T: (T.ti[:], T.tri[:]), [], [v("ti")], 512)
+    dma("Y", "l3", lambda T: (T.wq[:].bitcast(dt.uint8), T.wc[:]), [], [v("wq")], 768)
+    dma("Y", "l4", lambda T: (T.wp[:], T.ws[:]), [], [v("wp")], 832)
+    dma("Y", "l5", lambda T: (T.vt[:], T.v[:]), [], [v("vt")], 960)
+
+    memset(v("et"), 0.0)
+    select(v("et", 3, s=4, n=128), [[-1, 128]], 0.5, 0, 1)
+    for b in range(4):
+        quant(*pair("qe", "se", 128 * b, 128), v("et", 3 - b, n=512))
+    iota(v("ia", 0, 18), [[1, 18]], -1, 16)
+    iota(v("ia", 18, 34), [[1, 16]], 0, 16)
+    iota(v("ia", 34, 44), [[0, 10]], 15, 16)
+    ts(v("ib"), v("ia"), 255, ALU.bitwise_and)
+    copy(v("lm"), v("ib"))
+    iota(v("ik"), [[0, 16]], 0, 1)
+    ts(v("im"), v("ik"), 15, ALU.bitwise_and)
+    copy(v("ly"), v("im"))
+    ts(v("ip", 0, 1), v("ik", 0, 1), 4, ALU.logical_shift_right, 1, ALU.bitwise_and)
+    copy(v("gf", 0, 1), v("ip", 0, 1))
+    rep = v("col", 0, 1)
+    copy(rep, v("im", 0, 1))
+    ts(v("sb", 2, 3), v("im", 0, 1), 15.0, ALU.is_lt, 16.0, ALU.mult)
+    act(v("col", 3, 4), v("sb", 2, 3), scale=16.0, bias=rep)
+    iota(v("ic"), [[1, 2], [1, 16]], 1, 1)
+    iota(v("ij"), [[1, 2], [1, 16]], 0, 0)
+    ts(v("ie"), v("ic"), 15, ALU.bitwise_and)
+    tt(v("ig", 0, 16), v("ie", 0, 16), v("ij", 0, 16), ALU.min)
+    ts(v("iw", 0, 16), v("ig", 0, 16), 1.0, ALU.add)
+    tt(v("iw", 16, 32), v("ie", 16, 32), v("ij", 16, 32), ALU.max)
+    ts(v("ig"), v("iw"), v("gf", 0, 1), ALU.add)
+    ts(v("ih"), v("ig"), 1, ALU.bitwise_and)
+    ts(v("ig"), v("ih"), 15.0, ALU.mult)
+    tt(v("ih"), v("ig"), v("iw"), ALU.add)
+    ts(v("lab"), v("ih"), 16.0, ALU.mult)
+    copy(v("lx"), v("ij", 0, 16))
+    memset(v("kf"), 1.0)
+    select(v("kf"), [[1, 15], [1, 16]], -1.0, -14, 0)
+    memset(v("kf", 0, 240, 16), 0.0)
+    memset(v("sc", 240, 256), 100.0)
+    iota(v("jc"), [[1, 9], [1, 16]], -12, 0)
+    iota(v("iq"), [[1, 16]], 128, -1)
+    ts(v("ir"), v("iq"), 15, ALU.bitwise_and)
+    ts(v("ka"), v("ir"), 0.0, ALU.is_equal, 128.0, ALU.mult)
+    ts(v("kb"), v("ir"), 1.0, ALU.is_equal, -16.0, ALU.mult)
+    tt(v("kc"), v("ka"), v("kb"), ALU.add)
+    act(v("kd"), ind(v("kc"), v("ly", 0, 8)))
+    memset(v("xt", 0, 64), 0.0)
+    memset(v("lc"), 15)
+    memset(v("lc", 2, 3), 31)
+    memset(v("lc", 5, 6), 143)
+    memset(v("kr"), -1.0)
+    memset(v("kr", 15, 256, 16), 15.0)
+    memset(v("zt", 256, 512), 0.0)
+    for out, c in ((v("ch"), 0), (v("ne", 0, 256, 8), 0), (v("ne", 7, 256, 8), -1), (v("nk"), 0), (v("nk", 0, 256, 8), 1),
+                   (v("nk", 7, 256, 8), 1), (v("dm", 0, 1280, 5), 0), (v("dm", 1, 1280, 5), -1), (v("dm", 3, 1280, 5), 1),
+                   (v("dm", 4, 1280, 5), 1), (v("ua", 0, 32, 2), 128)):
+        act(out, v("kr", 0, count(out)), scale=0.0, bias=float(c))
+    iota(v("ct"), [[-1, 16]], 12, 0)
+    iota(v("ub", 1, 32, 2), [[1, 16]], 8, 0)
+    ts(v("it", 0, 1), v("ik", 0, 1), 31, ALU.bitwise_and)
+    copy(v("lt", 0, 1), v("it", 0, 1))
+
+    quant(v("qu"), v("su"), v("ut"))
+    copy(v("tb"), v("ti"))
+    quant(v("qv"), v("sv"), v("vt"))
+    uq = pair("qu", "su", 0, 128)
+
+    for h in range(ROUNDS):
+        qx, sx, qa, sa, qz, sz = ["%s%d" % (k, h) for k in ("qx", "sx", "qa", "sa", "qz", "sz")]
+        last = h == ROUNDS - 1
+        d1, tn = ("da", "db") if h % 2 == 0 else ("db", "da")
+        if h == 0:
+            quant(v("qn"), v("sn"), v("xn"))
+            copy(words(v(qx)), ind(words(v("qn")), v("lm", 0, 17)))
+            act(v(sx), ind(v("sn"), v("lm", 0, 17)), func=ACT.Copy)
+            tab, win, mul, plus = v("tb"), v("tb"), 1.0, 0.0
+            mm(v("ps", 0, 272), uq, pair(qx, sx, 0, 272))
+            transpose(v("ts", 0, 256), v("ps", 0, 256))
+            transpose(v("ts", 256, 512), v("ps", 16, 272))
+        else:
+            quant(*pair(qx, sx, 0, 144), v("xt", 0, 576))
+            quant(*pair(qx, sx, 144, 128), v("xt", 576, 1088))
+            tab, win, mul, plus = v(d1, 4, 1280, 5), v(d1), 5.0, 4.0
+            for k, bank in enumerate(("ps", "pt")):
+                mm(v(bank, 0, 144), uq, pair(qx, sx, 128 * k, 144))
+                transpose(v("ts", 128 * k, n=128), v(bank, 0, 128))
+                transpose(v("ts", 256 + 128 * k, n=128), v(bank, 16, 144))
+        plane = [v("fh", 256 * b, n=256) for b in range(4)]
+        for b in range(4):
+            mm(v("pd", 512 * b, n=256), pair("qe", "se", 128 * b, 128), pair(qx, sx, 16, 256))
+            act(plane[b], v("pd", 512 * b, n=256))
+        act(v("aa"), ind(v("ts"), v("lab", 16, 31)))
+        tt(v("gg"), ind(v("ts"), v("lab", 0, 15)), v("aa"), ALU.is_ge)
+        scan(v("sc", 0, 240), v("kf"), v("gg"))
+        tt(v("ee"), ind(v("sc"), v("lm", 34, 43)), v("jc"), ALU.not_equal)
+        scan(v("st"), v("ee"), v("kr", 0, 144))
+        ts(v("oj"), v("st", 31, s=16, n=8), 16.0, ALU.mult, rep, ALU.add)
+        ts(v("oa"), v("st", 15, s=16, n=8), 16.0, ALU.mult)
+        tt(v("ob"), v("oa"), v("st", 31, s=16, n=8), ALU.add)
+        ts(v("oi"), v("ob"), mul, ALU.mult, plus, ALU.add)
+        copy(v("gt"), ind(win, v("oi")))
+        scan(v("ms"), v("kd"), v("gt"), ALU.add, ALU.min)
+        ts(v("ok"), v("ms", 15, 128, 16), 16.0, ALU.mult, v("col", 3, 4), ALU.add)
+        for j in (0, 4):
+            for b in range(4):
+                first = v("ab", 64 * (j + b), n=64)
+                act(first, ind(plane[b], v("oj", j, n=4)))
+                tt(v("zt", 64 * j + b, s=4, n=64), ind(plane[b], v("ok", j, n=4)), first, ALU.add)
+            quant(*(pair(qa, sa, 0, 128) if j == 0 else pair(qz, sz, 0, 128)), v("zt"))
+            if j == 0:
+                snd = add("G", "r", h, [v(qa, 0, 66), v(sa, 0, 88)], [], 150.0, lat=cfg["lat"])
+            act(v("zs", 64 * j, n=256), v("zt", 64 * j, n=256), scale=32.0)
+        for b in range(4):
+            act(v("wn", 384 * b + 128, n=256), plane[b], scale=64.0)
+            mm(v("pd", 512 * b, n=128), pair("wq", "wp", 128 * b, 128), pair(qz, sz, 0, 128))
+            tt(v("wn", 384 * b + 64, n=64), v("pd", 512 * b + 64, n=64), v("zs", 256 + b, s=4, n=64), ALU.add)
+        tt(v("ub", 0, 32, 2), v("sc", 15, 256, 16), v("ct"), ALU.add)
+        act(v("ua", 1, 32, 2), v("ub", 0, 32, 2), func=ACT.Relu, scale=64.0, bias=-448.0)
+        scan(v("uc"), v("ua"), v("ub"), ALU.max, ALU.min)
+        if not last:
+            ts(v("il"), v("uc", 1, 32, 2), 16.0, ALU.mult, rep, ALU.add)
+        else:
+            act(v("wv", 0, 16), v("uc", 1, 32, 2), scale=16.0, bias=rep)
+            act(v("wv", 16, 32), v("uc", 1, 32, 2), scale=16.0, bias=rep)
+            transpose(v("wt"), v("wv"))
+            act(v("wu"), ind(v("wt"), v("lt", 0, 1)))
+            copy(v("il"), v("wu"))
+        a_, b_, o2_, o3_ = [v("st", 16 * i + 15, n=1) for i in range(4)]
+        ts(v(d1, 0, 1280, 5), tab, a_, ALU.not_equal)
+        ts(v(d1, 1, 1280, 5), tab, b_, ALU.not_equal)
+        scan(v("rs", 0, 256), v(d1, 0, 1280, 5), v("kr"))
+        scan(v("rs", 256, 512), v(d1, 1, 1280, 5), v("kr"))
+        if h == 0:
+            act(v(d1, 4, 1280, 5), tab)
+        act(v("sb", 0, 1), o3_, scale=-1.0, bias=o2_)
+        act(v("sm", 1, 2), a_, scale=-1.0, bias=b_)
+        ts(v("sm", 2, 3), v("ms", 15, 16), v("sb", 2, 3), ALU.add, o2_, ALU.not_equal)
+        ts(v("ch", 15, 16), v("sm", 2, 3), v("sb", 0, 1), ALU.mult, o3_, ALU.add)
+        rows = v("rs", 15, 512, 16)
+        for s in range(1, 7):
+            src = ind(v("ch", 32 * (s - 1), n=32), v("lc", 0 if s == 1 else 2, n=2)) if s < 6 else \
+                ind(v("ch", 32, 192), v("lc", 4, 6))
+            tt(v("ne", s, 256, 8), src, rows, ALU.not_equal)
+            if s < 6:
+                scan(v("ch", 32 * s, n=32), v("ne", s, 256, 8), v("kr", 0, 32))
+        scan(v("cs"), v("ne"), v("nk"))
+        tt(v("cc"), v("cs", 7, 128, 8), v("cs", 135, 256, 8), ALU.max)
+        tt(v("rho"), v("rs", 271, 512, 16), v("rs", 15, 256, 16), ALU.subtract)
+        tt(v("dl"), v("cc"), v("rho"), ALU.mult)
+        act(v("er"), rows, func=ACT.Relu, bias=-14.0)
+        tt(v("ev"), v("er", 0, 16), v("er", 16, 32), ALU.subtract)
+        act(v("ey"), ind(v("ev"), v("ly")))
+        act(v("dm", 2, 1280, 5), ind(v("cc"), v("lx")), scale=v("sm", 1, 2))
+        tt(v("tt"), ind(v("dl"), v("lx")), v("ey"), ALU.mult)
+        act(v(d1, 3, 1280, 5), ind(v("tt"), v("lm", 18, 34)))
+        act(v(d1, 2, 1280, 5), v("tt"))
+        scan(v(tn), v("dm"), v(d1))
+        if last:
+            act(v("otf"), v(tn, 4, 1280, 5))
+            dma("Y", "sot", lambda T: (T.ot[:], T.otf[:]), [v("otf")], [], 128)
+        add("A", "a", h, [], [v(qz, 128, 194), v(sz, 128, 216)], 0.0, after=[snd["id"]])
+        for b in range(4):
+            mm(v("pd", 512 * b, n=128), pair("wq", "wp", 128 * b, 128), pair(qz, sz, 64, 128))
+            tt(v("wn", 384 * b, n=64), v("pd", 512 * b + 64, n=64), v("zs", b, s=4, n=64), ALU.add)
+        for k, e in enumerate(cfg["xeng"]):
+            b, p = k % 4, 8 * (k // 4)
+            out, src = v("xt", 64 + b + 64 * p, s=4, n=128), ind(v("wn", 384 * b, n=384), v("il", p, n=8))
+            if e == "V":
+                ts(out, src, 0.03125, ALU.mult)
+            else:
+                act(out, src, scale=0.03125)
+
+    for k in range(2):
+        quant(*pair("qf", "sf", 128 * k, 128), v("xt", 64 + 512 * k, n=512))
+        mm(v("py", 512 * k, n=128), pair("qv", "sv", 0, 128), pair("qf", "sf", 128 * k, 128))
+    dma("Y", "soc", lambda T: (T.oc[:], T.qf[:].bitcast(dt.uint8)), [v("qf")], [], 128)
+    for k in range(4):
+        dma("SSYY"[k], "ss%d" % k, lambda T, k=k: (T.osc[4 * k:4 * k + 4, :], T.sf[32 * k:32 * k + 4, :]), [v("sf")], [], 1)
+    act(v("ys", 0, 128), v("py", 0, 128))
+    copy(v("ys", 128, 256), v("py", 512, 640))
+    for k in range(2):
+        dma("SY"[k], "sy%d" % k, lambda T, k=k: (T.y[:, 128 * k:128 * k + 128], T.ys[:, 128 * k:128 * k + 128]),
+            [v("ys", 128 * k, n=128)], [], 64)
+    return ops
+
+
+def depend(ops):
+    writer, readers = {}, {}
+    for o in ops:
+        d = set(o["after"])
+        rk, wk = set(), set()
+        for ws, ks in ((o["r"], rk), (o["w"], wk)):
+            for x in ws:
+                if x[1] in PSUM:
+                    ks.update((x[1], c) for c in range(x[2] // 512, (x[3] - 1) // 512 + 1))
+                else:
+                    ks.update((x[1], c) for c in range(x[2], x[3], x[4]))
+        for k in rk:
+            if k in writer:
+                d.add(writer[k])
+            if k[0] in PSUM:
+                d.update(r for r in readers.get(k, ()) if ops[r]["eng"] != o["eng"])
+        for k in wk:
+            if k in writer:
+                d.add(writer[k])
+            d.update(readers.get(k, ()))
+        for k in rk:
+            readers.setdefault(k, []).append(o["id"])
+        for k in wk:
+            writer[k] = o["id"]
+            readers[k] = []
+        d.discard(o["id"])
+        o["dep"] = sorted(d)
+
+
+def gap(cfg, a, b):
+    if b["kind"] == "a":
+        return a["lat"]
+    return a["lat"] + (cfg["ws"] if a["eng"] == b["eng"] and a["kind"] == "c" else cfg["wx"])
+
+
+def schedule(ops, cfg):
+    rank = [o["cost"] + o["lat"] for o in ops]
+    for o in reversed(ops):
+        for d in o["dep"]:
+            rank[d] = max(rank[d], ops[d]["cost"] + gap(cfg, ops[d], o) + rank[o["id"]])
+    busy = {}
+    loads = [o["id"] for o in ops if o["kind"] == "d" and not o["r"]]
+    for i in loads + sorted((i for i in range(len(ops)) if i not in loads), key=lambda i: (-rank[i], i)):
+        o = ops[i]
+        t = max([ops[d]["end"] + gap(cfg, ops[d], o) for d in o["dep"]] + [0.0])
+        line = busy.setdefault(o["eng"], [])
+        for s, e in line:
+            if t + o["cost"] <= s:
+                break
+            t = max(t, e)
+        o["start"], o["end"] = t, t + o["cost"]
+        line.append((o["start"], o["end"]))
+        line.sort()
+    return [o["id"] for o in sorted(ops, key=lambda o: (o["start"], o["id"]))]
+
+
+def span(order, tab):
+    end, free, top = [0.0] * len(tab), {}, 0.0
+    for i in order:
+        e, c, ds, lat = tab[i]
+        t = free.get(e, 0.0)
+        for d, gp in ds:
+            x = end[d] + gp
+            if x > t:
+                t = x
+        t += c
+        end[i] = t
+        free[e] = t
+        if t + lat > top:
+            top = t + lat
+    return top
+
+
+def refine(ops, order, cfg):
+    n, tabs = len(ops), []
+    for m in COSTS:
+        c = dict(cfg)
+        c.update(m)
+        new = build(c)
+        tabs.append([(o["eng"], new[o["id"]]["cost"], [(d, gap(c, new[d], new[o["id"]])) for d in o["dep"]],
+                      new[o["id"]]["lat"] if o["kind"] == "d" else 0.0) for o in ops])
+    succ = [[] for o in ops]
+    for o in ops:
+        for d in o["dep"]:
+            succ[d].append(o["id"])
+    base = [span(order, t) for t in tabs]
+    cur = best = float(len(tabs))
+    keep = list(order)
+    rng = np.random.default_rng(1)
+    movable = [o["id"] for o in ops if o["kind"] == "c"]
+    for it in range(cfg["iters"]):
+        i = movable[int(rng.integers(len(movable)))]
+        pos = {x: k for k, x in enumerate(order)}
+        lo = max([pos[d] for d in ops[i]["dep"]] + [-1]) + 1
+        hi = min([pos[s] for s in succ[i]] + [n])
+        p = pos[i]
+        cand = [k for k in range(max(lo, p - 40), min(hi, p + 40)) if k != p and ops[order[k]]["eng"] == ops[i]["eng"]
+                and not (ops[order[k]]["kind"] == "d" and not ops[order[k]]["r"])]
+        if not cand:
+            continue
+        new = list(order)
+        new.pop(p)
+        new.insert(cand[int(rng.integers(len(cand)))], i)
+        x = sum(span(new, t) / b for t, b in zip(tabs, base))
+        if x <= cur + 0.004 * (1 - it / cfg["iters"]) * float(rng.random()):
+            order, cur = new, x
+            if x < best:
+                best, keep = x, list(new)
+    return keep, [round(span(keep, t)) for t in tabs]
+
+
+def waits(ops, order, arrive):
+    done, known, pos = {}, {}, {x: k for k, x in enumerate(order)}
+    for i in order:
+        o = ops[i]
+        if o["kind"] == "c":
+            done[o["eng"]] = done.get(o["eng"], 0) + 1
+            o["mark"] = ("c" + o["eng"], done[o["eng"]])
+        elif o["kind"] == "d":
+            o["mark"] = (o["sem"], 16)
+        elif o["kind"] == "a":
+            o["mark"] = ("arr%d" % o["emit"], arrive)
+            o["know"] = {}
+            continue
+        kn = known.setdefault(o["eng"], {})
+        o["wait"] = []
+        for d in sorted(o["dep"], key=lambda d: -pos[d]):
+            s, n = ops[d]["mark"]
+            if kn.get(s, 0) < n:
+                o["wait"].append((s, n))
+                kn[s] = n
+                for s2, n2 in ops[d]["know"].items():
+                    kn[s2] = max(kn.get(s2, 0), n2)
+        o["know"] = dict(kn)
+
+
+PLAN = {}
+
+
+def plan(arrive):
+    if arrive not in PLAN:
+        ops = build(CFG)
+        depend(ops)
+        order = refine(ops, schedule(ops, CFG), CFG)[0]
+        waits(ops, order, arrive)
+        PLAN[arrive] = (ops, order)
+    return PLAN[arrive]
+
+
+def bits(engines):
+    return sum(1 << e for e in engines)
+
+
+def rank_program(g, core, T, topo):
+    rank = T.rank_of(core)
+    if rank is None:
+        return
+    nxt = T.cores[(rank + 1) % len(T.cores)]
+    rid, pid = topo.addr(nxt)[:2]
+    engines = topo.engines(core, nxt)
+    ops, order = plan(len(engines))
+    queue = {"V": g.vector, "S": g.scalar, "P": g.tensor, "G": g, "Y": g.sync}
+
+    def pass_on(h):
+        qa, sa, qz, sz = [T["%s%d" % (k, h)] for k in ("qa", "sa", "qz", "sz")]
+        arr = T.sem["arr%d" % h]
+        if CFG["send"] == "fused4":
+            pairs = [(qa[:, 22 * k:22 * k + 22].bitcast(dt.uint8), qz[:, 128 + 22 * k:150 + 22 * k].bitcast(dt.uint8))
+                     for k in range(3)] + [(sa[:, 0:88], sz[:, 128:216])]
+            n = len(engines) // 4
+            g.remote_dma_fused([RemoteDMATransfer(dst_ids=[DstId(rid=rid, pnc=pid)], dma_engine_mask=bits(engines[n * k:n * k + n]),
+                                                  remote_sem=arr, src=s, dst=d) for k, (s, d) in enumerate(pairs)],
+                               local_sem=T.sem.sent)
+        else:
+            n = len(engines) // 2
+            g.remote_dma(qz[:, 128:192].bitcast(dt.uint8), qa[:, 0:64].bitcast(dt.uint8), arr, T.sem.sent, pid, rid, bits(engines[:n]))
+            g.remote_dma(sz[:, 128:192], sa[:, 0:64], arr, T.sem.sent, pid, rid, bits(engines[n:]))
+
+    for i in order:
+        o = ops[i]
+        if o["kind"] == "a":
+            continue
+        q = queue[o["eng"]]
+        for s, n in o["wait"]:
+            q.wait_ge(T.sem[s], n)
+        if o["kind"] == "r":
+            pass_on(o["emit"])
+        else:
+            o["emit"](g, T).then_inc(T.sem[o["mark"][0]], 1 if o["kind"] == "c" else 16)
+    total = {"sent": ROUNDS * len(engines)}
+    for o in ops:
+        if o["kind"] in "cd":
+            total[o["mark"][0]] = max(total.get(o["mark"][0], 0), o["mark"][1])
+    for s, n in total.items():
+        g.wait_ge(T.sem[s], n)

@@ -3,25 +3,25 @@ from concourse.bass import DstId, RemoteDMATransfer
 from concourse.mybir import dt, AluOpType as ALU, ActivationFunctionType as ACT
 
 ROUNDS = 3
-CFG = {"send": "fused4", "iters": 24000, "xeng": "SSVVSSSV",
-       "ws": 60.0, "wx": 100.0, "lat": 2600.0, "f": 1.2, "gc": 1.56, "sfix": 30.0, "pe": 0.6}
-COSTS = [{}, {"ws": 30.0, "wx": 60.0, "lat": 2000.0, "f": 1.0, "gc": 1.1, "sfix": 0.0, "pe": 0.45},
-         {"ws": 130.0, "wx": 180.0, "lat": 3200.0, "f": 1.35, "gc": 1.9, "sfix": 60.0, "pe": 0.9}]
+CFG = {"iters": 36000, "xeng": "SSVVSSSV", "asplit": 8,
+       "ws": 200.0, "wx": 200.0, "lat": 3000.0, "f": 1.05, "gc": 1.4, "sfix": 30.0, "pe": 0.6}
+COSTS = [{}, {"ws": 100.0, "wx": 120.0, "lat": 4500.0, "f": 1.1, "gc": 1.5},
+         {"ws": 150.0, "wx": 250.0, "lat": 3500.0, "f": 1.3, "gc": 1.8}]
 
 BF, F32, I32, U16, MXC, U8 = "bfloat16", "float32", "int32", "uint16", "float8_e4m3fn_x4", "uint8"
 SB = {}
 for _d, _names in (
-        (BF, "xn1024 ut512 vt512 et516 xt1088 gg240 sc256 fh1024 wn1536 ee144 st144 gt128 ms128 ab512 zt512 zs512 tb256 "
-             "dm1280 da1280 db1280 rs512 sb8 ch192 ne256 nk256 cs256 cc16 rho16 dl16 er32 ev16 ey256 tt256 kf240 kd128 "
-             "kr256 jc144 ka16 kb16 kc16 ua32 ub32 uc32"),
-        (F32, "ts512 aa240 oa8 ob8 wv32 wt32 wu16 sm8 otf256 ys256 ct16 col8 gf2"),
+        (BF, "xn1024 ut512 vt512 et516 xt1088 gg240 sc256 fh1024 wn1536 ee288 oo8 gt128 ms128 ab512 zt512 zs512 tb256 "
+             "dm1280 da1280 db1280 rs512 sb8 ch192 ne256 nk256 cs256 cc16 rho16 dl16 er32 ev16 ey256 tt256 kf240 kd64 "
+             "kr256 jc288 ka16 kb16 kc16 ua32 ub32 uc32"),
+        (F32, "ts512 aa240 st288 kh144 den16 rec16 wv32 wt32 wu16 sm8 otf256 ys256 ct16 col8 gf2"),
         (I32, "ti256 ia44 ib44 ic32 ij32 ie32 iw32 ig32 ih32 ik16 im16 iq16 ir16 ip2 it2"),
         (U16, "oi8 oj8 ok8 il16 lm44 lab32 ly16 lx16 lc6 lt2"),
         (MXC, "wq512 qn256 qu128 qv128 qe512 qf256"), (U8, "wp512 sn256 su128 sv128 se512 sf256")):
     for _n in _names.split():
         SB[_n.rstrip("0123456789")] = (int(_n.lstrip("abcdefghijklmnopqrstuvwxyz")), _d)
 for _h in range(ROUNDS):
-    for _n, _w, _d in (("qx", 272, MXC), ("sx", 272, U8), ("qa", 128, MXC), ("sa", 128, U8), ("qz", 196, MXC), ("sz", 224, U8)):
+    for _n, _w, _d in (("qx", 272, MXC), ("sx", 272, U8), ("qa", 128, MXC), ("sa", 128, U8), ("qz", 192, MXC), ("sz", 192, U8)):
         SB["%s%d" % (_n, _h)] = (_w, _d)
 PSUM = {"ps": 512, "pt": 512, "pd": 2048, "py": 1024}
 SCRATCH = {k: ("sbuf", [128, n], d) for k, (n, d) in SB.items()}
@@ -153,6 +153,7 @@ def build(cfg):
     copy(v("gf", 0, 1), v("ip", 0, 1))
     rep = v("col", 0, 1)
     copy(rep, v("im", 0, 1))
+    act(v("col", 1, 2), rep, bias=-15.75)
     ts(v("sb", 2, 3), v("im", 0, 1), 15.0, ALU.is_lt, 16.0, ALU.mult)
     act(v("col", 3, 4), v("sb", 2, 3), scale=16.0, bias=rep)
     iota(v("ic"), [[1, 2], [1, 16]], 1, 1)
@@ -171,13 +172,19 @@ def build(cfg):
     select(v("kf"), [[1, 15], [1, 16]], -1.0, -14, 0)
     memset(v("kf", 0, 240, 16), 0.0)
     memset(v("sc", 240, 256), 100.0)
-    iota(v("jc"), [[1, 9], [1, 16]], -12, 0)
+    iota(v("jc"), [[1, 9], [1, 2], [1, 16]], -12, 0)
+    iota(v("den"), [[1, 16]], 1, 0)
+    vec(lambda q: q.reciprocal, v("rec"), [v("den")], [], 18)
+    act(v("kh"), ind(v("rec"), v("ly", 0, 9)), scale=-1.0, bias=1.0)
+    memset(v("kh", 15, 144, 16), 15.0)
+    memset(v("kh", 0, 144, 32), 0.0)
+    memset(v("kh", 16, 144, 32), 16.0)
     iota(v("iq"), [[1, 16]], 128, -1)
     ts(v("ir"), v("iq"), 15, ALU.bitwise_and)
     ts(v("ka"), v("ir"), 0.0, ALU.is_equal, 128.0, ALU.mult)
     ts(v("kb"), v("ir"), 1.0, ALU.is_equal, -16.0, ALU.mult)
     tt(v("kc"), v("ka"), v("kb"), ALU.add)
-    act(v("kd"), ind(v("kc"), v("ly", 0, 8)))
+    act(v("kd"), ind(v("kc"), v("ly", 0, 4)))
     memset(v("xt", 0, 64), 0.0)
     memset(v("lc"), 15)
     memset(v("lc", 2, 3), 31)
@@ -223,26 +230,27 @@ def build(cfg):
         for b in range(4):
             mm(v("pd", 512 * b, n=256), pair("qe", "se", 128 * b, 128), pair(qx, sx, 16, 256))
             act(plane[b], v("pd", 512 * b, n=256))
-        act(v("aa"), ind(v("ts"), v("lab", 16, 31)))
+        k = cfg["asplit"]
+        copy(v("aa", 0, 16 * k), ind(v("ts"), v("lab", 16, 16 + k)))
+        act(v("aa", 16 * k, 240), ind(v("ts"), v("lab", 16 + k, 31)))
         tt(v("gg"), ind(v("ts"), v("lab", 0, 15)), v("aa"), ALU.is_ge)
         scan(v("sc", 0, 240), v("kf"), v("gg"))
-        tt(v("ee"), ind(v("sc"), v("lm", 34, 43)), v("jc"), ALU.not_equal)
-        scan(v("st"), v("ee"), v("kr", 0, 144))
-        ts(v("oj"), v("st", 31, s=16, n=8), 16.0, ALU.mult, rep, ALU.add)
-        ts(v("oa"), v("st", 15, s=16, n=8), 16.0, ALU.mult)
-        tt(v("ob"), v("oa"), v("st", 31, s=16, n=8), ALU.add)
-        ts(v("oi"), v("ob"), mul, ALU.mult, plus, ALU.add)
-        copy(v("gt"), ind(win, v("oi")))
-        scan(v("ms"), v("kd"), v("gt"), ALU.add, ALU.min)
-        ts(v("ok"), v("ms", 15, 128, 16), 16.0, ALU.mult, v("col", 3, 4), ALU.add)
         for j in (0, 4):
+            e = 36 * j
+            tt(v("ee", e, n=144), ind(v("sc"), v("lm", 34, 43)), v("jc", 32 * j, n=144), ALU.is_equal)
+            scan(v("st", e, n=144), v("kh"), v("ee", e, n=144))
+            ts(v("oi", j, n=4), v("st", e + 31, s=32, n=4), mul, ALU.mult, plus + 0.25 - 17.0 * mul, ALU.add)
+            ts(v("oj", j, n=4), v("st", e + 47, s=32, n=4), 16.0, ALU.mult, v("col", 1, 2), ALU.add)
+            copy(v("gt", 16 * j, n=64), ind(win, v("oi", j, n=4)))
+            scan(v("ms", 16 * j, n=64), v("kd"), v("gt", 16 * j, n=64), ALU.add, ALU.min)
+            ts(v("ok", j, n=4), v("ms", 16 * j + 15, s=16, n=4), 16.0, ALU.mult, v("col", 3, 4), ALU.add)
             for b in range(4):
                 first = v("ab", 64 * (j + b), n=64)
                 act(first, ind(plane[b], v("oj", j, n=4)))
                 tt(v("zt", 64 * j + b, s=4, n=64), ind(plane[b], v("ok", j, n=4)), first, ALU.add)
             quant(*(pair(qa, sa, 0, 128) if j == 0 else pair(qz, sz, 0, 128)), v("zt"))
             if j == 0:
-                snd = add("G", "r", h, [v(qa, 0, 66), v(sa, 0, 88)], [], 150.0, lat=cfg["lat"])
+                snd = add("G", "r", h, pair(qa, sa, 0, 64), [], 150.0, lat=cfg["lat"])
             act(v("zs", 64 * j, n=256), v("zt", 64 * j, n=256), scale=32.0)
         for b in range(4):
             act(v("wn", 384 * b + 128, n=256), plane[b], scale=64.0)
@@ -259,7 +267,8 @@ def build(cfg):
             transpose(v("wt"), v("wv"))
             act(v("wu"), ind(v("wt"), v("lt", 0, 1)))
             copy(v("il"), v("wu"))
-        a_, b_, o2_, o3_ = [v("st", 16 * i + 15, n=1) for i in range(4)]
+        ts(v("oo", 0, 4), v("st", 15, s=32, n=4), 12582912.0, ALU.add, 12582913.0, ALU.subtract)
+        a_, b_, o2_, o3_ = [v("oo", i, n=1) for i in range(4)]
         ts(v(d1, 0, 1280, 5), tab, a_, ALU.not_equal)
         ts(v(d1, 1, 1280, 5), tab, b_, ALU.not_equal)
         scan(v("rs", 0, 256), v(d1, 0, 1280, 5), v("kr"))
@@ -292,7 +301,7 @@ def build(cfg):
         if last:
             act(v("otf"), v(tn, 4, 1280, 5))
             dma("Y", "sot", lambda T: (T.ot[:], T.otf[:]), [v("otf")], [], 128)
-        add("A", "a", h, [], [v(qz, 128, 194), v(sz, 128, 216)], 0.0, after=[snd["id"]])
+        add("A", "a", h, [], pair(qz, sz, 128, 64), 0.0, after=[snd["id"]])
         for b in range(4):
             mm(v("pd", 512 * b, n=128), pair("wq", "wp", 128 * b, 128), pair(qz, sz, 64, 128))
             tt(v("wn", 384 * b, n=64), v("pd", 512 * b + 64, n=64), v("zs", b, s=4, n=64), ALU.add)
@@ -467,34 +476,22 @@ def plan(arrive):
     return PLAN[arrive]
 
 
-def bits(engines):
-    return sum(1 << e for e in engines)
-
-
 def rank_program(g, core, T, topo):
     rank = T.rank_of(core)
     if rank is None:
         return
     nxt = T.cores[(rank + 1) % len(T.cores)]
     rid, pid = topo.addr(nxt)[:2]
-    engines = topo.engines(core, nxt)
-    ops, order = plan(len(engines))
+    mask = topo.mask(core, nxt)
+    arrive = 2 * len(topo.engines(core, nxt))
+    ops, order = plan(arrive)
     queue = {"V": g.vector, "S": g.scalar, "P": g.tensor, "G": g, "Y": g.sync}
 
     def pass_on(h):
         qa, sa, qz, sz = [T["%s%d" % (k, h)] for k in ("qa", "sa", "qz", "sz")]
         arr = T.sem["arr%d" % h]
-        if CFG["send"] == "fused4":
-            pairs = [(qa[:, 22 * k:22 * k + 22].bitcast(dt.uint8), qz[:, 128 + 22 * k:150 + 22 * k].bitcast(dt.uint8))
-                     for k in range(3)] + [(sa[:, 0:88], sz[:, 128:216])]
-            n = len(engines) // 4
-            g.remote_dma_fused([RemoteDMATransfer(dst_ids=[DstId(rid=rid, pnc=pid)], dma_engine_mask=bits(engines[n * k:n * k + n]),
-                                                  remote_sem=arr, src=s, dst=d) for k, (s, d) in enumerate(pairs)],
-                               local_sem=T.sem.sent)
-        else:
-            n = len(engines) // 2
-            g.remote_dma(qz[:, 128:192].bitcast(dt.uint8), qa[:, 0:64].bitcast(dt.uint8), arr, T.sem.sent, pid, rid, bits(engines[:n]))
-            g.remote_dma(sz[:, 128:192], sa[:, 0:64], arr, T.sem.sent, pid, rid, bits(engines[n:]))
+        g.remote_dma(qz[:, 128:192].bitcast(dt.uint8), qa[:, 0:64].bitcast(dt.uint8), arr, T.sem.sent, pid, rid, mask)
+        g.remote_dma(sz[:, 128:192], sa[:, 0:64], arr, T.sem.sent, pid, rid, mask)
 
     for i in order:
         o = ops[i]
@@ -507,7 +504,7 @@ def rank_program(g, core, T, topo):
             pass_on(o["emit"])
         else:
             o["emit"](g, T).then_inc(T.sem[o["mark"][0]], 1 if o["kind"] == "c" else 16)
-    total = {"sent": ROUNDS * len(engines)}
+    total = {"sent": ROUNDS * arrive}
     for o in ops:
         if o["kind"] in "cd":
             total[o["mark"][0]] = max(total.get(o["mark"][0], 0), o["mark"][1])

@@ -1,12 +1,11 @@
 import numpy as np
-from concourse.bass import DstId, RemoteDMATransfer
 from concourse.mybir import dt, AluOpType as ALU, ActivationFunctionType as ACT
 
 ROUNDS = 3
-CFG = {"iters": 36000, "xeng": "SSVVSSSV", "asplit": 8,
-       "ws": 200.0, "wx": 200.0, "lat": 3000.0, "f": 1.05, "gc": 1.4, "sfix": 30.0, "pe": 0.6}
-COSTS = [{}, {"ws": 100.0, "wx": 120.0, "lat": 4500.0, "f": 1.1, "gc": 1.5},
-         {"ws": 150.0, "wx": 250.0, "lat": 3500.0, "f": 1.3, "gc": 1.8}]
+CFG = {"iters": 105000, "aim": 0.5, "temp": 0.006, "xeng": "SSVVSSSV", "asplit": 8,
+       "ws": 200.0, "wx": 200.0, "lat": 3000.0, "f": 1.05, "gc": 1.4, "sfix": 60.0, "pe": 0.9}
+COSTS = [{}, {"ws": 120.0, "wx": 150.0, "lat": 4500.0, "f": 1.1, "gc": 1.5, "sfix": 120.0, "pe": 0.6},
+         {"ws": 170.0, "wx": 250.0, "lat": 3500.0, "f": 1.3, "gc": 1.8, "pe": 1.2}]
 
 BF, F32, I32, U16, MXC, U8 = "bfloat16", "float32", "int32", "uint16", "float8_e4m3fn_x4", "uint8"
 SB = {}
@@ -26,7 +25,7 @@ for _h in range(ROUNDS):
 PSUM = {"ps": 512, "pt": 512, "pd": 2048, "py": 1024}
 SCRATCH = {k: ("sbuf", [128, n], d) for k, (n, d) in SB.items()}
 SCRATCH.update({k: ("psum", [128, n], F32) for k, n in PSUM.items()})
-SEMAPHORES = ["cV", "cS", "cP", "cG", "sent", "arr0", "arr1", "arr2", "l0", "l1", "l2", "l3", "l4", "l5",
+SEMAPHORES = ["cV", "cS", "cP", "cG", "sent", "arr0", "arr1", "arr2", "l0", "l1", "l2", "l3", "l4", "l5", "l6",
               "soc", "ss0", "ss1", "ss2", "ss3", "sot", "sy0", "sy1"]
 
 
@@ -130,12 +129,13 @@ def build(cfg):
         add(q, "d", lambda g, T: (g.sync if q == "Y" else g.scalar).dma_start(*sides(T)), reads, writes, 60.0,
             sem=sem, lat=1500.0 + 4.0 * kb)
 
-    dma("S", "l0", lambda T: (T.ut[:], T.u[:]), [], [v("ut")], 128)
-    dma("Y", "l1", lambda T: (T.xn[:], T.x[:]), [], [v("xn")], 384)
-    dma("Y", "l2", lambda T: (T.ti[:], T.tri[:]), [], [v("ti")], 512)
-    dma("Y", "l3", lambda T: (T.wq[:].bitcast(dt.uint8), T.wc[:]), [], [v("wq")], 768)
-    dma("Y", "l4", lambda T: (T.wp[:], T.ws[:]), [], [v("wp")], 832)
-    dma("Y", "l5", lambda T: (T.vt[:], T.v[:]), [], [v("vt")], 960)
+    dma("Y", "l1", lambda T: (T.xn[:, 0:512], T.x[:, 0:512]), [], [v("xn", 0, 512)], 192)
+    dma("S", "l6", lambda T: (T.xn[:, 512:1024], T.x[:, 512:1024]), [], [v("xn", 512)], 256)
+    dma("Y", "l0", lambda T: (T.ut[:], T.u[:]), [], [v("ut")], 384)
+    dma("Y", "l2", lambda T: (T.ti[:], T.tri[:]), [v("xn", 0, 512)], [v("ti")], 128)
+    dma("Y", "l3", lambda T: (T.wq[:].bitcast(dt.uint8), T.wc[:]), [v("xn", 0, 512)], [v("wq")], 384)
+    dma("Y", "l4", lambda T: (T.wp[:], T.ws[:]), [v("xn", 0, 512)], [v("wp")], 448)
+    dma("Y", "l5", lambda T: (T.vt[:], T.v[:]), [v("xn", 0, 512)], [v("vt")], 576)
 
     memset(v("et"), 0.0)
     select(v("et", 3, s=4, n=128), [[-1, 128]], 0.5, 0, 1)
@@ -211,21 +211,20 @@ def build(cfg):
         last = h == ROUNDS - 1
         d1, tn = ("da", "db") if h % 2 == 0 else ("db", "da")
         if h == 0:
-            quant(v("qn"), v("sn"), v("xn"))
-            copy(words(v(qx)), ind(words(v("qn")), v("lm", 0, 17)))
-            act(v(sx), ind(v("sn"), v("lm", 0, 17)), func=ACT.Copy)
+            for k in range(2):
+                quant(*pair("qn", "sn", 128 * k, 128), v("xn", 512 * k, n=512))
+            for a, b in ((0, 10), (10, 17)):
+                copy(words(v(qx, 16 * a, 16 * b)), ind(words(v("qn")), v("lm", a, b)))
+                act(v(sx, 16 * a, 16 * b), ind(v("sn"), v("lm", a, b)), func=ACT.Copy)
             tab, win, mul, plus = v("tb"), v("tb"), 1.0, 0.0
-            mm(v("ps", 0, 272), uq, pair(qx, sx, 0, 272))
-            transpose(v("ts", 0, 256), v("ps", 0, 256))
-            transpose(v("ts", 256, 512), v("ps", 16, 272))
         else:
             quant(*pair(qx, sx, 0, 144), v("xt", 0, 576))
             quant(*pair(qx, sx, 144, 128), v("xt", 576, 1088))
             tab, win, mul, plus = v(d1, 4, 1280, 5), v(d1), 5.0, 4.0
-            for k, bank in enumerate(("ps", "pt")):
-                mm(v(bank, 0, 144), uq, pair(qx, sx, 128 * k, 144))
-                transpose(v("ts", 128 * k, n=128), v(bank, 0, 128))
-                transpose(v("ts", 256 + 128 * k, n=128), v(bank, 16, 144))
+        for k, bank in enumerate(("ps", "pt")):
+            mm(v(bank, 0, 144), uq, pair(qx, sx, 128 * k, 144))
+            transpose(v("ts", 128 * k, n=128), v(bank, 0, 128))
+            transpose(v("ts", 256 + 128 * k, n=128), v(bank, 16, 144))
         plane = [v("fh", 256 * b, n=256) for b in range(4)]
         for b in range(4):
             mm(v("pd", 512 * b, n=256), pair("qe", "se", 128 * b, 128), pair(qx, sx, 16, 256))
@@ -292,12 +291,15 @@ def build(cfg):
         tt(v("dl"), v("cc"), v("rho"), ALU.mult)
         act(v("er"), rows, func=ACT.Relu, bias=-14.0)
         tt(v("ev"), v("er", 0, 16), v("er", 16, 32), ALU.subtract)
-        act(v("ey"), ind(v("ev"), v("ly")))
-        act(v("dm", 2, 1280, 5), ind(v("cc"), v("lx")), scale=v("sm", 1, 2))
-        tt(v("tt"), ind(v("dl"), v("lx")), v("ey"), ALU.mult)
-        act(v(d1, 3, 1280, 5), ind(v("tt"), v("lm", 18, 34)))
-        act(v(d1, 2, 1280, 5), v("tt"))
-        scan(v(tn), v("dm"), v(d1))
+        for k in (0, 8):
+            act(v("ey", 16 * k, n=128), ind(v("ev"), v("ly", k, n=8)))
+            act(v("dm", 80 * k + 2, s=5, n=128), ind(v("cc"), v("lx", k, n=8)), scale=v("sm", 1, 2))
+            tt(v("tt", 16 * k, n=128), ind(v("dl"), v("lx", k, n=8)), v("ey", 16 * k, n=128), ALU.mult)
+        for k in (0, 8):
+            act(v(d1, 80 * k + 3, s=5, n=128), ind(v("tt"), v("lm", 18 + k, n=8)))
+            act(v(d1, 80 * k + 2, s=5, n=128), v("tt", 16 * k, n=128))
+        for k in range(0, 1280, 320):
+            scan(v(tn, k, n=320), v("dm", k, n=320), v(d1, k, n=320))
         if last:
             act(v("otf"), v(tn, 4, 1280, 5))
             dma("Y", "sot", lambda T: (T.ot[:], T.otf[:]), [v("otf")], [], 128)
@@ -400,6 +402,26 @@ def span(order, tab):
     return top
 
 
+def blocked(order, tab):
+    end, free, last, prev, top, tail = [0.0] * len(tab), {}, {}, [None] * len(tab), 0.0, None
+    for i in order:
+        e, c, ds, lat = tab[i]
+        t, p = free.get(e, 0.0), (last.get(e), True)
+        for d, gp in ds:
+            if end[d] + gp > t:
+                t, p = end[d] + gp, (d, False)
+        end[i] = free[e] = t + c
+        last[e], prev[i] = i, p
+        if t + c + lat > top:
+            top, tail = t + c + lat, i
+    out = []
+    while tail is not None:
+        if prev[tail][1] and prev[tail][0] is not None:
+            out.append((prev[tail][0], tail))
+        tail = prev[tail][0]
+    return out
+
+
 def refine(ops, order, cfg):
     n, tabs = len(ops), []
     for m in COSTS:
@@ -417,22 +439,41 @@ def refine(ops, order, cfg):
     keep = list(order)
     rng = np.random.default_rng(1)
     movable = [o["id"] for o in ops if o["kind"] == "c"]
+    fixed = set(o["id"] for o in ops if o["kind"] == "d" and not o["r"])
+    head = max(k for k, x in enumerate(order) if x in fixed)
+    pos, pairs = {x: k for k, x in enumerate(order)}, None
     for it in range(cfg["iters"]):
-        i = movable[int(rng.integers(len(movable)))]
-        pos = {x: k for k, x in enumerate(order)}
-        lo = max([pos[d] for d in ops[i]["dep"]] + [-1]) + 1
-        hi = min([pos[s] for s in succ[i]] + [n])
+        if pairs is None:
+            pairs = [p for t in tabs for p in blocked(order, t) if p[0] not in fixed and p[1] not in fixed]
+        r = float(rng.random())
+        if pairs and r < cfg["aim"]:
+            j, i = pairs[int(rng.integers(len(pairs)))]
+            i, way = (i, -1) if r < cfg["aim"] / 2 else (j, 1)
+        else:
+            i, way = movable[int(rng.integers(len(movable)))], 0
         p = pos[i]
-        cand = [k for k in range(max(lo, p - 40), min(hi, p + 40)) if k != p and ops[order[k]]["eng"] == ops[i]["eng"]
-                and not (ops[order[k]]["kind"] == "d" and not ops[order[k]]["r"])]
+        lo = max([pos[d] for d in ops[i]["dep"]] + [-1]) + 1 if way < 1 else p
+        hi = min([pos[s] for s in succ[i]] + [n]) if way > -1 else p
+        cand = [k for k in range(max(lo, p - 50), min(hi, p + 50)) if k != p and ops[order[k]]["eng"] == ops[i]["eng"]
+                and order[k] not in fixed]
         if not cand:
-            continue
+            ds = [d for d in (ops[i]["dep"] if way < 0 else succ[i]) if ops[d]["kind"] in "cr"]
+            if way == 0 or not ds:
+                continue
+            i = max(ds, key=pos.get) if way < 0 else min(ds, key=pos.get)
+            p = pos[i]
+            if way < 0:
+                k = min(p, max([pos[d] for d in ops[i]["dep"]] + [head]) + 1)
+            else:
+                k = min([pos[s] for s in succ[i]] + [n]) - 1
+            cand = [max(p - 12, min(p + 12, k))]
         new = list(order)
         new.pop(p)
         new.insert(cand[int(rng.integers(len(cand)))], i)
         x = sum(span(new, t) / b for t, b in zip(tabs, base))
-        if x <= cur + 0.004 * (1 - it / cfg["iters"]) * float(rng.random()):
-            order, cur = new, x
+        if x <= cur + cfg["temp"] * (1 - it / cfg["iters"]) * float(rng.random()):
+            order, cur, pairs = new, x, (pairs if x == cur else None)
+            pos = {y: k for k, y in enumerate(order)}
             if x < best:
                 best, keep = x, list(new)
     return keep, [round(span(keep, t)) for t in tabs]
@@ -448,7 +489,7 @@ def waits(ops, order, arrive):
         elif o["kind"] == "d":
             o["mark"] = (o["sem"], 16)
         elif o["kind"] == "a":
-            o["mark"] = ("arr%d" % o["emit"], arrive)
+            o["mark"] = ("arr%d" % o["emit"], arrive[o["emit"]])
             o["know"] = {}
             continue
         kn = known.setdefault(o["eng"], {})
@@ -482,31 +523,33 @@ def rank_program(g, core, T, topo):
         return
     nxt = T.cores[(rank + 1) % len(T.cores)]
     rid, pid = topo.addr(nxt)[:2]
-    mask = topo.mask(core, nxt)
-    arrive = 2 * len(topo.engines(core, nxt))
+    engines = topo.engines(core, nxt)
+    n = len(engines) // 2
+    sets = [(engines[:n], engines[n:])] + [(engines, engines)] * (ROUNDS - 1)
+    arrive = tuple(len(a) + len(b) for a, b in sets)
     ops, order = plan(arrive)
     queue = {"V": g.vector, "S": g.scalar, "P": g.tensor, "G": g, "Y": g.sync}
 
     def pass_on(h):
         qa, sa, qz, sz = [T["%s%d" % (k, h)] for k in ("qa", "sa", "qz", "sz")]
-        arr = T.sem["arr%d" % h]
-        g.remote_dma(qz[:, 128:192].bitcast(dt.uint8), qa[:, 0:64].bitcast(dt.uint8), arr, T.sem.sent, pid, rid, mask)
-        g.remote_dma(sz[:, 128:192], sa[:, 0:64], arr, T.sem.sent, pid, rid, mask)
+        arr, (ma, mb) = T.sem["arr%d" % h], [sum(1 << e for e in s) for s in sets[h]]
+        g.remote_dma(qz[:, 128:192].bitcast(dt.uint8), qa[:, 0:64].bitcast(dt.uint8), arr, T.sem.sent, pid, rid, ma)
+        g.remote_dma(sz[:, 128:192], sa[:, 0:64], arr, T.sem.sent, pid, rid, mb)
 
     for i in order:
         o = ops[i]
         if o["kind"] == "a":
             continue
         q = queue[o["eng"]]
-        for s, n in o["wait"]:
-            q.wait_ge(T.sem[s], n)
+        for s, k in o["wait"]:
+            q.wait_ge(T.sem[s], k)
         if o["kind"] == "r":
             pass_on(o["emit"])
         else:
             o["emit"](g, T).then_inc(T.sem[o["mark"][0]], 1 if o["kind"] == "c" else 16)
-    total = {"sent": ROUNDS * arrive}
+    total = {"sent": sum(arrive)}
     for o in ops:
         if o["kind"] in "cd":
             total[o["mark"][0]] = max(total.get(o["mark"][0], 0), o["mark"][1])
-    for s, n in total.items():
-        g.wait_ge(T.sem[s], n)
+    for s, k in total.items():
+        g.wait_ge(T.sem[s], k)

@@ -2,7 +2,8 @@ import numpy as np
 from concourse.mybir import dt, AluOpType as ALU, ActivationFunctionType as ACT
 
 ROUNDS = 3
-CFG = {"iters": 105000, "aim": 0.5, "temp": 0.006, "xeng": "SSVVSSSV", "asplit": 8,
+CFG = {"iters": 105000, "aim": 0.5, "temp": 0.006, "xeng": "SSVVSSSV", "runs": 9, "look": 4,
+       "zs": "SS", "wn": "SSSS", "ex": "S", "cx": "S", "sym": "S", "cp": "S", "tb": "V", "rw": "S",
        "ws": 200.0, "wx": 200.0, "lat": 3000.0, "f": 1.05, "gc": 1.4, "sfix": 60.0, "pe": 0.9}
 COSTS = [{}, {"ws": 120.0, "wx": 150.0, "lat": 4500.0, "f": 1.1, "gc": 1.5, "sfix": 120.0, "pe": 0.6},
          {"ws": 170.0, "wx": 250.0, "lat": 3500.0, "f": 1.3, "gc": 1.8, "pe": 1.2}]
@@ -10,12 +11,12 @@ COSTS = [{}, {"ws": 120.0, "wx": 150.0, "lat": 4500.0, "f": 1.1, "gc": 1.5, "sfi
 BF, F32, I32, U16, MXC, U8 = "bfloat16", "float32", "int32", "uint16", "float8_e4m3fn_x4", "uint8"
 SB = {}
 for _d, _names in (
-        (BF, "xn1024 ut512 vt512 et516 xt1088 gg240 sc256 fh1024 wn1536 ee288 oo8 gt128 ms128 ab512 zt512 zs512 tb256 "
-             "dm1280 da1280 db1280 rs512 sb8 ch192 ne256 nk256 cs256 cc16 rho16 dl16 er32 ev16 ey256 tt256 kf240 kd64 "
-             "kr256 jc288 ka16 kb16 kc16 ua32 ub32 uc32"),
-        (F32, "ts512 aa240 st288 kh144 den16 rec16 wv32 wt32 wu16 sm8 otf256 ys256 ct16 col8 gf2"),
-        (I32, "ti256 ia44 ib44 ic32 ij32 ie32 iw32 ig32 ih32 ik16 im16 iq16 ir16 ip2 it2"),
-        (U16, "oi8 oj8 ok8 il16 lm44 lab32 ly16 lx16 lc6 lt2"),
+        (BF, "xn1024 ut512 vt512 et516 xt1088 gg256 sc256 fh1024 wn1536 ee144 oo10 gt128 ms128 ab512 zt512 zs512 tb256 "
+             "dm1280 da1280 db1280 rs528 sb8 ch96 ne256 nk256 cs256 cc16 rho16 dl16 er32 ev16 ex256 tt256 kf240 kw240 "
+             "kd128 kr256 jc144 ka16 kb16 kc16 ua32 ub32 uc32 rw64 df32 hk256 hy256 hz256"),
+        (F32, "ts512 aa256 st144 kh144 kg16 den16 rec16 wv32 wt32 wu16 sm8 otf256 ys256 ct16 col8 gf8"),
+        (I32, "ti256 ia44 ib44 ic18 ij16 ie36 iw36 ig36 ih36 iu36 ik16 im16 iq16 ir16 ip4 it2"),
+        (U16, "oi8 oj8 ok8 il16 lm44 lab36 ly16 lx16 lc2 lt2"),
         (MXC, "wq512 qn256 qu128 qv128 qe512 qf256"), (U8, "wp512 sn256 su128 sv128 se512 sf256")):
     for _n in _names.split():
         SB[_n.rstrip("0123456789")] = (int(_n.lstrip("abcdefghijklmnopqrstuvwxyz")), _d)
@@ -91,8 +92,8 @@ def build(cfg):
     def ts(out, a, s1, op0, s2=None, op1=None):
         vec(lambda q: q.tensor_scalar, out, [a], [s1, None, op0] if op1 is None else [s1, s2, op0, op1])
 
-    def scan(out, a, b, op0=ALU.mult, op1=ALU.add):
-        vec(lambda q: q.tensor_tensor_scan, out, [a, b], [0.0, op0, op1])
+    def scan(out, a, b, op0=ALU.mult, op1=ALU.add, first=0.0):
+        vec(lambda q: q.tensor_tensor_scan, out, [a, b], [first, op0, op1])
 
     def transpose(out, a):
         vec(lambda q: q.transpose, out, [a], [])
@@ -110,6 +111,12 @@ def build(cfg):
         add("S", "c", lambda g, T: g.scalar.activation(ap(T, out), ap(T, a), func, **{k: ap(T, x) for k, x in kw.items()}),
             [a] + list(kw.values()), [out], cost)
 
+    def times(eng, out, a, c):
+        if eng == "V":
+            ts(out, a, c, ALU.mult)
+        else:
+            act(out, a, scale=c)
+
     def mm(out, l, r):
         add("P", "c", lambda g, T: g.tensor.matmul_mx(*[ap(T, x) for x in [out] + l + r], True, True),
             l + r, [out], (count(r[0]) + 16) * cfg["pe"])
@@ -121,8 +128,8 @@ def build(cfg):
         kw = {} if SB[out[1]][1] == I32 else {"allow_small_or_imprecise_dtypes": True}
         add("G", "c", lambda g, T: g.iota(ap(T, out), pattern, base, cm, **kw), [], [out], 130 + 2 * count(out) * cyc)
 
-    def select(out, pattern, val, base, cm):
-        add("G", "c", lambda g, T: g.affine_select(ap(T, out), ap(T, out), pattern, ALU.not_equal, val, base, cm),
+    def select(out, pattern, val, base, cm, op=ALU.not_equal):
+        add("G", "c", lambda g, T: g.affine_select(ap(T, out), ap(T, out), pattern, op, val, base, cm),
             [out], [out], 170 + 2 * count(out) * cyc)
 
     def dma(q, sem, sides, reads, writes, kb):
@@ -153,48 +160,66 @@ def build(cfg):
     copy(v("gf", 0, 1), v("ip", 0, 1))
     rep = v("col", 0, 1)
     copy(rep, v("im", 0, 1))
-    act(v("col", 1, 2), rep, bias=-15.75)
     ts(v("sb", 2, 3), v("im", 0, 1), 15.0, ALU.is_lt, 16.0, ALU.mult)
     act(v("col", 3, 4), v("sb", 2, 3), scale=16.0, bias=rep)
-    iota(v("ic"), [[1, 2], [1, 16]], 1, 1)
-    iota(v("ij"), [[1, 2], [1, 16]], 0, 0)
-    ts(v("ie"), v("ic"), 15, ALU.bitwise_and)
-    tt(v("ig", 0, 16), v("ie", 0, 16), v("ij", 0, 16), ALU.min)
-    ts(v("iw", 0, 16), v("ig", 0, 16), 1.0, ALU.add)
-    tt(v("iw", 16, 32), v("ie", 16, 32), v("ij", 16, 32), ALU.max)
-    ts(v("ig"), v("iw"), v("gf", 0, 1), ALU.add)
+    act(v("col", 1, 2), v("sb", 2, 3), scale=-1.0)
+    for a, n, base in ((0, 8, 0), (8, 4, 0), (12, 6, 6)):
+        iota(v("ic", a, n=n), [[2, n]], base, 0)
+    ts(v("ip", 1, 2), v("ik", 0, 1), 3, ALU.logical_shift_right, 1, ALU.bitwise_and)
+    ts(v("ip", 2, 3), v("ik", 0, 1), 7, ALU.bitwise_and)
+    copy(v("gf", 1, 3), v("ip", 1, 3))
+    act(v("gf", 3, 4), v("gf", 2, 3), bias=7.0)
+    ts(v("gf", 4, 5), v("gf", 2, 3), 7.0, ALU.is_lt)
+    act(v("gf", 5, 6), v("gf", 0, 1), scale=-1.0, bias=1.0)
+    act(v("gf", 6, 7), v("gf", 0, 1), scale=16.0)
+    ts(v("ie", 0, 18), v("ic"), v("gf", 1, 2), ALU.add, 14.0, ALU.min)
+    for a, op in ((0, ALU.min), (18, ALU.max)):
+        ts(v("iw", a, n=8), v("ie", 0, 8), v("gf", 2, 3), op, v("gf", 4, 5), ALU.mult)
+        ts(v("iw", a + 8, n=10), v("ie", 8, 18), v("gf", 3, 4), op)
+    ts(v("ig"), v("iw"), v("gf", 5, 6), ALU.add)
     ts(v("ih"), v("ig"), 1, ALU.bitwise_and)
-    ts(v("ig"), v("ih"), 15.0, ALU.mult)
-    tt(v("ih"), v("ig"), v("iw"), ALU.add)
-    ts(v("lab"), v("ih"), 16.0, ALU.mult)
-    copy(v("lx"), v("ij", 0, 16))
-    memset(v("kf"), 1.0)
-    select(v("kf"), [[1, 15], [1, 16]], -1.0, -14, 0)
+    ts(v("iu"), v("ig"), 8, ALU.bitwise_and)
+    ts(v("ie"), v("ih"), 7.0, ALU.mult)
+    tt(v("iw"), v("ie"), v("iu"), ALU.add)
+    tt(v("ih"), v("iw"), v("ig"), ALU.add)
+    ts(v("lab"), v("ih"), 16.0, ALU.mult, v("gf", 6, 7), ALU.add)
+    iota(v("ij"), [[1, 16]], 0, 0)
+    copy(v("lx"), v("ij"))
+    memset(v("kw"), 1.0)
+    select(v("kw"), [[1, 15], [-1, 8], [7, 2]], -1.0, -7, 0, ALU.is_ge)
+    memset(v("kw", 15, 240, 16), 1.0)
+    tt(v("kf", 1, 240), v("kw", 0, 239), v("kw", 1, 240), ALU.mult)
     memset(v("kf", 0, 240, 16), 0.0)
     memset(v("sc", 240, 256), 100.0)
-    iota(v("jc"), [[1, 9], [1, 2], [1, 16]], -12, 0)
-    iota(v("den"), [[1, 16]], 1, 0)
+    iota(v("jc"), [[1, 9], [1, 16]], -12, 0)
+    iota(v("kg"), [[1, 16]], 0, 0)
+    act(v("den"), v("kg"), bias=-0.4375)
     vec(lambda q: q.reciprocal, v("rec"), [v("den")], [], 18)
-    act(v("kh"), ind(v("rec"), v("ly", 0, 9)), scale=-1.0, bias=1.0)
-    memset(v("kh", 15, 144, 16), 15.0)
-    memset(v("kh", 0, 144, 32), 0.0)
-    memset(v("kh", 16, 144, 32), 16.0)
+    tt(v("kg", 1, 15), v("den", 0, 14), v("rec", 1, 15), ALU.mult)
+    act(v("kg", 0, 1), v("rec", 0, 1), scale=0.0625)
+    act(v("kg", 15, 16), v("den", 14, 15))
+    act(v("kh"), ind(v("kg"), v("ly", 0, 9)))
     iota(v("iq"), [[1, 16]], 128, -1)
     ts(v("ir"), v("iq"), 15, ALU.bitwise_and)
     ts(v("ka"), v("ir"), 0.0, ALU.is_equal, 128.0, ALU.mult)
     ts(v("kb"), v("ir"), 1.0, ALU.is_equal, -16.0, ALU.mult)
     tt(v("kc"), v("ka"), v("kb"), ALU.add)
-    act(v("kd"), ind(v("kc"), v("ly", 0, 4)))
+    act(v("kd"), ind(v("kc"), v("ly", 0, 8)))
     memset(v("xt", 0, 64), 0.0)
-    memset(v("lc"), 15)
-    memset(v("lc", 2, 3), 31)
-    memset(v("lc", 5, 6), 143)
+    iota(v("it", 0, 2), [[-256, 2]], 256, 0)
+    tt(v("ip", 0, 2), v("it"), v("ib", 34, 36), ALU.add)
+    copy(v("lc"), v("ip", 0, 2))
+    iota(v("rw", 1, 64, 2), [[0, 2], [1, 16]], 0, 0)
     memset(v("kr"), -1.0)
     memset(v("kr", 15, 256, 16), 15.0)
     memset(v("zt", 256, 512), 0.0)
-    for out, c in ((v("ch"), 0), (v("ne", 0, 256, 8), 0), (v("ne", 7, 256, 8), -1), (v("nk"), 0), (v("nk", 0, 256, 8), 1),
-                   (v("nk", 7, 256, 8), 1), (v("dm", 0, 1280, 5), 0), (v("dm", 1, 1280, 5), -1), (v("dm", 3, 1280, 5), 1),
-                   (v("dm", 4, 1280, 5), 1), (v("ua", 0, 32, 2), 128)):
+    w = 5
+    fills = [(v("ne", 0, 256, 8), 0), (v("ne", 132, 256, 8), 1), (v("ne", 135, 256, 8), -1), (v("nk"), 0), (v("nk", 0, 256, 8), 1),
+             (v("nk", 135, 256, 8), 1), (v("rs", 512, 528), 0), (v("ua", 0, 32, 2), 128)]
+    fills += [(v("dm", k, 256 * w, w), c) for k, c in enumerate((0, -1, 1, 1, 1)[:w]) if k != 2]
+    if "V" in cfg["ex"] + cfg["cx"]:
+        fills += [(v("hk"), 1), (v("hk", 0, 256, 16), 0), (v("hy"), 0), (v("hz"), 0)]
+    for out, c in fills:
         act(out, v("kr", 0, count(out)), scale=0.0, bias=float(c))
     iota(v("ct"), [[-1, 16]], 12, 0)
     iota(v("ub", 1, 32, 2), [[1, 16]], 8, 0)
@@ -216,33 +241,38 @@ def build(cfg):
             for a, b in ((0, 10), (10, 17)):
                 copy(words(v(qx, 16 * a, 16 * b)), ind(words(v("qn")), v("lm", a, b)))
                 act(v(sx, 16 * a, 16 * b), ind(v("sn"), v("lm", a, b)), func=ACT.Copy)
-            tab, win, mul, plus = v("tb"), v("tb"), 1.0, 0.0
         else:
             quant(*pair(qx, sx, 0, 144), v("xt", 0, 576))
             quant(*pair(qx, sx, 144, 128), v("xt", 576, 1088))
-            tab, win, mul, plus = v(d1, 4, 1280, 5), v(d1), 5.0, 4.0
+        tab = v("tb")
         for k, bank in enumerate(("ps", "pt")):
             mm(v(bank, 0, 144), uq, pair(qx, sx, 128 * k, 144))
-            transpose(v("ts", 128 * k, n=128), v(bank, 0, 128))
-            transpose(v("ts", 256 + 128 * k, n=128), v(bank, 16, 144))
+            transpose(v("ts", 256 * k, n=128), v(bank, 0, 128))
+            transpose(v("ts", 256 * k + 128, n=128), v(bank, 16, 144))
         plane = [v("fh", 256 * b, n=256) for b in range(4)]
         for b in range(4):
             mm(v("pd", 512 * b, n=256), pair("qe", "se", 128 * b, 128), pair(qx, sx, 16, 256))
             act(plane[b], v("pd", 512 * b, n=256))
-        k = cfg["asplit"]
-        copy(v("aa", 0, 16 * k), ind(v("ts"), v("lab", 16, 16 + k)))
-        act(v("aa", 16 * k, 240), ind(v("ts"), v("lab", 16 + k, 31)))
-        tt(v("gg"), ind(v("ts"), v("lab", 0, 15)), v("aa"), ALU.is_ge)
-        scan(v("sc", 0, 240), v("kf"), v("gg"))
+        for e, a, n, width in ((1, 0, 8, 256), (0, 8, 3, 256), (96, 12, 5, 512)):
+            act(v("aa", e, s=2, n=16 * n), ind(v("ts", 0, width), v("lab", a, n=n)))
+            tt(v("gg", e, s=2, n=16 * n), ind(v("ts"), v("lab", 18 + a, n=n)), v("aa", e, s=2, n=16 * n), ALU.is_le)
+        scan(v("sc", 0, 240), v("kf"), v("gg", 0, 240))
+        for a, b in ((0, cfg["runs"]), (cfg["runs"], 9)):
+            if a == b:
+                continue
+            tt(v("ee", 16 * a, 16 * b), ind(v("sc"), v("lm", 34, n=b - a)), v("jc", 16 * a, 16 * b), ALU.is_equal)
+            scan(v("st", 16 * a, 16 * b), v("kh", 16 * a, 16 * b), v("ee", 16 * a, 16 * b),
+                 first=v("st", 16 * a - 1, n=1) if a else 0.0)
+            ts(v("oo", a, b), v("st", 16 * a + 15, 16 * b, 16), 12582912.0, ALU.add, 12582912.0, ALU.subtract)
+            j = max(a - 1, 0)
+            ts(v("oi", j, b - 1), v("st", 16 * j + 31, 16 * b, 16), 16.0, ALU.mult, 7.0225, ALU.add)
+            ts(v("oj", j, b - 1), v("oo", j + 1, b), 16.0, ALU.mult, rep, ALU.add)
+        n = cfg["look"]
+        for j in range(0, 8, n):
+            copy(v("gt", 16 * j, n=16 * n), ind(tab, v("oi", j, n=n)))
+            scan(v("ms", 16 * j, n=16 * n), v("kd", 0, 16 * n), v("gt", 16 * j, n=16 * n), ALU.add, ALU.min)
+            ts(v("ok", j, n=n), v("ms", 16 * j + 15, s=16, n=n), 16.0, ALU.mult, v("col", 3, 4), ALU.add)
         for j in (0, 4):
-            e = 36 * j
-            tt(v("ee", e, n=144), ind(v("sc"), v("lm", 34, 43)), v("jc", 32 * j, n=144), ALU.is_equal)
-            scan(v("st", e, n=144), v("kh"), v("ee", e, n=144))
-            ts(v("oi", j, n=4), v("st", e + 31, s=32, n=4), mul, ALU.mult, plus + 0.25 - 17.0 * mul, ALU.add)
-            ts(v("oj", j, n=4), v("st", e + 47, s=32, n=4), 16.0, ALU.mult, v("col", 1, 2), ALU.add)
-            copy(v("gt", 16 * j, n=64), ind(win, v("oi", j, n=4)))
-            scan(v("ms", 16 * j, n=64), v("kd"), v("gt", 16 * j, n=64), ALU.add, ALU.min)
-            ts(v("ok", j, n=4), v("ms", 16 * j + 15, s=16, n=4), 16.0, ALU.mult, v("col", 3, 4), ALU.add)
             for b in range(4):
                 first = v("ab", 64 * (j + b), n=64)
                 act(first, ind(plane[b], v("oj", j, n=4)))
@@ -250,9 +280,9 @@ def build(cfg):
             quant(*(pair(qa, sa, 0, 128) if j == 0 else pair(qz, sz, 0, 128)), v("zt"))
             if j == 0:
                 snd = add("G", "r", h, pair(qa, sa, 0, 64), [], 150.0, lat=cfg["lat"])
-            act(v("zs", 64 * j, n=256), v("zt", 64 * j, n=256), scale=32.0)
+            times(cfg["zs"][j // 4], v("zs", 64 * j, n=256), v("zt", 64 * j, n=256), 32.0)
         for b in range(4):
-            act(v("wn", 384 * b + 128, n=256), plane[b], scale=64.0)
+            times(cfg["wn"][b], v("wn", 384 * b + 128, n=256), plane[b], 64.0)
             mm(v("pd", 512 * b, n=128), pair("wq", "wp", 128 * b, 128), pair(qz, sz, 0, 128))
             tt(v("wn", 384 * b + 64, n=64), v("pd", 512 * b + 64, n=64), v("zs", 256 + b, s=4, n=64), ALU.add)
         tt(v("ub", 0, 32, 2), v("sc", 15, 256, 16), v("ct"), ALU.add)
@@ -266,43 +296,69 @@ def build(cfg):
             transpose(v("wt"), v("wv"))
             act(v("wu"), ind(v("wt"), v("lt", 0, 1)))
             copy(v("il"), v("wu"))
-        ts(v("oo", 0, 4), v("st", 15, s=32, n=4), 12582912.0, ALU.add, 12582913.0, ALU.subtract)
         a_, b_, o2_, o3_ = [v("oo", i, n=1) for i in range(4)]
-        ts(v(d1, 0, 1280, 5), tab, a_, ALU.not_equal)
-        ts(v(d1, 1, 1280, 5), tab, b_, ALU.not_equal)
-        scan(v("rs", 0, 256), v(d1, 0, 1280, 5), v("kr"))
-        scan(v("rs", 256, 512), v(d1, 1, 1280, 5), v("kr"))
+        slot = lambda buf, k, a=0, n=256: v(buf, w * a + k, s=w, n=n)
+        ts(slot(d1, 0), tab, a_, ALU.not_equal)
+        ts(slot(d1, 1), tab, b_, ALU.not_equal)
+        scan(v("rs", 256, 512), slot(d1, 0), v("kr"))
+        scan(v("rs", 0, 256), slot(d1, 1), v("kr"))
         if h == 0:
-            act(v(d1, 4, 1280, 5), tab)
-        act(v("sb", 0, 1), o3_, scale=-1.0, bias=o2_)
+            act(slot(d1, w - 1), tab)
+        if cfg["rw"] == "S":
+            act(v("rw", 0, 64, 2), ind(v("rs", 0, 512), v("lc")))
+        else:
+            copy(v("rw", 0, 64, 2), ind(v("rs", 0, 512), v("lc")))
+        tt(v("df"), v("rs", 15, 512, 16), v("rs", 31, 528, 16), ALU.subtract)
+        act(v("sb", 0, 1), o2_, scale=-1.0, bias=o3_)
+        act(v("sb", 1, 2), o2_, bias=v("col", 1, 2))
         act(v("sm", 1, 2), a_, scale=-1.0, bias=b_)
-        ts(v("sm", 2, 3), v("ms", 15, 16), v("sb", 2, 3), ALU.add, o2_, ALU.not_equal)
-        ts(v("ch", 15, 16), v("sm", 2, 3), v("sb", 0, 1), ALU.mult, o3_, ALU.add)
-        rows = v("rs", 15, 512, 16)
-        for s in range(1, 7):
-            src = ind(v("ch", 32 * (s - 1), n=32), v("lc", 0 if s == 1 else 2, n=2)) if s < 6 else \
-                ind(v("ch", 32, 192), v("lc", 4, 6))
-            tt(v("ne", s, 256, 8), src, rows, ALU.not_equal)
-            if s < 6:
-                scan(v("ch", 32 * s, n=32), v("ne", s, 256, 8), v("kr", 0, 32))
+        ts(v("sb", 3, 4), v("ms", 15, 16), v("sb", 1, 2), ALU.is_equal, v("sb", 0, 1), ALU.mult)
+        ts(v("ne", 3, 256, 8), v("rw", 0, 64, 2), o2_, ALU.subtract, v("sb", 3, 4), ALU.not_equal)
+        ts(v("ne", 7, 128, 8), v("rw", 1, 32, 2), o2_, ALU.subtract, v("sb", 3, 4), ALU.not_equal)
+        z_ = v("rs", 271, 272)
+        for s, k in enumerate((3, 1, 2)):
+            n = 32 if s < 2 else 16
+            scan(v("ch", 32 * s, n=n), v("ne", k, s=8, n=n), v("df", 0, n))
+            if s < 2:
+                ts(v("ne", s + 1, 128, 4), v("rw", 0, 32), z_, ALU.subtract, v("ch", 32 * s + 15, n=1), ALU.not_equal)
+                ts(v("ne", 129 + s, 256, 4), v("rw", 32, 64), v("ch", 32 * s + 31, n=1), ALU.not_equal)
+            else:
+                ts(v("ne", 4, 128, 8), v("rw", 1, 32, 2), z_, ALU.subtract, v("ch", 32 * s + 15, n=1), ALU.not_equal)
         scan(v("cs"), v("ne"), v("nk"))
-        tt(v("cc"), v("cs", 7, 128, 8), v("cs", 135, 256, 8), ALU.max)
-        tt(v("rho"), v("rs", 271, 512, 16), v("rs", 15, 256, 16), ALU.subtract)
+        tt(v("cc"), v("cs", 135, 256, 8), v("cs", 7, 128, 8), ALU.is_ge)
+        tt(v("rho"), v("rs", 15, 256, 16), v("rs", 271, 512, 16), ALU.subtract)
         tt(v("dl"), v("cc"), v("rho"), ALU.mult)
-        act(v("er"), rows, func=ACT.Relu, bias=-14.0)
-        tt(v("ev"), v("er", 0, 16), v("er", 16, 32), ALU.subtract)
+        act(v("er"), v("rs", 15, 512, 16), func=ACT.Relu, bias=-14.0)
+        if cfg["ex"] == "V":
+            tt(v("hy", 0, 256, 16), v("er", 16, 32), v("er", 0, 16), ALU.subtract)
+            scan(v("ex"), v("hk"), v("hy"))
+        else:
+            tt(v("ev"), v("er", 16, 32), v("er", 0, 16), ALU.subtract)
+        if cfg["cx"] == "V":
+            ts(v("hz", 0, 256, 16), v("cc"), v("sm", 1, 2), ALU.mult)
+            scan(slot("dm", 2), v("hk"), v("hz"))
         for k in (0, 8):
-            act(v("ey", 16 * k, n=128), ind(v("ev"), v("ly", k, n=8)))
-            act(v("dm", 80 * k + 2, s=5, n=128), ind(v("cc"), v("lx", k, n=8)), scale=v("sm", 1, 2))
-            tt(v("tt", 16 * k, n=128), ind(v("dl"), v("lx", k, n=8)), v("ey", 16 * k, n=128), ALU.mult)
+            if cfg["ex"] == "S":
+                act(v("ex", 16 * k, n=128), ind(v("ev"), v("lx", k, n=8)))
+            if cfg["cx"] == "S":
+                act(slot("dm", 2, 16 * k, 128), ind(v("cc"), v("lx", k, n=8)), scale=v("sm", 1, 2))
+            if cfg["sym"] == "D":
+                act(v("tt", 16 * k, n=128), ind(v("ev"), v("ly", k, n=8)))
+                tt(slot(d1, 2, 16 * k, 128), ind(v("dl"), v("ly", k, n=8)), v("ex", 16 * k, n=128), ALU.mult)
+                tt(slot(d1, 3, 16 * k, 128), ind(v("dl"), v("lx", k, n=8)), v("tt", 16 * k, n=128), ALU.mult)
+            else:
+                tt(v("tt", 16 * k, n=128), ind(v("dl"), v("ly", k, n=8)), v("ex", 16 * k, n=128), ALU.mult)
         for k in (0, 8):
-            act(v(d1, 80 * k + 3, s=5, n=128), ind(v("tt"), v("lm", 18 + k, n=8)))
-            act(v(d1, 80 * k + 2, s=5, n=128), v("tt", 16 * k, n=128))
-        for k in range(0, 1280, 320):
-            scan(v(tn, k, n=320), v("dm", k, n=320), v(d1, k, n=320))
+            if cfg["sym"] == "S":
+                act(slot(d1, 3, 16 * k, 128), ind(v("tt"), v("lm", 18 + k, n=8)))
+                times(cfg["cp"], slot(d1, 2, 16 * k, 128), v("tt", 16 * k, n=128), 1.0)
+        for k in range(0, 256 * w, 64 * w):
+            scan(v(tn, k, n=64 * w), v("dm", k, n=64 * w), v(d1, k, n=64 * w))
         if last:
-            act(v("otf"), v(tn, 4, 1280, 5))
+            act(v("otf"), slot(tn, w - 1))
             dma("Y", "sot", lambda T: (T.ot[:], T.otf[:]), [v("otf")], [], 128)
+        else:
+            times(cfg["tb"], tab, slot(tn, w - 1), 1.0)
         add("A", "a", h, [], pair(qz, sz, 128, 64), 0.0, after=[snd["id"]])
         for b in range(4):
             mm(v("pd", 512 * b, n=128), pair("wq", "wp", 128 * b, 128), pair(qz, sz, 64, 128))

@@ -2,26 +2,28 @@ import numpy as np
 from concourse.mybir import dt, AluOpType as ALU, ActivationFunctionType as ACT
 
 ROUNDS = 3
-CFG = {"iters": 105000, "aim": 0.5, "temp": 0.006, "xeng": "SSVVSSSV", "runs": 9, "look": 4,
+CFG = {"iters": 105000, "aim": 0.5, "temp": 0.006, "xeng": "SSVVSSSV", "xlast": "SVSVSVSV", "runs": 9, "look": 8, "P": 9, "aa": "SSS", "sc": 2,
+       "passes": 34, "moves": 1500, "width": 120, "heat": 0.008, "seed": 1, "weight": (1.0, 1.0, 1.0),
        "zs": "SS", "wn": "SSSS", "ex": "S", "cx": "S", "sym": "S", "cp": "S", "tb": "V", "rw": "S",
-       "ws": 200.0, "wx": 200.0, "lat": 3000.0, "f": 1.05, "gc": 1.4, "sfix": 60.0, "pe": 0.9}
-COSTS = [{}, {"ws": 120.0, "wx": 150.0, "lat": 4500.0, "f": 1.1, "gc": 1.5, "sfix": 120.0, "pe": 0.6},
-         {"ws": 170.0, "wx": 250.0, "lat": 3500.0, "f": 1.3, "gc": 1.8, "pe": 1.2}]
+       "ws": 200.0, "wx": 200.0, "lat": 2400.0, "f": 1.1, "gc": 1.5, "sfix": 60.0, "pe": 0.8}
+COSTS = [{"lat": 2000.0, "f": 1.0, "gc": 1.3, "pe": 0.6},
+         {"lat": 2400.0, "f": 1.1, "gc": 1.5, "sfix": 90.0, "pe": 0.8},
+         {"ws": 230.0, "wx": 230.0, "lat": 2800.0, "f": 1.3, "gc": 1.8, "pe": 1.0}]
 
 BF, F32, I32, U16, MXC, U8 = "bfloat16", "float32", "int32", "uint16", "float8_e4m3fn_x4", "uint8"
 SB = {}
 for _d, _names in (
-        (BF, "xn1024 ut512 vt512 et516 xt1088 gg256 sc256 fh1024 wn1536 ee144 oo10 gt128 ms128 ab512 zt512 zs512 tb256 "
+        (BF, "xn1024 ut512 vt512 et516 xt1216 gg256 sc256 fh1024 wn1536 ee144 oo10 gt128 ms128 ab512 zt512 zs512 tb256 "
              "dm1280 da1280 db1280 rs528 sb8 ch96 ne256 nk256 cs256 cc16 rho16 dl16 er32 ev16 ex256 tt256 kf240 kw240 "
              "kd128 kr256 jc144 ka16 kb16 kc16 ua32 ub32 uc32 rw64 df32 hk256 hy256 hz256"),
-        (F32, "ts512 aa256 st144 kh144 kg16 den16 rec16 wv32 wt32 wu16 sm8 otf256 ys256 ct16 col8 gf8"),
-        (I32, "ti256 ia44 ib44 ic18 ij16 ie36 iw36 ig36 ih36 iu36 ik16 im16 iq16 ir16 ip4 it2"),
-        (U16, "oi8 oj8 ok8 il16 lm44 lab36 ly16 lx16 lc2 lt2"),
+        (F32, "ts512 aa256 st144 kh144 kg16 den16 rec16 wv32 wt32 wu16 sm8 otf256 ys256 num16 col12 gf6"),
+        (I32, "ti256 ia45 ib45 ic16 ie32 iw32 ig32 ih32 iu32 ik16 im16 iq32 ir32 ip7"),
+        (U16, "oi8 oj8 ok8 il16 lm46 lab32 ly16 lx16 lc2 lt2 lk4"),
         (MXC, "wq512 qn256 qu128 qv128 qe512 qf256"), (U8, "wp512 sn256 su128 sv128 se512 sf256")):
     for _n in _names.split():
         SB[_n.rstrip("0123456789")] = (int(_n.lstrip("abcdefghijklmnopqrstuvwxyz")), _d)
 for _h in range(ROUNDS):
-    for _n, _w, _d in (("qx", 272, MXC), ("sx", 272, U8), ("qa", 128, MXC), ("sa", 128, U8), ("qz", 192, MXC), ("sz", 192, U8)):
+    for _n, _w, _d in (("qx", 304, MXC), ("sx", 304, U8), ("qa", 128, MXC), ("sa", 128, U8), ("qz", 192, MXC), ("sz", 192, U8)):
         SB["%s%d" % (_n, _h)] = (_w, _d)
 PSUM = {"ps": 512, "pt": 512, "pd": 2048, "py": 1024}
 SCRATCH = {k: ("sbuf", [128, n], d) for k, (n, d) in SB.items()}
@@ -68,7 +70,7 @@ def ap(T, x):
 
 def build(cfg):
     ops = []
-    cyc = 0.83 * cfg["f"]
+    cyc, P = 0.83 * cfg["f"], cfg["P"]
 
     def add(eng, kind, emit, reads, writes, cost, **kw):
         o = {"eng": eng, "kind": kind, "emit": emit, "r": [w for x in reads for w in views(x)],
@@ -148,83 +150,82 @@ def build(cfg):
     select(v("et", 3, s=4, n=128), [[-1, 128]], 0.5, 0, 1)
     for b in range(4):
         quant(*pair("qe", "se", 128 * b, 128), v("et", 3 - b, n=512))
-    iota(v("ia", 0, 18), [[1, 18]], -1, 16)
-    iota(v("ia", 18, 34), [[1, 16]], 0, 16)
-    iota(v("ia", 34, 44), [[0, 10]], 15, 16)
+    def fill(out, c):
+        iota(out, [[0, count(out)]], c, 0)
+
+    iota(v("ia", 0, 11), [[0, 11]], 15, 16)
+    iota(v("ia", 11, 45), [[0, 2], [1, 17]], 0, 16)
     ts(v("ib"), v("ia"), 255, ALU.bitwise_and)
-    copy(v("lm"), v("ib"))
+    copy(v("lm", 0, 45), v("ib"))
     iota(v("ik"), [[0, 16]], 0, 1)
     ts(v("im"), v("ik"), 15, ALU.bitwise_and)
     copy(v("ly"), v("im"))
-    ts(v("ip", 0, 1), v("ik", 0, 1), 4, ALU.logical_shift_right, 1, ALU.bitwise_and)
-    copy(v("gf", 0, 1), v("ip", 0, 1))
-    rep = v("col", 0, 1)
-    copy(rep, v("im", 0, 1))
-    ts(v("sb", 2, 3), v("im", 0, 1), 15.0, ALU.is_lt, 16.0, ALU.mult)
-    act(v("col", 3, 4), v("sb", 2, 3), scale=16.0, bias=rep)
-    act(v("col", 1, 2), v("sb", 2, 3), scale=-1.0)
-    for a, n, base in ((0, 8, 0), (8, 4, 0), (12, 6, 6)):
-        iota(v("ic", a, n=n), [[2, n]], base, 0)
-    ts(v("ip", 1, 2), v("ik", 0, 1), 3, ALU.logical_shift_right, 1, ALU.bitwise_and)
-    ts(v("ip", 2, 3), v("ik", 0, 1), 7, ALU.bitwise_and)
-    copy(v("gf", 1, 3), v("ip", 1, 3))
-    act(v("gf", 3, 4), v("gf", 2, 3), bias=7.0)
-    ts(v("gf", 4, 5), v("gf", 2, 3), 7.0, ALU.is_lt)
-    act(v("gf", 5, 6), v("gf", 0, 1), scale=-1.0, bias=1.0)
-    act(v("gf", 6, 7), v("gf", 0, 1), scale=16.0)
-    ts(v("ie", 0, 18), v("ic"), v("gf", 1, 2), ALU.add, 14.0, ALU.min)
-    for a, op in ((0, ALU.min), (18, ALU.max)):
-        ts(v("iw", a, n=8), v("ie", 0, 8), v("gf", 2, 3), op, v("gf", 4, 5), ALU.mult)
-        ts(v("iw", a + 8, n=10), v("ie", 8, 18), v("gf", 3, 4), op)
-    ts(v("ig"), v("iw"), v("gf", 5, 6), ALU.add)
+    for k, (shift, mask) in enumerate(((0, 15), (4, 1), (3, 1), (0, 7), (0, 3), (2, 3), (0, 31))):
+        ts(v("ip", k, n=1), v("ik", 0, 1), shift, ALU.logical_shift_right, mask, ALU.bitwise_and)
+    copy(v("gf", 0, 6), v("ip", 0, 6))
+    copy(v("lt", 0, 1), v("ip", 6, 7))
+    rep, odd, high, low, mod4, div4 = [v("gf", k, n=1) for k in range(6)]
+    col = [v("col", k, n=1) for k in range(12)]
+    ts(v("sb", 2, 3), rep, 15.0, ALU.is_lt, 16.0, ALU.mult)
+    act(col[3], v("sb", 2, 3), scale=16.0, bias=rep)
+    act(col[1], v("sb", 2, 3), scale=-1.0)
+    iota(v("ic"), [[0, 2], [2, 8]], 0, 0)
+    act(col[4], low, bias=7.0)
+    act(col[5], low, scale=-1.0, bias=7.0)
+    act(col[6], low, func=ACT.Sign)
+    act(col[7], odd, scale=-1.0, bias=1.0)
+    act(col[8], odd, scale=16.0)
+    ts(v("ie", 0, 16), v("ic"), high, ALU.add, 14.0, ALU.min)
+    for a, op in ((0, ALU.min), (16, ALU.max)):
+        ts(v("iw", a, n=8), v("ie", 0, 8), col[5], op)
+        ts(v("iw", a + 8, n=8), v("ie", 8, 16), col[4], op, col[6], ALU.mult)
+    ts(v("ig"), v("iw"), col[7], ALU.add)
     ts(v("ih"), v("ig"), 1, ALU.bitwise_and)
-    ts(v("iu"), v("ig"), 8, ALU.bitwise_and)
-    ts(v("ie"), v("ih"), 7.0, ALU.mult)
-    tt(v("iw"), v("ie"), v("iu"), ALU.add)
-    tt(v("ih"), v("iw"), v("ig"), ALU.add)
-    ts(v("lab"), v("ih"), 16.0, ALU.mult, v("gf", 6, 7), ALU.add)
-    iota(v("ij"), [[1, 16]], 0, 0)
-    copy(v("lx"), v("ij"))
+    al, be, ga = {8: (7.0, 8.0, 0.0), 9: (9.0, 16.0, -16.0), 10: (9.0, 10.0, -4.0)}[P]
+    ts(v("iu"), v("ig"), float(P), ALU.is_ge)
+    ts(v("ie"), v("ih"), ga, ALU.mult, be, ALU.add)
+    tt(v("iw"), v("ie"), v("iu"), ALU.mult)
+    ts(v("iq"), v("ih"), al, ALU.mult)
+    tt(v("ir"), v("iq"), v("ig"), ALU.add)
+    tt(v("ih"), v("ir"), v("iw"), ALU.add)
+    ts(v("lab"), v("ih"), 16.0, ALU.mult, col[8], ALU.add)
+    iota(v("num"), [[1, 16]], 0, 0)
+    copy(v("lx"), v("num"))
     memset(v("kw"), 1.0)
-    select(v("kw"), [[1, 15], [-1, 8], [7, 2]], -1.0, -7, 0, ALU.is_ge)
-    memset(v("kw", 15, 240, 16), 1.0)
-    tt(v("kf", 1, 240), v("kw", 0, 239), v("kw", 1, 240), ALU.mult)
+    select(v("kw", 0, 240, 2), [[1, 15], [-1, 8]], -1.0, -7, 0, ALU.is_ge)
+    select(v("kw", 1, 240, 2), [[1, 15], [1, 8]], -1.0, -7, 0, ALU.is_ge)
+    act(v("kw", 0, 240, 16), v("num", 0, 15), scale=-1.0, bias=13.0)
+    tt(v("kf", 1, 120), v("kw", 0, 119), v("kw", 1, 120), ALU.mult)
+    tt(v("kf", 120, 240), v("kw", 119, 239), v("kw", 120, 240), ALU.mult)
     memset(v("kf", 0, 240, 16), 0.0)
-    memset(v("sc", 240, 256), 100.0)
-    iota(v("jc"), [[1, 9], [1, 16]], -12, 0)
-    iota(v("kg"), [[1, 16]], 0, 0)
-    act(v("den"), v("kg"), bias=-0.4375)
+    act(col[9], mod4, scale=256.0, bias=div4)
+    ts(v("lk"), v("num", 0, 16, 4), col[9], ALU.add)
+    iota(v("jc"), [[1, 9], [0, 16]], 0, 0)
+    act(v("den"), v("num"), bias=-0.4375)
     vec(lambda q: q.reciprocal, v("rec"), [v("den")], [], 18)
     tt(v("kg", 1, 15), v("den", 0, 14), v("rec", 1, 15), ALU.mult)
     act(v("kg", 0, 1), v("rec", 0, 1), scale=0.0625)
     act(v("kg", 15, 16), v("den", 14, 15))
     act(v("kh"), ind(v("kg"), v("ly", 0, 9)))
-    iota(v("iq"), [[1, 16]], 128, -1)
-    ts(v("ir"), v("iq"), 15, ALU.bitwise_and)
-    ts(v("ka"), v("ir"), 0.0, ALU.is_equal, 128.0, ALU.mult)
-    ts(v("kb"), v("ir"), 1.0, ALU.is_equal, -16.0, ALU.mult)
+    ts(v("ka"), v("num"), rep, ALU.is_equal, 128.0, ALU.mult)
+    act(col[10], rep, bias=1.0)
+    ts(v("kb"), v("num"), col[10], ALU.is_equal, -16.0, ALU.mult)
     tt(v("kc"), v("ka"), v("kb"), ALU.add)
     act(v("kd"), ind(v("kc"), v("ly", 0, 8)))
-    memset(v("xt", 0, 64), 0.0)
-    iota(v("it", 0, 2), [[-256, 2]], 256, 0)
-    tt(v("ip", 0, 2), v("it"), v("ib", 34, 36), ALU.add)
-    copy(v("lc"), v("ip", 0, 2))
+    act(v("sm", 4, 5), rep, scale=16.0, bias=271.0)
+    act(v("sm", 5, 6), rep, scale=16.0, bias=15.0)
+    copy(v("lc"), v("sm", 4, 6))
     iota(v("rw", 1, 64, 2), [[0, 2], [1, 16]], 0, 0)
-    memset(v("kr"), -1.0)
-    memset(v("kr", 15, 256, 16), 15.0)
-    memset(v("zt", 256, 512), 0.0)
+    iota(v("ub", 1, 30, 2), [[1, 15]], 9, 0)
     w = 5
-    fills = [(v("ne", 0, 256, 8), 0), (v("ne", 132, 256, 8), 1), (v("ne", 135, 256, 8), -1), (v("nk"), 0), (v("nk", 0, 256, 8), 1),
-             (v("nk", 135, 256, 8), 1), (v("rs", 512, 528), 0), (v("ua", 0, 32, 2), 128)]
+    fills = [(v("sc", 240, 256), 100), (v("kr"), -1), (v("kr", 15, 256, 16), 15), (v("zt", 256, 512), 0), (v("xt", 1024, 1216), 0),
+             (v("ne", 0, 256, 8), 0), (v("ne", 132, 256, 8), 1), (v("ne", 135, 256, 8), -1), (v("nk"), 0), (v("nk", 0, 256, 8), 1),
+             (v("nk", 135, 256, 8), 1), (v("rs", 512, 528), 0), (v("ua", 0, 32, 2), 128), (v("ub", 31, 32), 8)]
     fills += [(v("dm", k, 256 * w, w), c) for k, c in enumerate((0, -1, 1, 1, 1)[:w]) if k != 2]
     if "V" in cfg["ex"] + cfg["cx"]:
         fills += [(v("hk"), 1), (v("hk", 0, 256, 16), 0), (v("hy"), 0), (v("hz"), 0)]
     for out, c in fills:
-        act(out, v("kr", 0, count(out)), scale=0.0, bias=float(c))
-    iota(v("ct"), [[-1, 16]], 12, 0)
-    iota(v("ub", 1, 32, 2), [[1, 16]], 8, 0)
-    ts(v("it", 0, 1), v("ik", 0, 1), 31, ALU.bitwise_and)
-    copy(v("lt", 0, 1), v("it", 0, 1))
+        fill(out, c)
 
     quant(v("qu"), v("su"), v("ut"))
     copy(v("tb"), v("ti"))
@@ -238,29 +239,37 @@ def build(cfg):
         if h == 0:
             for k in range(2):
                 quant(*pair("qn", "sn", 128 * k, 128), v("xn", 512 * k, n=512))
-            for a, b in ((0, 10), (10, 17)):
-                copy(words(v(qx, 16 * a, 16 * b)), ind(words(v("qn")), v("lm", a, b)))
-                act(v(sx, 16 * a, 16 * b), ind(v("sn"), v("lm", a, b)), func=ACT.Copy)
+            for a, b in ((0, P + 2 - P % 2 - P % 2 + P % 2), (P + 2 - P % 2, 17)):
+                copy(words(v(qx, 16 * a, 16 * b)), ind(words(v("qn")), v("lm", 10 + a, 10 + b)))
+                act(v(sx, 16 * a, 16 * b), ind(v("sn"), v("lm", 10 + a, 10 + b)), func=ACT.Copy)
         else:
-            quant(*pair(qx, sx, 0, 144), v("xt", 0, 576))
-            quant(*pair(qx, sx, 144, 128), v("xt", 576, 1088))
-        tab = v("tb")
-        for k, bank in enumerate(("ps", "pt")):
-            mm(v(bank, 0, 144), uq, pair(qx, sx, 128 * k, 144))
-            transpose(v("ts", 256 * k, n=128), v(bank, 0, 128))
-            transpose(v("ts", 256 * k + 128, n=128), v(bank, 16, 144))
-        plane = [v("fh", 256 * b, n=256) for b in range(4)]
+            quant(*pair(qx, sx, 0, 16 * P + 16), v("xt", 0, 64 * P + 64))
+            quant(*pair(qx, sx, 16 * P + 16, 128), v("xt", 64 * P + 64, n=512))
+        tab, k = v("tb"), 16 if P == 10 and h == 0 else 0
+        mm(v("ps", 0, 16 * P + 16), uq, pair(qx, sx, 0, 16 * P + 16))
+        n = max(128, 272 - 16 * P)
+        mm(v("pt", 0, n), uq, pair(qx, sx, 16 * P - k, n))
+        a = 0
+        for bank, e, n in (("ps", 0, (P + 1) // 2), ("ps", 16, P // 2), ("pt", k, (17 - P) // 2), ("pt", k + 16, (16 - P) // 2)):
+            transpose(v("ts", a, n=32 * n), v(bank, e, n=32 * n))
+            a += 32 * n
+        whole = [v("fh", 256 * b, n=256) for b in range(4)]
+        plane = [v("fh", 256 * b + 16, n=240) for b in range(4)]
         for b in range(4):
-            mm(v("pd", 512 * b, n=256), pair("qe", "se", 128 * b, 128), pair(qx, sx, 16, 256))
-            act(plane[b], v("pd", 512 * b, n=256))
-        for e, a, n, width in ((1, 0, 8, 256), (0, 8, 3, 256), (96, 12, 5, 512)):
-            act(v("aa", e, s=2, n=16 * n), ind(v("ts", 0, width), v("lab", a, n=n)))
-            tt(v("gg", e, s=2, n=16 * n), ind(v("ts"), v("lab", 18 + a, n=n)), v("aa", e, s=2, n=16 * n), ALU.is_le)
-        scan(v("sc", 0, 240), v("kf"), v("gg", 0, 240))
+            mm(v("pd", 512 * b, n=256), pair("qe", "se", 128 * b, 128), pair(qx, sx, 0, 256))
+            act(whole[b], v("pd", 512 * b, n=256))
+        if not last:
+            act(v("xt", 0, 64), ind(v("fh"), v("lk")), scale=2.0)
+        for (e, a, n, width), eng in zip(((1, 0, 8, 32 * P), (0, 8, 4, 32 * P), (128, 12, 4, 512)) if P > 8 else
+                                         ((1, 0, 8, 512), (0, 8, 3, 512), (96, 10, 5, 512)), cfg["aa"]):
+            (act if eng == "S" else copy)(v("aa", e, s=2, n=16 * n), ind(v("ts", 0, width), v("lab", a, n=n)))
+            tt(v("gg", e, s=2, n=16 * n), ind(v("ts"), v("lab", 16 + a, n=n)), v("aa", e, s=2, n=16 * n), ALU.is_le)
+        for a, b in ((0, 128), (128, 240)) if cfg["sc"] == 2 else ((0, 240),):
+            scan(v("sc", a, b), v("kf", a, b), v("gg", a, b))
         for a, b in ((0, cfg["runs"]), (cfg["runs"], 9)):
             if a == b:
                 continue
-            tt(v("ee", 16 * a, 16 * b), ind(v("sc"), v("lm", 34, n=b - a)), v("jc", 16 * a, 16 * b), ALU.is_equal)
+            tt(v("ee", 16 * a, 16 * b), ind(v("sc"), v("lm", 0, n=b - a)), v("jc", 16 * a, 16 * b), ALU.is_equal)
             scan(v("st", 16 * a, 16 * b), v("kh", 16 * a, 16 * b), v("ee", 16 * a, 16 * b),
                  first=v("st", 16 * a - 1, n=1) if a else 0.0)
             ts(v("oo", a, b), v("st", 16 * a + 15, 16 * b, 16), 12582912.0, ALU.add, 12582912.0, ALU.subtract)
@@ -271,7 +280,7 @@ def build(cfg):
         for j in range(0, 8, n):
             copy(v("gt", 16 * j, n=16 * n), ind(tab, v("oi", j, n=n)))
             scan(v("ms", 16 * j, n=16 * n), v("kd", 0, 16 * n), v("gt", 16 * j, n=16 * n), ALU.add, ALU.min)
-            ts(v("ok", j, n=n), v("ms", 16 * j + 15, s=16, n=n), 16.0, ALU.mult, v("col", 3, 4), ALU.add)
+            ts(v("ok", j, n=n), v("ms", 16 * j + 15, s=16, n=n), 16.0, ALU.mult, col[3], ALU.add)
         for j in (0, 4):
             for b in range(4):
                 first = v("ab", 64 * (j + b), n=64)
@@ -282,14 +291,15 @@ def build(cfg):
                 snd = add("G", "r", h, pair(qa, sa, 0, 64), [], 150.0, lat=cfg["lat"])
             times(cfg["zs"][j // 4], v("zs", 64 * j, n=256), v("zt", 64 * j, n=256), 32.0)
         for b in range(4):
-            times(cfg["wn"][b], v("wn", 384 * b + 128, n=256), plane[b], 64.0)
+            times(cfg["wn"][b], v("wn", 384 * b + 128, n=256), whole[b], 64.0)
             mm(v("pd", 512 * b, n=128), pair("wq", "wp", 128 * b, 128), pair(qz, sz, 0, 128))
             tt(v("wn", 384 * b + 64, n=64), v("pd", 512 * b + 64, n=64), v("zs", 256 + b, s=4, n=64), ALU.add)
-        tt(v("ub", 0, 32, 2), v("sc", 15, 256, 16), v("ct"), ALU.add)
-        act(v("ua", 1, 32, 2), v("ub", 0, 32, 2), func=ACT.Relu, scale=64.0, bias=-448.0)
+        act(v("ub", 0, 32, 2), v("sc", 15, 256, 16))
+        act(v("ua", 1, 32, 2), v("sc", 15, 256, 16), func=ACT.Relu, scale=64.0, bias=-448.0)
         scan(v("uc"), v("ua"), v("ub"), ALU.max, ALU.min)
         if not last:
-            ts(v("il"), v("uc", 1, 32, 2), 16.0, ALU.mult, rep, ALU.add)
+            for a, b in ((0, P), (P, 15)) if P % 2 else ((0, 15),):
+                ts(v("il", a + a % 2, n=b - a), v("uc", 2 * a + 1, s=2, n=b - a), 16.0, ALU.mult, rep, ALU.add)
         else:
             act(v("wv", 0, 16), v("uc", 1, 32, 2), scale=16.0, bias=rep)
             act(v("wv", 16, 32), v("uc", 1, 32, 2), scale=16.0, bias=rep)
@@ -350,7 +360,7 @@ def build(cfg):
                 tt(v("tt", 16 * k, n=128), ind(v("dl"), v("ly", k, n=8)), v("ex", 16 * k, n=128), ALU.mult)
         for k in (0, 8):
             if cfg["sym"] == "S":
-                act(slot(d1, 3, 16 * k, 128), ind(v("tt"), v("lm", 18 + k, n=8)))
+                act(slot(d1, 3, 16 * k, 128), ind(v("tt"), v("lm", 28 + k, n=8)))
                 times(cfg["cp"], slot(d1, 2, 16 * k, 128), v("tt", 16 * k, n=128), 1.0)
         for k in range(0, 256 * w, 64 * w):
             scan(v(tn, k, n=64 * w), v("dm", k, n=64 * w), v(d1, k, n=64 * w))
@@ -363,13 +373,9 @@ def build(cfg):
         for b in range(4):
             mm(v("pd", 512 * b, n=128), pair("wq", "wp", 128 * b, 128), pair(qz, sz, 64, 128))
             tt(v("wn", 384 * b, n=64), v("pd", 512 * b + 64, n=64), v("zs", b, s=4, n=64), ALU.add)
-        for k, e in enumerate(cfg["xeng"]):
-            b, p = k % 4, 8 * (k // 4)
-            out, src = v("xt", 64 + b + 64 * p, s=4, n=128), ind(v("wn", 384 * b, n=384), v("il", p, n=8))
-            if e == "V":
-                ts(out, src, 0.03125, ALU.mult)
-            else:
-                act(out, src, scale=0.03125)
+        for k, e in enumerate(cfg["xlast" if last else "xeng"]):
+            b, (p, n) = k % 4, (((0, 8), (8, 8)) if last else ((0, P), (P, 15 - P)))[k // 4]
+            times(e, v("xt", 64 + b + 64 * p, s=4, n=16 * n), ind(v("wn", 384 * b, n=384), v("il", p + p % 2, n=n)), 0.03125)
 
     for k in range(2):
         quant(*pair("qf", "sf", 128 * k, 128), v("xt", 64 + 512 * k, n=512))
@@ -535,6 +541,147 @@ def refine(ops, order, cfg):
     return keep, [round(span(keep, t)) for t in tabs]
 
 
+def tables(ops, cfg):
+    tabs = []
+    for m in COSTS:
+        c = dict(cfg)
+        c.update(m)
+        new = build(c)
+        tabs.append([(o["eng"], new[o["id"]]["cost"], [(d, gap(c, new[d], new[o["id"]])) for d in o["dep"]],
+                      new[o["id"]]["lat"] if o["kind"] == "d" else 0.0) for o in ops])
+    reach, out = [0] * len(ops), [[] for t in tabs]
+    for i, o in enumerate(ops):
+        for d in o["dep"]:
+            reach[i] |= reach[d]
+        keep = [k for k, d in enumerate(o["dep"]) if not (reach[i] >> d) & 1 or ops[d]["lat"] > 0]
+        for d in o["dep"]:
+            reach[i] |= 1 << d
+        for t, x in zip(tabs, out):
+            x.append((t[i][0], t[i][1], [t[i][2][k] for k in keep], t[i][3]))
+    return out
+
+
+def window(tab, succ, order, a, b):
+    end, free, rest, q = {}, {}, {}, {}
+    for i in order[:a]:
+        e, c, ds, lat = tab[i]
+        end[i] = free[e] = max([free.get(e, 0.0)] + [end[d] + gp for d, gp in ds]) + c
+    for i in reversed(order[b:]):
+        e, c, ds, lat = tab[i]
+        q[i] = rest[e] = max([rest.get(e, 0.0), lat] + [q[d] + gp for d, gp in succ[i]]) + c
+    past = max([end[i] + tab[i][3] for i in end] + [end[i] + gp + q[d] for i in end for d, gp in succ[i] if d in q] + [0.0])
+    row = {i: (tab[i][0], tab[i][1], [(d, gp) for d, gp in tab[i][2] if d not in end],
+               max([end[d] + gp for d, gp in tab[i][2] if d in end] + [0.0]),
+               max([q[d] + gp for d, gp in succ[i] if d in q] + [tab[i][3]])) for i in order[a:b]}
+    return row, free, rest, past
+
+
+def value(w, loc, base):
+    tot = 0.0
+    for (row, free0, rest, top), bs in zip(loc, base):
+        free, end = dict(free0), {}
+        for i in w:
+            e, c, ds, t, q = row[i]
+            x = free.get(e, 0.0)
+            if x > t:
+                t = x
+            for d, gp in ds:
+                x = end[d] + gp
+                if x > t:
+                    t = x
+            t += c
+            end[i] = free[e] = t
+            if t + q > top:
+                top = t + q
+        for e, x in rest.items():
+            x += free.get(e, 0.0)
+            if x > top:
+                top = x
+        tot += top / bs
+    return tot
+
+
+def tight(w, loc):
+    out = []
+    for row, free0, rest, past in loc:
+        free, end, last, prev, top, tail = dict(free0), {}, {}, {}, 0.0, None
+        for i in w:
+            e, c, ds, t, q = row[i]
+            p = None
+            if free.get(e, 0.0) > t:
+                t, p = free[e], (last.get(e), True)
+            for d, gp in ds:
+                if end[d] + gp > t:
+                    t, p = end[d] + gp, (d, False)
+            end[i] = free[e] = t + c
+            last[e], prev[i] = i, p
+            if t + c + q > top:
+                top, tail = t + c + q, i
+        for e, x in rest.items():
+            if e in last and free[e] + x > top:
+                top, tail = free[e] + x, last[e]
+        while tail is not None and prev[tail] is not None:
+            if prev[tail][1] and prev[tail][0] is not None:
+                out.append((prev[tail][0], tail))
+            tail = prev[tail][0]
+    return out
+
+
+def improve(ops, order, cfg):
+    tabs, n, width, passes = tables(ops, cfg), len(ops), cfg["width"], cfg["passes"]
+    succ = [[[] for i in range(n)] for t in tabs]
+    for t, s in zip(tabs, succ):
+        for i in range(n):
+            for d, gp in t[i][2]:
+                s[d].append((i, gp))
+    near = {-1: [[d for d, g in t[2]] for t in tabs[0]], 1: [[d for d, g in s] for s in succ[0]]}
+    head = len([o for o in ops if o["kind"] == "d" and not o["r"]])
+    base = [span(order, t) / x for t, x in zip(tabs, cfg["weight"])]
+    rng = np.random.default_rng(cfg["seed"])
+    order = list(order)
+    best, keep = 1e9, list(order)
+    for ps in range(passes):
+        hot = cfg["heat"] * (1 - ps / passes) ** 2
+        for lo in range(head - (width // 4 if ps % 2 else 0), n - width // 4, width // 2):
+            a, b = max(lo, head), min(n, lo + width)
+            win = order[a:b]
+            loc = [window(t, s, order, a, b) for t, s in zip(tabs, succ)]
+            cur = low = value(win, loc, base)
+            good, pairs, m = win, None, len(win)
+            for r0, r1, r2, r3 in rng.random((cfg["moves"], 4)).tolist():
+                if pairs is None:
+                    pairs, pos = tight(win, loc), {x: k for k, x in enumerate(win)}
+                if pairs and r0 < 0.6:
+                    u, w = pairs[int(r1 * len(pairs))]
+                    i, way = (w, -1) if r0 < 0.3 else (u, 1)
+                    k = (pos[u] if way < 0 else pos[w]) + way * int(r2 * r2 * 16)
+                else:
+                    i, way = win[int(r1 * m)], (-1 if r0 < 0.8 else 1)
+                    k = pos[i] + way * (1 + int(r2 * r2 * 30))
+                k, p = max(0, min(m - 1, k)), pos[i]
+                if k == p:
+                    continue
+                grp, stack = {i}, [i]
+                while stack:
+                    for y in near[way][stack.pop()]:
+                        if y in pos and y not in grp and (pos[y] - k) * way <= 0:
+                            grp.add(y)
+                            stack.append(y)
+                s, e = min(k, p), max(k, p) + 1
+                one, two = [x for x in win[s:e] if x in grp], [x for x in win[s:e] if x not in grp]
+                new = win[:s] + (one + two if way < 0 else two + one) + win[e:]
+                x = value(new, loc, base)
+                if x <= cur + hot * r3:
+                    win, pairs, cur = new, None, x
+                    if x < low:
+                        low, good = x, new
+            order[a:b] = win if ps < passes - 1 and cur < low + hot else good
+        x = sum(span(order, t) / bs for t, bs in zip(tabs, base))
+        if x < best:
+            best, keep = x, list(order)
+    return keep, [round(span(keep, t)) for t in tabs]
+
+
 def waits(ops, order, arrive):
     done, known, pos = {}, {}, {x: k for k, x in enumerate(order)}
     for i in order:
@@ -567,7 +714,7 @@ def plan(arrive):
     if arrive not in PLAN:
         ops = build(CFG)
         depend(ops)
-        order = refine(ops, schedule(ops, CFG), CFG)[0]
+        order = improve(ops, schedule(ops, CFG), CFG)[0]
         waits(ops, order, arrive)
         PLAN[arrive] = (ops, order)
     return PLAN[arrive]

@@ -2,21 +2,21 @@ import numpy as np
 from concourse.mybir import dt, AluOpType as ALU, ActivationFunctionType as ACT
 
 ROUNDS = 3
-CFG = {"iters": 105000, "aim": 0.5, "temp": 0.006, "xeng": "SSVVSSSV", "xlast": "SVSVSVSV", "runs": 9, "look": 8, "P": 9, "aa": "SSS", "sc": 2,
-       "passes": 34, "moves": 1500, "width": 120, "heat": 0.008, "seed": 1, "weight": (1.0, 1.0, 1.0),
-       "zs": "SS", "wn": "SSSS", "ex": "S", "cx": "S", "sym": "S", "cp": "S", "tb": "V", "rw": "S",
-       "ws": 200.0, "wx": 200.0, "lat": 2400.0, "f": 1.1, "gc": 1.5, "sfix": 60.0, "pe": 0.8}
-COSTS = [{"lat": 2000.0, "f": 1.0, "gc": 1.3, "pe": 0.6},
-         {"lat": 2400.0, "f": 1.1, "gc": 1.5, "sfix": 90.0, "pe": 0.8},
-         {"ws": 230.0, "wx": 230.0, "lat": 2800.0, "f": 1.3, "gc": 1.8, "pe": 1.0}]
+CFG = {"xeng": "SSVVSSSV", "xlast": "SSVVSSVV", "runs": 5, "look": 4, "P": 9, "aa": 4, "gg": 4, "fill": "nk hk hy kr", "t0": "S", "sc": 2, "first": 4, "z": 4,
+       "passes": 72, "moves": 1500, "width": 120, "heat": 0.008, "seed": 1,
+       "gt": "SS", "ub": "S", "zs": "SS", "wn": "SSSS", "ex": "V", "oo": 2, "sym": "SSS", "otf": "VV", "cp": "GGG", "tb": "V", "rw": "S",
+       "ws": 200.0, "wx": 200.0, "lat": 2000.0, "f": 1.1, "gc": 1.5, "sfix": 60.0, "pe": 0.8, "issue": 150.0, "once": 300.0, "kb": 4.0}
+COSTS = [{"lat": 1900.0, "issue": 600.0, "once": 800.0, "f": 1.0, "gc": 1.3, "pe": 0.6},
+         {"lat": 1700.0, "f": 1.1, "gc": 1.5, "sfix": 90.0, "pe": 0.8},
+         {"ws": 220.0, "wx": 220.0, "lat": 1900.0, "issue": 300.0, "f": 1.35, "gc": 1.7, "pe": 1.0}]
 
 BF, F32, I32, U16, MXC, U8 = "bfloat16", "float32", "int32", "uint16", "float8_e4m3fn_x4", "uint8"
 SB = {}
 for _d, _names in (
         (BF, "xn1024 ut512 vt512 et516 xt1216 gg256 sc256 fh1024 wn1536 ee144 oo10 gt128 ms128 ab512 zt512 zs512 tb256 "
-             "dm1280 da1280 db1280 rs528 sb8 ch96 ne256 nk256 cs256 cc16 rho16 dl16 er32 ev16 ex256 tt256 kf240 kw240 "
-             "kd128 kr256 jc144 ka16 kb16 kc16 ua32 ub32 uc32 rw64 df32 hk256 hy256 hz256"),
-        (F32, "ts512 aa256 st144 kh144 kg16 den16 rec16 wv32 wt32 wu16 sm8 otf256 ys256 num16 col12 gf6"),
+             "dm1280 da1280 db1280 rs528 sb8 ch96 ne256 nk256 cs256 cc16 dl16 ev16 ex256 tt256 kf240 "
+             "kd128 kr256 jc144 ka16 kb16 kc16 ua32 ub32 uc32 rw64 df32 hk256 hy256"),
+        (F32, "rho16 ts512 aa256 st144 kh144 kg16 den16 rec16 wv32 wt32 wu16 sm8 otf256 ys256 num16 col12 gf6"),
         (I32, "ti256 ia45 ib45 ic16 ie32 iw32 ig32 ih32 iu32 ik16 im16 iq32 ir32 ip7"),
         (U16, "oi8 oj8 ok8 il16 lm46 lab32 ly16 lx16 lc2 lt2 lk4"),
         (MXC, "wq512 qn256 qu128 qv128 qe512 qf256"), (U8, "wp512 sn256 su128 sv128 se512 sf256")):
@@ -29,7 +29,7 @@ PSUM = {"ps": 512, "pt": 512, "pd": 2048, "py": 1024}
 SCRATCH = {k: ("sbuf", [128, n], d) for k, (n, d) in SB.items()}
 SCRATCH.update({k: ("psum", [128, n], F32) for k, n in PSUM.items()})
 SEMAPHORES = ["cV", "cS", "cP", "cG", "sent", "arr0", "arr1", "arr2", "l0", "l1", "l2", "l3", "l4", "l5", "l6",
-              "soc", "ss0", "ss1", "ss2", "ss3", "sot", "sy0", "sy1"]
+              "sc0", "sc1", "ss0", "ss1", "ss2", "ss3", "so0", "so1", "sy0", "sy1"]
 
 
 def v(name, a=0, b=None, s=1, n=None):
@@ -114,7 +114,10 @@ def build(cfg):
             [a] + list(kw.values()), [out], cost)
 
     def times(eng, out, a, c):
-        if eng == "V":
+        if eng == "G":
+            add("G", "c", lambda g, T: g.affine_select(ap(T, out), ap(T, a), [[0, count(a)]], ALU.is_ge, 0.0, 0, 0),
+                [a], [out], 170 + 2 * count(out) * cyc)
+        elif eng == "V":
             ts(out, a, c, ALU.mult)
         else:
             act(out, a, scale=c)
@@ -135,8 +138,10 @@ def build(cfg):
             [out], [out], 170 + 2 * count(out) * cyc)
 
     def dma(q, sem, sides, reads, writes, kb):
-        add(q, "d", lambda g, T: (g.sync if q == "Y" else g.scalar).dma_start(*sides(T)), reads, writes, 60.0,
-            sem=sem, lat=1500.0 + 4.0 * kb)
+        o = add(q, "d", lambda g, T: (g.sync if q == "Y" else g.scalar).dma_start(*sides(T)), reads, writes, 60.0,
+                sem=sem, lat=1500.0 + (cfg["kb"] * kb if writes else 0.0))
+        if not writes:
+            add("D", "t", None, [], [], cfg["kb"] * kb, after=[o["id"]])
 
     dma("Y", "l1", lambda T: (T.xn[:, 0:512], T.x[:, 0:512]), [], [v("xn", 0, 512)], 192)
     dma("S", "l6", lambda T: (T.xn[:, 512:1024], T.x[:, 512:1024]), [], [v("xn", 512)], 256)
@@ -151,7 +156,10 @@ def build(cfg):
     for b in range(4):
         quant(*pair("qe", "se", 128 * b, 128), v("et", 3 - b, n=512))
     def fill(out, c):
-        iota(out, [[0, count(out)]], c, 0)
+        if count(out) > 64 and out[1] not in cfg["fill"]:
+            memset(out, float(c))
+        else:
+            iota(out, [[0, count(out)]], c, 0)
 
     iota(v("ia", 0, 11), [[0, 11]], 15, 16)
     iota(v("ia", 11, 45), [[0, 2], [1, 17]], 0, 16)
@@ -191,13 +199,13 @@ def build(cfg):
     ts(v("lab"), v("ih"), 16.0, ALU.mult, col[8], ALU.add)
     iota(v("num"), [[1, 16]], 0, 0)
     copy(v("lx"), v("num"))
-    memset(v("kw"), 1.0)
-    select(v("kw", 0, 240, 2), [[1, 15], [-1, 8]], -1.0, -7, 0, ALU.is_ge)
-    select(v("kw", 1, 240, 2), [[1, 15], [1, 8]], -1.0, -7, 0, ALU.is_ge)
-    act(v("kw", 0, 240, 16), v("num", 0, 15), scale=-1.0, bias=13.0)
-    tt(v("kf", 1, 120), v("kw", 0, 119), v("kw", 1, 120), ALU.mult)
-    tt(v("kf", 120, 240), v("kw", 119, 239), v("kw", 120, 240), ALU.mult)
-    memset(v("kf", 0, 240, 16), 0.0)
+    memset(v("kf"), 1.0)
+    for e in (0, 1):
+        select(v("kf", e, 240, 2), [[-1, 15], [-1, 8]], -1.0, 8 - e, 0, ALU.is_gt)
+        select(v("kf", e, 240, 2), [[-1, 15], [1, 8]], 1.0, 7, 0, ALU.is_gt)
+    act(v("kf", 1, 112, 16), v("num", 0, 7), bias=-13.0)
+    act(v("kf", 113, 240, 16), v("num", 7, 15), scale=-1.0, bias=13.0)
+    act(v("kf", 0, 240, 16), v("num", 0, 15), scale=0.0)
     act(col[9], mod4, scale=256.0, bias=div4)
     ts(v("lk"), v("num", 0, 16, 4), col[9], ALU.add)
     iota(v("jc"), [[1, 9], [0, 16]], 0, 0)
@@ -222,13 +230,14 @@ def build(cfg):
              (v("ne", 0, 256, 8), 0), (v("ne", 132, 256, 8), 1), (v("ne", 135, 256, 8), -1), (v("nk"), 0), (v("nk", 0, 256, 8), 1),
              (v("nk", 135, 256, 8), 1), (v("rs", 512, 528), 0), (v("ua", 0, 32, 2), 128), (v("ub", 31, 32), 8)]
     fills += [(v("dm", k, 256 * w, w), c) for k, c in enumerate((0, -1, 1, 1, 1)[:w]) if k != 2]
-    if "V" in cfg["ex"] + cfg["cx"]:
-        fills += [(v("hk"), 1), (v("hk", 0, 256, 16), 0), (v("hy"), 0), (v("hz"), 0)]
+    if cfg["ex"] == "V":
+        fills += [(v("hk"), 1), (v("hk", 0, 256, 16), 0), (v("hy"), 0)]
     for out, c in fills:
         fill(out, c)
 
     quant(v("qu"), v("su"), v("ut"))
-    copy(v("tb"), v("ti"))
+    for a in (0, 128):
+        copy(v("tb", a, n=128), v("ti", a, n=128))
     quant(v("qv"), v("sv"), v("vt"))
     uq = pair("qu", "su", 0, 128)
 
@@ -260,10 +269,11 @@ def build(cfg):
             act(whole[b], v("pd", 512 * b, n=256))
         if not last:
             act(v("xt", 0, 64), ind(v("fh"), v("lk")), scale=2.0)
-        for (e, a, n, width), eng in zip(((1, 0, 8, 32 * P), (0, 8, 4, 32 * P), (128, 12, 4, 512)) if P > 8 else
-                                         ((1, 0, 8, 512), (0, 8, 3, 512), (96, 10, 5, 512)), cfg["aa"]):
-            (act if eng == "S" else copy)(v("aa", e, s=2, n=16 * n), ind(v("ts", 0, width), v("lab", a, n=n)))
-            tt(v("gg", e, s=2, n=16 * n), ind(v("ts"), v("lab", 16 + a, n=n)), v("aa", e, s=2, n=16 * n), ALU.is_le)
+        odd = ((1, 0, 4, 32 * P), (129, 4, 4, 512)) if cfg["gg"] == 4 else ((1, 0, 8, 512),)
+        for e, a, n, width in (odd if cfg["aa"] == 4 else ((1, 0, 8, 0),)) + ((0, 8, 4, 0), (128, 12, 4, 0)):
+            act(v("aa", e, s=2, n=16 * n), ind(v("ts", 0, 512 if a == 12 else 32 * P), v("lab", a, n=n)))
+        for e, a, n, width in odd + ((0, 8, 4, 512), (128, 12, 4, 512)):
+            tt(v("gg", e, s=2, n=16 * n), ind(v("ts", 0, width), v("lab", 16 + a, n=n)), v("aa", e, s=2, n=16 * n), ALU.is_le)
         for a, b in ((0, 128), (128, 240)) if cfg["sc"] == 2 else ((0, 240),):
             scan(v("sc", a, b), v("kf", a, b), v("gg", a, b))
         for a, b in ((0, cfg["runs"]), (cfg["runs"], 9)):
@@ -272,29 +282,38 @@ def build(cfg):
             tt(v("ee", 16 * a, 16 * b), ind(v("sc"), v("lm", 0, n=b - a)), v("jc", 16 * a, 16 * b), ALU.is_equal)
             scan(v("st", 16 * a, 16 * b), v("kh", 16 * a, 16 * b), v("ee", 16 * a, 16 * b),
                  first=v("st", 16 * a - 1, n=1) if a else 0.0)
-            ts(v("oo", a, b), v("st", 16 * a + 15, 16 * b, 16), 12582912.0, ALU.add, 12582912.0, ALU.subtract)
             j = max(a - 1, 0)
             ts(v("oi", j, b - 1), v("st", 16 * j + 31, 16 * b, 16), 16.0, ALU.mult, 7.0225, ALU.add)
+            if cfg["oo"] == 1:
+                if b < 9:
+                    continue
+                a = j = 0
+            ts(v("oo", a, b), v("st", 16 * a + 15, 16 * b, 16), 12582912.0, ALU.add, 12582912.0, ALU.subtract)
             ts(v("oj", j, b - 1), v("oo", j + 1, b), 16.0, ALU.mult, rep, ALU.add)
         n = cfg["look"]
         for j in range(0, 8, n):
-            copy(v("gt", 16 * j, n=16 * n), ind(tab, v("oi", j, n=n)))
+            (act if cfg["gt"][j // 4] == "S" else copy)(v("gt", 16 * j, n=16 * n), ind(tab, v("oi", j, n=n)))
             scan(v("ms", 16 * j, n=16 * n), v("kd", 0, 16 * n), v("gt", 16 * j, n=16 * n), ALU.add, ALU.min)
             ts(v("ok", j, n=n), v("ms", 16 * j + 15, s=16, n=n), 16.0, ALU.mult, col[3], ALU.add)
-        for j in (0, 4):
+        n, m = cfg["first"], cfg["z"]
+        for j in range(0, 8, n):
             for b in range(4):
-                first = v("ab", 64 * (j + b), n=64)
-                act(first, ind(plane[b], v("oj", j, n=4)))
-                tt(v("zt", 64 * j + b, s=4, n=64), ind(plane[b], v("ok", j, n=4)), first, ALU.add)
-            quant(*(pair(qa, sa, 0, 128) if j == 0 else pair(qz, sz, 0, 128)), v("zt"))
+                act(v("ab", 128 * b + 16 * j, n=16 * n), ind(plane[b], v("oj", j, n=n)))
+        for j in range(0, 8, m):
+            for b in range(4):
+                tt(v("zt", 64 * j + b, s=4, n=16 * m), ind(plane[b], v("ok", j, n=m)), v("ab", 128 * b + 16 * j, n=16 * m), ALU.add)
+            quant(*(pair(qa, sa, 0, 128) if j + m < 8 else pair(qz, sz, 0, 128)), v("zt"))
             if j == 0:
-                snd = add("G", "r", h, pair(qa, sa, 0, 64), [], 150.0, lat=cfg["lat"])
+                snd = add("G", "r", h, pair(qa, sa, 0, 64) if m < 8 else pair(qz, sz, 0, 64), [],
+                          cfg["issue"] + (0 if h else cfg["once"]), lat=cfg["lat"],
+                          after=[o["id"] for o in ops if o["eng"] == "G" and h == 0])
+        for j in (0, 4):
             times(cfg["zs"][j // 4], v("zs", 64 * j, n=256), v("zt", 64 * j, n=256), 32.0)
         for b in range(4):
             times(cfg["wn"][b], v("wn", 384 * b + 128, n=256), whole[b], 64.0)
             mm(v("pd", 512 * b, n=128), pair("wq", "wp", 128 * b, 128), pair(qz, sz, 0, 128))
             tt(v("wn", 384 * b + 64, n=64), v("pd", 512 * b + 64, n=64), v("zs", 256 + b, s=4, n=64), ALU.add)
-        act(v("ub", 0, 32, 2), v("sc", 15, 256, 16))
+        times(cfg["ub"], v("ub", 0, 32, 2), v("sc", 15, 256, 16), 1.0)
         act(v("ua", 1, 32, 2), v("sc", 15, 256, 16), func=ACT.Relu, scale=64.0, bias=-448.0)
         scan(v("uc"), v("ua"), v("ub"), ALU.max, ALU.min)
         if not last:
@@ -313,7 +332,7 @@ def build(cfg):
         scan(v("rs", 256, 512), slot(d1, 0), v("kr"))
         scan(v("rs", 0, 256), slot(d1, 1), v("kr"))
         if h == 0:
-            act(slot(d1, w - 1), tab)
+            times(cfg["t0"], slot(d1, w - 1), tab, 1.0)
         if cfg["rw"] == "S":
             act(v("rw", 0, 64, 2), ind(v("rs", 0, 512), v("lc")))
         else:
@@ -321,7 +340,6 @@ def build(cfg):
         tt(v("df"), v("rs", 15, 512, 16), v("rs", 31, 528, 16), ALU.subtract)
         act(v("sb", 0, 1), o2_, scale=-1.0, bias=o3_)
         act(v("sb", 1, 2), o2_, bias=v("col", 1, 2))
-        act(v("sm", 1, 2), a_, scale=-1.0, bias=b_)
         ts(v("sb", 3, 4), v("ms", 15, 16), v("sb", 1, 2), ALU.is_equal, v("sb", 0, 1), ALU.mult)
         ts(v("ne", 3, 256, 8), v("rw", 0, 64, 2), o2_, ALU.subtract, v("sb", 3, 4), ALU.not_equal)
         ts(v("ne", 7, 128, 8), v("rw", 1, 32, 2), o2_, ALU.subtract, v("sb", 3, 4), ALU.not_equal)
@@ -338,35 +356,25 @@ def build(cfg):
         tt(v("cc"), v("cs", 135, 256, 8), v("cs", 7, 128, 8), ALU.is_ge)
         tt(v("rho"), v("rs", 15, 256, 16), v("rs", 271, 512, 16), ALU.subtract)
         tt(v("dl"), v("cc"), v("rho"), ALU.mult)
-        act(v("er"), v("rs", 15, 512, 16), func=ACT.Relu, bias=-14.0)
         if cfg["ex"] == "V":
-            tt(v("hy", 0, 256, 16), v("er", 16, 32), v("er", 0, 16), ALU.subtract)
+            tt(v("hy", 0, 256, 16), v("ee", 0, 16), v("ee", 16, 32), ALU.subtract)
             scan(v("ex"), v("hk"), v("hy"))
         else:
-            tt(v("ev"), v("er", 16, 32), v("er", 0, 16), ALU.subtract)
-        if cfg["cx"] == "V":
-            ts(v("hz", 0, 256, 16), v("cc"), v("sm", 1, 2), ALU.mult)
-            scan(slot("dm", 2), v("hk"), v("hz"))
+            tt(v("ev"), v("ee", 0, 16), v("ee", 16, 32), ALU.subtract)
         for k in (0, 8):
             if cfg["ex"] == "S":
                 act(v("ex", 16 * k, n=128), ind(v("ev"), v("lx", k, n=8)))
-            if cfg["cx"] == "S":
-                act(slot("dm", 2, 16 * k, 128), ind(v("cc"), v("lx", k, n=8)), scale=v("sm", 1, 2))
-            if cfg["sym"] == "D":
-                act(v("tt", 16 * k, n=128), ind(v("ev"), v("ly", k, n=8)))
-                tt(slot(d1, 2, 16 * k, 128), ind(v("dl"), v("ly", k, n=8)), v("ex", 16 * k, n=128), ALU.mult)
-                tt(slot(d1, 3, 16 * k, 128), ind(v("dl"), v("lx", k, n=8)), v("tt", 16 * k, n=128), ALU.mult)
-            else:
-                tt(v("tt", 16 * k, n=128), ind(v("dl"), v("ly", k, n=8)), v("ex", 16 * k, n=128), ALU.mult)
+            act(slot("dm", 2, 16 * k, 128), ind(v("cc"), v("lx", k, n=8)), scale=v("rho", 15, 16))
+            tt(v("tt", 16 * k, n=128), ind(v("dl"), v("ly", k, n=8)), v("ex", 16 * k, n=128), ALU.mult)
         for k in (0, 8):
-            if cfg["sym"] == "S":
-                act(slot(d1, 3, 16 * k, 128), ind(v("tt"), v("lm", 28 + k, n=8)))
-                times(cfg["cp"], slot(d1, 2, 16 * k, 128), v("tt", 16 * k, n=128), 1.0)
+            act(slot(d1, 3, 16 * k, 128), ind(v("tt"), v("lm", 28 + k, n=8)))
+            times(cfg["cp"][h], slot(d1, 2, 16 * k, 128), v("tt", 16 * k, n=128), 1.0)
         for k in range(0, 256 * w, 64 * w):
             scan(v(tn, k, n=64 * w), v("dm", k, n=64 * w), v(d1, k, n=64 * w))
         if last:
-            act(v("otf"), slot(tn, w - 1))
-            dma("Y", "sot", lambda T: (T.ot[:], T.otf[:]), [v("otf")], [], 128)
+            for k in range(0, 256, 128):
+                times(cfg["otf"][k // 128], v("otf", k, n=128), slot(tn, w - 1, k, 128), 1.0)
+                dma("Y", "so%d" % (k // 128), lambda T, k=k: (T.ot[:, k:k + 128], T.otf[:, k:k + 128]), [v("otf", k, n=128)], [], 64)
         else:
             times(cfg["tb"], tab, slot(tn, w - 1), 1.0)
         add("A", "a", h, [], pair(qz, sz, 128, 64), 0.0, after=[snd["id"]])
@@ -380,7 +388,8 @@ def build(cfg):
     for k in range(2):
         quant(*pair("qf", "sf", 128 * k, 128), v("xt", 64 + 512 * k, n=512))
         mm(v("py", 512 * k, n=128), pair("qv", "sv", 0, 128), pair("qf", "sf", 128 * k, 128))
-    dma("Y", "soc", lambda T: (T.oc[:], T.qf[:].bitcast(dt.uint8)), [v("qf")], [], 128)
+        dma("Y", "sc%d" % k, lambda T, k=k: (T.oc[:, 512 * k:512 * k + 512], T.qf[:, 128 * k:128 * k + 128].bitcast(dt.uint8)),
+            [v("qf", 128 * k, n=128)], [], 64)
     for k in range(4):
         dma("SSYY"[k], "ss%d" % k, lambda T, k=k: (T.osc[4 * k:4 * k + 4, :], T.sf[32 * k:32 * k + 4, :]), [v("sf")], [], 1)
     act(v("ys", 0, 128), v("py", 0, 128))
@@ -421,7 +430,7 @@ def depend(ops):
 
 
 def gap(cfg, a, b):
-    if b["kind"] == "a":
+    if b["kind"] in "at":
         return a["lat"]
     return a["lat"] + (cfg["ws"] if a["eng"] == b["eng"] and a["kind"] == "c" else cfg["wx"])
 
@@ -464,83 +473,6 @@ def span(order, tab):
     return top
 
 
-def blocked(order, tab):
-    end, free, last, prev, top, tail = [0.0] * len(tab), {}, {}, [None] * len(tab), 0.0, None
-    for i in order:
-        e, c, ds, lat = tab[i]
-        t, p = free.get(e, 0.0), (last.get(e), True)
-        for d, gp in ds:
-            if end[d] + gp > t:
-                t, p = end[d] + gp, (d, False)
-        end[i] = free[e] = t + c
-        last[e], prev[i] = i, p
-        if t + c + lat > top:
-            top, tail = t + c + lat, i
-    out = []
-    while tail is not None:
-        if prev[tail][1] and prev[tail][0] is not None:
-            out.append((prev[tail][0], tail))
-        tail = prev[tail][0]
-    return out
-
-
-def refine(ops, order, cfg):
-    n, tabs = len(ops), []
-    for m in COSTS:
-        c = dict(cfg)
-        c.update(m)
-        new = build(c)
-        tabs.append([(o["eng"], new[o["id"]]["cost"], [(d, gap(c, new[d], new[o["id"]])) for d in o["dep"]],
-                      new[o["id"]]["lat"] if o["kind"] == "d" else 0.0) for o in ops])
-    succ = [[] for o in ops]
-    for o in ops:
-        for d in o["dep"]:
-            succ[d].append(o["id"])
-    base = [span(order, t) for t in tabs]
-    cur = best = float(len(tabs))
-    keep = list(order)
-    rng = np.random.default_rng(1)
-    movable = [o["id"] for o in ops if o["kind"] == "c"]
-    fixed = set(o["id"] for o in ops if o["kind"] == "d" and not o["r"])
-    head = max(k for k, x in enumerate(order) if x in fixed)
-    pos, pairs = {x: k for k, x in enumerate(order)}, None
-    for it in range(cfg["iters"]):
-        if pairs is None:
-            pairs = [p for t in tabs for p in blocked(order, t) if p[0] not in fixed and p[1] not in fixed]
-        r = float(rng.random())
-        if pairs and r < cfg["aim"]:
-            j, i = pairs[int(rng.integers(len(pairs)))]
-            i, way = (i, -1) if r < cfg["aim"] / 2 else (j, 1)
-        else:
-            i, way = movable[int(rng.integers(len(movable)))], 0
-        p = pos[i]
-        lo = max([pos[d] for d in ops[i]["dep"]] + [-1]) + 1 if way < 1 else p
-        hi = min([pos[s] for s in succ[i]] + [n]) if way > -1 else p
-        cand = [k for k in range(max(lo, p - 50), min(hi, p + 50)) if k != p and ops[order[k]]["eng"] == ops[i]["eng"]
-                and order[k] not in fixed]
-        if not cand:
-            ds = [d for d in (ops[i]["dep"] if way < 0 else succ[i]) if ops[d]["kind"] in "cr"]
-            if way == 0 or not ds:
-                continue
-            i = max(ds, key=pos.get) if way < 0 else min(ds, key=pos.get)
-            p = pos[i]
-            if way < 0:
-                k = min(p, max([pos[d] for d in ops[i]["dep"]] + [head]) + 1)
-            else:
-                k = min([pos[s] for s in succ[i]] + [n]) - 1
-            cand = [max(p - 12, min(p + 12, k))]
-        new = list(order)
-        new.pop(p)
-        new.insert(cand[int(rng.integers(len(cand)))], i)
-        x = sum(span(new, t) / b for t, b in zip(tabs, base))
-        if x <= cur + cfg["temp"] * (1 - it / cfg["iters"]) * float(rng.random()):
-            order, cur, pairs = new, x, (pairs if x == cur else None)
-            pos = {y: k for k, y in enumerate(order)}
-            if x < best:
-                best, keep = x, list(new)
-    return keep, [round(span(keep, t)) for t in tabs]
-
-
 def tables(ops, cfg):
     tabs = []
     for m in COSTS:
@@ -561,6 +493,9 @@ def tables(ops, cfg):
     return out
 
 
+QUEUES = "VSPGYAD"
+
+
 def window(tab, succ, order, a, b):
     end, free, rest, q = {}, {}, {}, {}
     for i in order[:a]:
@@ -576,13 +511,13 @@ def window(tab, succ, order, a, b):
     return row, free, rest, past
 
 
-def value(w, loc, base):
+def fits(w, s, loc, base, state, limit):
     tot = 0.0
-    for (row, free0, rest, top), bs in zip(loc, base):
-        free, end = dict(free0), {}
-        for i in w:
+    for (row, free0, rest, past), bs, (end0, frees, tops), lim in zip(loc, base, state, limit):
+        free, top, end = list(frees[s]), tops[s], list(end0)
+        for i in w[s:]:
             e, c, ds, t, q = row[i]
-            x = free.get(e, 0.0)
+            x = free[e]
             if x > t:
                 t = x
             for d, gp in ds:
@@ -591,25 +526,30 @@ def value(w, loc, base):
                     t = x
             t += c
             end[i] = free[e] = t
-            if t + q > top:
-                top = t + q
-        for e, x in rest.items():
-            x += free.get(e, 0.0)
-            if x > top:
-                top = x
-        tot += top / bs
-    return tot
+            t += q
+            if t > top:
+                top = t
+        for x, y in zip(rest, free):
+            if x + y > top:
+                top = x + y
+        tot += (top + 0.1 * sum(end) / len(end)) / bs
+        if tot > lim:
+            return False
+    return True
 
 
-def tight(w, loc):
-    out = []
+def trace(w, loc):
+    state, pairs, spans = [], [], []
     for row, free0, rest, past in loc:
-        free, end, last, prev, top, tail = dict(free0), {}, {}, {}, 0.0, None
+        free, top, end = list(free0), past, [0.0] * len(row)
+        frees, tops, last, prev, tail = [], [], [None] * len(free), [None] * len(row), None
         for i in w:
+            frees.append(tuple(free))
+            tops.append(top)
             e, c, ds, t, q = row[i]
             p = None
-            if free.get(e, 0.0) > t:
-                t, p = free[e], (last.get(e), True)
+            if free[e] > t:
+                t, p = free[e], (last[e], True)
             for d, gp in ds:
                 if end[d] + gp > t:
                     t, p = end[d] + gp, (d, False)
@@ -617,14 +557,16 @@ def tight(w, loc):
             last[e], prev[i] = i, p
             if t + c + q > top:
                 top, tail = t + c + q, i
-        for e, x in rest.items():
-            if e in last and free[e] + x > top:
-                top, tail = free[e] + x, last[e]
+        for e in range(len(free)):
+            if free[e] + rest[e] > top:
+                top, tail = free[e] + rest[e], last[e]
         while tail is not None and prev[tail] is not None:
             if prev[tail][1] and prev[tail][0] is not None:
-                out.append((prev[tail][0], tail))
+                pairs.append((prev[tail][0], tail))
             tail = prev[tail][0]
-    return out
+        state.append((end, frees, tops))
+        spans.append(top + 0.1 * sum(end) / len(end))
+    return state, pairs, spans
 
 
 def improve(ops, order, cfg):
@@ -634,48 +576,64 @@ def improve(ops, order, cfg):
         for i in range(n):
             for d, gp in t[i][2]:
                 s[d].append((i, gp))
-    near = {-1: [[d for d, g in t[2]] for t in tabs[0]], 1: [[d for d, g in s] for s in succ[0]]}
     head = len([o for o in ops if o["kind"] == "d" and not o["r"]])
-    base = [span(order, t) / x for t, x in zip(tabs, cfg["weight"])]
+    base = [span(order, t) for t in tabs]
     rng = np.random.default_rng(cfg["seed"])
     order = list(order)
     best, keep = 1e9, list(order)
     for ps in range(passes):
         hot = cfg["heat"] * (1 - ps / passes) ** 2
-        for lo in range(head - (width // 4 if ps % 2 else 0), n - width // 4, width // 2):
+        for lo in range(head - int(rng.integers(width // 2)), n - width // 4, width // 2):
             a, b = max(lo, head), min(n, lo + width)
-            win = order[a:b]
-            loc = [window(t, s, order, a, b) for t, s in zip(tabs, succ)]
-            cur = low = value(win, loc, base)
-            good, pairs, m = win, None, len(win)
-            for r0, r1, r2, r3 in rng.random((cfg["moves"], 4)).tolist():
+            ids = order[a:b]
+            m, at, loc = len(ids), {x: k for k, x in enumerate(ids)}, []
+            for t, s in zip(tabs, succ):
+                row, free, rest, past = window(t, s, order, a, b)
+                loc.append(([(QUEUES.index(row[i][0]), row[i][1], [(at[d], g) for d, g in row[i][2]]) + row[i][3:] for i in ids],
+                            [free.get(e, 0.0) for e in QUEUES], [rest.get(e, -1e9) for e in QUEUES], past))
+            eng = [r[0] for r in loc[0][0]]
+            near = {-1: [[d for d, g in r[2]] for r in loc[0][0]], 1: [[] for i in ids]}
+            for i, ds in enumerate(near[-1]):
+                for d in ds:
+                    near[1][d].append(i)
+            win, pairs, low = list(range(m)), None, 1e9
+            for r0, r1, r2, r3 in rng.random((cfg["moves"], 4)).tolist() + [[2.0] * 4]:
                 if pairs is None:
-                    pairs, pos = tight(win, loc), {x: k for k, x in enumerate(win)}
+                    state, pairs, spans = trace(win, loc)
+                    parts = [x / y for x, y in zip(spans, base)]
+                    cur, pos = sum(parts), [0] * m
+                    if cur < low:
+                        low, good = cur, win
+                    for k, x in enumerate(win):
+                        pos[x] = k
+                if r0 > 1.0:
+                    break
                 if pairs and r0 < 0.6:
                     u, w = pairs[int(r1 * len(pairs))]
                     i, way = (w, -1) if r0 < 0.3 else (u, 1)
-                    k = (pos[u] if way < 0 else pos[w]) + way * int(r2 * r2 * 16)
+                    k, hops = (pos[u] if way < 0 else pos[w]), int(r2 * r2 * 6)
                 else:
                     i, way = win[int(r1 * m)], (-1 if r0 < 0.8 else 1)
-                    k = pos[i] + way * (1 + int(r2 * r2 * 30))
-                k, p = max(0, min(m - 1, k)), pos[i]
-                if k == p:
-                    continue
+                    k, hops = pos[i], 1 + int(r2 * r2 * 8)
+                j, p = k, pos[i]
+                while hops and 0 <= j + way < m:
+                    j += way
+                    if eng[win[j]] == eng[i]:
+                        k, hops = j, hops - 1
                 grp, stack = {i}, [i]
                 while stack:
                     for y in near[way][stack.pop()]:
-                        if y in pos and y not in grp and (pos[y] - k) * way <= 0:
+                        if y not in grp and (pos[y] - k) * way <= 0:
                             grp.add(y)
                             stack.append(y)
                 s, e = min(k, p), max(k, p) + 1
                 one, two = [x for x in win[s:e] if x in grp], [x for x in win[s:e] if x not in grp]
-                new = win[:s] + (one + two if way < 0 else two + one) + win[e:]
-                x = value(new, loc, base)
-                if x <= cur + hot * r3:
-                    win, pairs, cur = new, None, x
-                    if x < low:
-                        low, good = x, new
-            order[a:b] = win if ps < passes - 1 and cur < low + hot else good
+                if two:
+                    new = win[:s] + (one + two if way < 0 else two + one) + win[e:]
+                    limit = [cur + hot * r3 - sum(parts[k + 1:]) + 0.004 * len(parts[k + 1:]) for k in range(len(parts))]
+                    if fits(new, s, loc, base, state, limit):
+                        win, pairs = new, None
+            order[a:b] = [ids[k] for k in (win if ps < passes - 1 and cur < low + hot else good)]
         x = sum(span(order, t) / bs for t, bs in zip(tabs, base))
         if x < best:
             best, keep = x, list(order)
@@ -686,6 +644,8 @@ def waits(ops, order, arrive):
     done, known, pos = {}, {}, {x: k for k, x in enumerate(order)}
     for i in order:
         o = ops[i]
+        if o["kind"] == "t":
+            continue
         if o["kind"] == "c":
             done[o["eng"]] = done.get(o["eng"], 0) + 1
             o["mark"] = ("c" + o["eng"], done[o["eng"]])
@@ -734,14 +694,14 @@ def rank_program(g, core, T, topo):
     queue = {"V": g.vector, "S": g.scalar, "P": g.tensor, "G": g, "Y": g.sync}
 
     def pass_on(h):
-        qa, sa, qz, sz = [T["%s%d" % (k, h)] for k in ("qa", "sa", "qz", "sz")]
+        qa, sa, qz, sz = [T["%s%d" % (k, h)] for k in (("qa", "sa") if CFG["z"] < 8 else ("qz", "sz")) + ("qz", "sz")]
         arr, (ma, mb) = T.sem["arr%d" % h], [sum(1 << e for e in s) for s in sets[h]]
         g.remote_dma(qz[:, 128:192].bitcast(dt.uint8), qa[:, 0:64].bitcast(dt.uint8), arr, T.sem.sent, pid, rid, ma)
         g.remote_dma(sz[:, 128:192], sa[:, 0:64], arr, T.sem.sent, pid, rid, mb)
 
     for i in order:
         o = ops[i]
-        if o["kind"] == "a":
+        if o["kind"] in "at":
             continue
         q = queue[o["eng"]]
         for s, k in o["wait"]:

@@ -2,23 +2,23 @@ import numpy as np
 from concourse.mybir import dt, AluOpType as ALU, ActivationFunctionType as ACT
 
 ROUNDS = 3
-CFG = {"xeng": "SSVVSSSV", "xlast": "SSVVSSVV", "runs": 5, "look": 4, "P": 9, "aa": 4, "gg": 4, "fill": "nk hk hy kr", "t0": "S", "sc": 2, "first": 4, "z": 4,
-       "passes": 72, "moves": 1500, "width": 120, "heat": 0.008, "seed": 1,
-       "gt": "SS", "ub": "S", "zs": "SS", "wn": "SSSS", "ex": "V", "oo": 2, "sym": "SSS", "otf": "VV", "cp": "GGG", "tb": "V", "rw": "S",
-       "ws": 200.0, "wx": 200.0, "lat": 2000.0, "f": 1.1, "gc": 1.5, "sfix": 60.0, "pe": 0.8, "issue": 150.0, "once": 300.0, "kb": 4.0}
-COSTS = [{"lat": 1900.0, "issue": 600.0, "once": 800.0, "f": 1.0, "gc": 1.3, "pe": 0.6},
-         {"lat": 1700.0, "f": 1.1, "gc": 1.5, "sfix": 90.0, "pe": 0.8},
-         {"ws": 220.0, "wx": 220.0, "lat": 1900.0, "issue": 300.0, "f": 1.35, "gc": 1.7, "pe": 1.0}]
+P = 9
+CFG = {"xeng": "SSVVSSSV", "xlast": "SSVVSSVV", "fill": "nk hk hq hx hy hz kr", "dl": (4, 4, 4), "parts": 4, "fast": (2,), "dq": 80.0,
+       "passes": 110, "moves": 400, "width": 44, "heat": 0.016, "seed": 1, "flip": 0.06, "put": 0.6,
+       "wake": 225.0, "lat": 1900.0, "f": 1.1, "gc": 1.5, "sfix": 60.0, "pe": 0.8, "issue": 150.0, "once": 300.0, "dma": 1500.0, "kb": 4.0}
+COSTS = [{"wake": 230.0, "lat": 1500.0, "issue": 300.0, "once": 800.0, "f": 1.05, "gc": 1.35, "pe": 0.6, "dma": 1200.0, "kb": 3.0},
+         {"wake": 200.0, "lat": 2200.0, "issue": 500.0, "f": 1.2, "gc": 1.8, "sfix": 80.0, "pe": 0.8, "dma": 1600.0, "kb": 4.0},
+         {"wake": 240.0, "lat": 1700.0, "issue": 200.0, "f": 1.45, "gc": 1.6, "pe": 0.7, "dma": 1300.0, "kb": 3.5}]
 
 BF, F32, I32, U16, MXC, U8 = "bfloat16", "float32", "int32", "uint16", "float8_e4m3fn_x4", "uint8"
 SB = {}
 for _d, _names in (
         (BF, "xn1024 ut512 vt512 et516 xt1216 gg256 sc256 fh1024 wn1536 ee144 oo10 gt128 ms128 ab512 zt512 zs512 tb256 "
-             "dm1280 da1280 db1280 rs528 sb8 ch96 ne256 nk256 cs256 cc16 dl16 ev16 ex256 tt256 kf240 "
-             "kd128 kr256 jc144 ka16 kb16 kc16 ua32 ub32 uc32 rw64 df32 hk256 hy256"),
-        (F32, "rho16 ts512 aa256 st144 kh144 kg16 den16 rec16 wv32 wt32 wu16 sm8 otf256 ys256 num16 col12 gf6"),
-        (I32, "ti256 ia45 ib45 ic16 ie32 iw32 ig32 ih32 iu32 ik16 im16 iq32 ir32 ip7"),
-        (U16, "oi8 oj8 ok8 il16 lm46 lab32 ly16 lx16 lc2 lt2 lk4"),
+             "dm1205 da1280 db1280 rs528 sb8 ch96 ne256 nk256 cs256 dl16 kf240 "
+             "kd64 kr256 jc144 ka16 kb16 kc16 ua32 ub32 uc32 rw64 df32 fl9 hk240 hq240 hx256 hy256 hz256"),
+        (F32, "ts576 aa256 st144 kh144 kg16 den15 rec14 wv32 wt32 wu16 sm2 otf256 ys256 nm17 col16 pc25 pb1 ia30"),
+        (I32, "ti256 ic16 ie16 iw32 ih32"),
+        (U16, "oi8 oj8 ok8 il16 lm30 lab32 lx16 ly16 lt2 lk4"),
         (MXC, "wq512 qn256 qu128 qv128 qe512 qf256"), (U8, "wp512 sn256 su128 sv128 se512 sf256")):
     for _n in _names.split():
         SB[_n.rstrip("0123456789")] = (int(_n.lstrip("abcdefghijklmnopqrstuvwxyz")), _d)
@@ -70,7 +70,7 @@ def ap(T, x):
 
 def build(cfg):
     ops = []
-    cyc, P = 0.83 * cfg["f"], cfg["P"]
+    cyc = 0.83 * cfg["f"]
 
     def add(eng, kind, emit, reads, writes, cost, **kw):
         o = {"eng": eng, "kind": kind, "emit": emit, "r": [w for x in reads for w in views(x)],
@@ -113,14 +113,26 @@ def build(cfg):
         add("S", "c", lambda g, T: g.scalar.activation(ap(T, out), ap(T, a), func, **{k: ap(T, x) for k, x in kw.items()}),
             [a] + list(kw.values()), [out], cost)
 
-    def times(eng, out, a, c):
-        if eng == "G":
-            add("G", "c", lambda g, T: g.affine_select(ap(T, out), ap(T, a), [[0, count(a)]], ALU.is_ge, 0.0, 0, 0),
-                [a], [out], 170 + 2 * count(out) * cyc)
-        elif eng == "V":
-            ts(out, a, c, ALU.mult)
-        else:
-            act(out, a, scale=c)
+    def either(engs):
+        forms = ops[-len(engs):]
+        del ops[len(ops) - len(engs) + 1:]
+        alts = {o["eng"]: (o["emit"], o["cost"]) for o in forms}
+        ops[-1].update(alts={**ops[-1].get("alts", {}), **alts}, r=[x for o in forms for x in o["r"]])
+
+    def lin(engs, out, a, scale=1.0, bias=None):
+        for e in engs:
+            if e == "G":
+                add("G", "c", lambda g, T: g.affine_select(ap(T, out), ap(T, a), [[0, count(a)]], ALU.is_ge, 0.0, 0, 0),
+                    [a], [out], 170 + 2 * count(out) * cyc)
+            elif e == "S":
+                act(out, a, **({"scale": scale} if bias is None else {"scale": scale, "bias": bias}))
+            elif bias is not None:
+                ts(out, a, scale, ALU.mult, bias, ALU.add)
+            elif scale == 1.0:
+                copy(out, a)
+            else:
+                ts(out, a, scale, ALU.mult)
+        either(engs)
 
     def mm(out, l, r):
         add("P", "c", lambda g, T: g.tensor.matmul_mx(*[ap(T, x) for x in [out] + l + r], True, True),
@@ -137,107 +149,110 @@ def build(cfg):
         add("G", "c", lambda g, T: g.affine_select(ap(T, out), ap(T, out), pattern, op, val, base, cm),
             [out], [out], 170 + 2 * count(out) * cyc)
 
+    def fill(out, c):
+        engs = "VG" if count(out) > 64 and out[1] not in cfg["fill"] else "GV"
+        for e in engs:
+            if e == "V":
+                memset(out, float(c))
+            else:
+                iota(out, [[0, count(out)]], c, 0)
+        either(engs)
+
     def dma(q, sem, sides, reads, writes, kb):
-        o = add(q, "d", lambda g, T: (g.sync if q == "Y" else g.scalar).dma_start(*sides(T)), reads, writes, 60.0,
-                sem=sem, lat=1500.0 + (cfg["kb"] * kb if writes else 0.0))
+        for e in q:
+            add(e, "d", lambda g, T, e=e: (g.sync if e == "Y" else g.scalar).dma_start(*sides(T)), reads, writes, cfg["dq"],
+                sem=sem, lat=cfg["dma"] + (cfg["kb"] * kb if writes else 0.0))
+        either(q)
+        o = ops[-1]
         if not writes:
             add("D", "t", None, [], [], cfg["kb"] * kb, after=[o["id"]])
 
     dma("Y", "l1", lambda T: (T.xn[:, 0:512], T.x[:, 0:512]), [], [v("xn", 0, 512)], 192)
     dma("S", "l6", lambda T: (T.xn[:, 512:1024], T.x[:, 512:1024]), [], [v("xn", 512)], 256)
     dma("Y", "l0", lambda T: (T.ut[:], T.u[:]), [], [v("ut")], 384)
-    dma("Y", "l2", lambda T: (T.ti[:], T.tri[:]), [v("xn", 0, 512)], [v("ti")], 128)
-    dma("Y", "l3", lambda T: (T.wq[:].bitcast(dt.uint8), T.wc[:]), [v("xn", 0, 512)], [v("wq")], 384)
-    dma("Y", "l4", lambda T: (T.wp[:], T.ws[:]), [v("xn", 0, 512)], [v("wp")], 448)
-    dma("Y", "l5", lambda T: (T.vt[:], T.v[:]), [v("xn", 0, 512)], [v("vt")], 576)
+    k = len(ops)
+    dma("Y", "l2", lambda T: (T.ti[:], T.tri[:]), [v("ut")], [v("ti")], 128)
+    dma("Y", "l3", lambda T: (T.wq[:].bitcast(dt.uint8), T.wc[:]), [v("ut")], [v("wq")], 384)
+    dma("Y", "l4", lambda T: (T.wp[:], T.ws[:]), [v("ut")], [v("wp")], 448)
+    dma("Y", "l5", lambda T: (T.vt[:], T.v[:]), [v("ut")], [v("vt")], 576)
 
     memset(v("et"), 0.0)
     select(v("et", 3, s=4, n=128), [[-1, 128]], 0.5, 0, 1)
     for b in range(4):
         quant(*pair("qe", "se", 128 * b, 128), v("et", 3 - b, n=512))
-    def fill(out, c):
-        if count(out) > 64 and out[1] not in cfg["fill"]:
-            memset(out, float(c))
-        else:
-            iota(out, [[0, count(out)]], c, 0)
-
-    iota(v("ia", 0, 11), [[0, 11]], 15, 16)
-    iota(v("ia", 11, 45), [[0, 2], [1, 17]], 0, 16)
-    ts(v("ib"), v("ia"), 255, ALU.bitwise_and)
-    copy(v("lm", 0, 45), v("ib"))
-    iota(v("ik"), [[0, 16]], 0, 1)
-    ts(v("im"), v("ik"), 15, ALU.bitwise_and)
-    copy(v("ly"), v("im"))
-    for k, (shift, mask) in enumerate(((0, 15), (4, 1), (3, 1), (0, 7), (0, 3), (2, 3), (0, 31))):
-        ts(v("ip", k, n=1), v("ik", 0, 1), shift, ALU.logical_shift_right, mask, ALU.bitwise_and)
-    copy(v("gf", 0, 6), v("ip", 0, 6))
-    copy(v("lt", 0, 1), v("ip", 6, 7))
-    rep, odd, high, low, mod4, div4 = [v("gf", k, n=1) for k in range(6)]
-    col = [v("col", k, n=1) for k in range(12)]
+    iota(v("pc"), [[256, 25]], 0, 1)
+    iota(v("pb"), [[0, 1]], 197184, 256)
+    iota(v("nm"), [[1, 17]], -1, 0)
+    num = lambda a=0, b=16, s=1: v("nm", a + 1, b + 1, s)
+    pc, fl, col = [[v(n, k, n=1) for k in range(SB[n][0])] for n in ("pc", "fl", "col")]
+    lin("SV", v("fl"), num(0, 9), pc[0], 6128.4)
+    rep, low, odd, high = col[12:16]
+    lin("SV", rep, fl[2], -0.5, pc[12])
+    lin("SV", col[2], fl[2], -0.5, pc[4])
+    lin("SV", low, fl[4], -0.25, pc[6])
+    lin("SV", odd, fl[1], -2.0, fl[2])
+    lin("SV", high, fl[2], -2.0, fl[4])
+    lin("SV", col[10], fl[8], -31.96875, v("pb"))
+    lin("SV", col[9], fl[2], -0.125, col[10])
+    lin("SV", col[1], rep, 16.0)
+    ts(v("lt", 0, 1), fl[1], -1.0, ALU.mult, pc[24], ALU.add)
+    ts(v("ly"), num(), 0.0, ALU.mult, rep, ALU.add)
+    ts(v("lx"), num(), 16.0, ALU.mult)
+    iota(v("ia"), [[0, 30]], 15, 0)
+    iota(v("ia", 11, 27), [[1, 16]], 0, 0)
+    iota(v("ia", 28, 29), [[0, 1]], 271, 0)
+    ts(v("lm"), v("ia"), col[1], ALU.add)
     ts(v("sb", 2, 3), rep, 15.0, ALU.is_lt, 16.0, ALU.mult)
-    act(col[3], v("sb", 2, 3), scale=16.0, bias=rep)
-    act(col[1], v("sb", 2, 3), scale=-1.0)
-    iota(v("ic"), [[0, 2], [2, 8]], 0, 0)
-    act(col[4], low, bias=7.0)
-    act(col[5], low, scale=-1.0, bias=7.0)
-    act(col[6], low, func=ACT.Sign)
-    act(col[7], odd, scale=-1.0, bias=1.0)
-    act(col[8], odd, scale=16.0)
-    ts(v("ie", 0, 16), v("ic"), high, ALU.add, 14.0, ALU.min)
+    lin("SV", col[3], v("sb", 2, 3), 16.0, col[2])
+    iota(v("ic"), [[0, 2], [66, 8]], 66, 0)
+    lin("SV", col[11], odd, -1.03125, -6039.0)
+    lin("SV", col[7], odd, -1.03125, -5808.0)
+    ts(col[0], high, odd, ALU.subtract, 1.03125, ALU.mult)
+    lin("SV", col[4], low, 33.0, col[11])
+    lin("SV", col[5], low, -33.0, col[11])
+    lin("SV", col[6], low, 512.0)
+    lin("SV", col[8], odd, 1.0, 6144.0)
+    ts(v("ie"), v("ic"), col[0], ALU.add, col[7], ALU.min)
     for a, op in ((0, ALU.min), (16, ALU.max)):
         ts(v("iw", a, n=8), v("ie", 0, 8), col[5], op)
-        ts(v("iw", a + 8, n=8), v("ie", 8, 16), col[4], op, col[6], ALU.mult)
-    ts(v("ig"), v("iw"), col[7], ALU.add)
-    ts(v("ih"), v("ig"), 1, ALU.bitwise_and)
-    al, be, ga = {8: (7.0, 8.0, 0.0), 9: (9.0, 16.0, -16.0), 10: (9.0, 10.0, -4.0)}[P]
-    ts(v("iu"), v("ig"), float(P), ALU.is_ge)
-    ts(v("ie"), v("ih"), ga, ALU.mult, be, ALU.add)
-    tt(v("iw"), v("ie"), v("iu"), ALU.mult)
-    ts(v("iq"), v("ih"), al, ALU.mult)
-    tt(v("ir"), v("iq"), v("ig"), ALU.add)
-    tt(v("ih"), v("ir"), v("iw"), ALU.add)
-    ts(v("lab"), v("ih"), 16.0, ALU.mult, col[8], ALU.add)
-    iota(v("num"), [[1, 16]], 0, 0)
-    copy(v("lx"), v("num"))
+        ts(v("iw", a + 8, n=8), v("ie", 8, 16), col[4], op, col[6], ALU.min)
+    ts(v("ih"), v("iw"), 0x3C1, ALU.bitwise_and)
+    ts(v("lab"), v("ih"), col[8], ALU.add)
     memset(v("kf"), 1.0)
-    for e in (0, 1):
-        select(v("kf", e, 240, 2), [[-1, 15], [-1, 8]], -1.0, 8 - e, 0, ALU.is_gt)
-        select(v("kf", e, 240, 2), [[-1, 15], [1, 8]], 1.0, 7, 0, ALU.is_gt)
-    act(v("kf", 1, 112, 16), v("num", 0, 7), bias=-13.0)
-    act(v("kf", 113, 240, 16), v("num", 7, 15), scale=-1.0, bias=13.0)
-    act(v("kf", 0, 240, 16), v("num", 0, 15), scale=0.0)
-    act(col[9], mod4, scale=256.0, bias=div4)
-    ts(v("lk"), v("num", 0, 16, 4), col[9], ALU.add)
+    select(v("kf"), [[-1, 15], [-1, 8], [-1, 2]], -1.0, 8, 0, ALU.is_gt)
+    select(v("kf"), [[-1, 15], [1, 8], [0, 2]], 1.0, 7, 0, ALU.is_gt)
+    for a, b, x, step, base in ((1, 112, 0, 1, -13), (113, 240, 7, -1, 13), (0, 240, 0, 0, 0)):
+        out = v("kf", a, b, 16)
+        lin("SV", out, num(x, x + count(out)), float(step), float(base))
+        iota(out, [[step, count(out)]], base + step * x, 0)
+        either("SG")
+    ts(v("lk"), num(0, 16, 4), col[9], ALU.add)
     iota(v("jc"), [[1, 9], [0, 16]], 0, 0)
-    act(v("den"), v("num"), bias=-0.4375)
-    vec(lambda q: q.reciprocal, v("rec"), [v("den")], [], 18)
-    tt(v("kg", 1, 15), v("den", 0, 14), v("rec", 1, 15), ALU.mult)
-    act(v("kg", 0, 1), v("rec", 0, 1), scale=0.0625)
-    act(v("kg", 15, 16), v("den", 14, 15))
-    act(v("kh"), ind(v("kg"), v("ly", 0, 9)))
-    ts(v("ka"), v("num"), rep, ALU.is_equal, 128.0, ALU.mult)
-    act(col[10], rep, bias=1.0)
-    ts(v("kb"), v("num"), col[10], ALU.is_equal, -16.0, ALU.mult)
+    iota(v("den"), [[16, 15]], -7, 0)
+    vec(lambda q: q.reciprocal, v("rec"), [v("den", 1, 15)], [])
+    ops[-1]["cost"] = 190 + 84 * cyc
+    tt(v("kg", 1, 15), v("den", 0, 14), v("rec"), ALU.mult)
+    lin("SV", v("kg", 0, 1), num(0, 1), 0.0, -1 / 7)
+    lin("SV", v("kg", 15, 16), num(0, 1), 0.0, 13.5625)
+    lin("SV", v("kh"), ind(v("kg"), v("ly", 0, 9)))
+    ts(v("ka"), num(), rep, ALU.is_equal, 256.0, ALU.mult)
+    ts(v("kb"), v("nm", 0, 16), rep, ALU.is_equal, -16.0, ALU.mult)
     tt(v("kc"), v("ka"), v("kb"), ALU.add)
-    act(v("kd"), ind(v("kc"), v("ly", 0, 8)))
-    act(v("sm", 4, 5), rep, scale=16.0, bias=271.0)
-    act(v("sm", 5, 6), rep, scale=16.0, bias=15.0)
-    copy(v("lc"), v("sm", 4, 6))
-    iota(v("rw", 1, 64, 2), [[0, 2], [1, 16]], 0, 0)
+    lin("SV", v("kd"), ind(v("kc"), v("ly", 0, 4)))
+    iota(v("rw", 1, 64, 2), [[0, 2], [1, 16]], 128, 0)
     iota(v("ub", 1, 30, 2), [[1, 15]], 9, 0)
     w = 5
-    fills = [(v("sc", 240, 256), 100), (v("kr"), -1), (v("kr", 15, 256, 16), 15), (v("zt", 256, 512), 0), (v("xt", 1024, 1216), 0),
-             (v("ne", 0, 256, 8), 0), (v("ne", 132, 256, 8), 1), (v("ne", 135, 256, 8), -1), (v("nk"), 0), (v("nk", 0, 256, 8), 1),
-             (v("nk", 135, 256, 8), 1), (v("rs", 512, 528), 0), (v("ua", 0, 32, 2), 128), (v("ub", 31, 32), 8)]
-    fills += [(v("dm", k, 256 * w, w), c) for k, c in enumerate((0, -1, 1, 1, 1)[:w]) if k != 2]
-    if cfg["ex"] == "V":
-        fills += [(v("hk"), 1), (v("hk", 0, 256, 16), 0), (v("hy"), 0)]
-    for out, c in fills:
+    for out, c in ((v("sc", 240, 256), 100), (v("ts", 0, 64, 2), 0), (v("ts", 513, 576, 2), 0), (v("kr"), -1), (v("kr", 15, 256, 16), 143), (v("zt", 256, 512), 0), (v("xt", 1024, 1216), 0),
+                   (v("ne", 0, 256, 8), 0), (v("ne", 132, 256, 8), 1), (v("ne", 135, 256, 8), -1), (v("nk"), 0), (v("nk", 0, 256, 8), 1),
+                   (v("nk", 135, 256, 8), 1), (v("rs", 512, 528), 0), (v("ua", 0, 32, 2), 128), (v("ub", 31, 32), 8),
+                   (v("dm", w, 241 * w, w), 0), (v("dm", w + 2, 241 * w, w), -1), (v("dm", 1204, 1205), 0), (v("hk"), 1), (v("hk", 0, 240, 16), 0),
+                   (v("hq"), 1), (v("hq", 0, 240, 16), 0), (v("hq", 1, 240, 16), -4096), (v("hx"), 0), (v("hy"), 0), (v("hz"), 0)):
         fill(out, c)
 
     quant(v("qu"), v("su"), v("ut"))
     for a in (0, 128):
-        copy(v("tb", a, n=128), v("ti", a, n=128))
+        lin("VS", v("tb", a, n=128), v("ti", a, n=128), 1.0, 128.0)
+    lin("SV", v("otf", 240, 256), v("ti", 240, 256))
     quant(v("qv"), v("sv"), v("vt"))
     uq = pair("qu", "su", 0, 128)
 
@@ -248,100 +263,88 @@ def build(cfg):
         if h == 0:
             for k in range(2):
                 quant(*pair("qn", "sn", 128 * k, 128), v("xn", 512 * k, n=512))
-            for a, b in ((0, P + 2 - P % 2 - P % 2 + P % 2), (P + 2 - P % 2, 17)):
+            for a, b in ((0, P + 1), (P + 1, 17)):
                 copy(words(v(qx, 16 * a, 16 * b)), ind(words(v("qn")), v("lm", 10 + a, 10 + b)))
                 act(v(sx, 16 * a, 16 * b), ind(v("sn"), v("lm", 10 + a, 10 + b)), func=ACT.Copy)
         else:
             quant(*pair(qx, sx, 0, 16 * P + 16), v("xt", 0, 64 * P + 64))
             quant(*pair(qx, sx, 16 * P + 16, 128), v("xt", 64 * P + 64, n=512))
-        tab, k = v("tb"), 16 if P == 10 and h == 0 else 0
+        tab = v("tb")
         mm(v("ps", 0, 16 * P + 16), uq, pair(qx, sx, 0, 16 * P + 16))
-        n = max(128, 272 - 16 * P)
-        mm(v("pt", 0, n), uq, pair(qx, sx, 16 * P - k, n))
-        a = 0
-        for bank, e, n in (("ps", 0, (P + 1) // 2), ("ps", 16, P // 2), ("pt", k, (17 - P) // 2), ("pt", k + 16, (16 - P) // 2)):
-            transpose(v("ts", a, n=32 * n), v(bank, e, n=32 * n))
-            a += 32 * n
+        mm(v("pt", 0, 128), uq, pair(qx, sx, 16 * P, 128))
+        for a, bank, e, n in ((1, "ps", 0, 160), (64, "ps", 16, 128), (320, "pt", 0, 128), (321, "pt", 16, 96)):
+            transpose(v("ts", a, s=2, n=n), v(bank, e, n=n))
         whole = [v("fh", 256 * b, n=256) for b in range(4)]
         plane = [v("fh", 256 * b + 16, n=240) for b in range(4)]
         for b in range(4):
             mm(v("pd", 512 * b, n=256), pair("qe", "se", 128 * b, 128), pair(qx, sx, 0, 256))
-            act(whole[b], v("pd", 512 * b, n=256))
+            lin("SV", whole[b], v("pd", 512 * b, n=256))
         if not last:
-            act(v("xt", 0, 64), ind(v("fh"), v("lk")), scale=2.0)
-        odd = ((1, 0, 4, 32 * P), (129, 4, 4, 512)) if cfg["gg"] == 4 else ((1, 0, 8, 512),)
-        for e, a, n, width in (odd if cfg["aa"] == 4 else ((1, 0, 8, 0),)) + ((0, 8, 4, 0), (128, 12, 4, 0)):
-            act(v("aa", e, s=2, n=16 * n), ind(v("ts", 0, 512 if a == 12 else 32 * P), v("lab", a, n=n)))
-        for e, a, n, width in odd + ((0, 8, 4, 512), (128, 12, 4, 512)):
-            tt(v("gg", e, s=2, n=16 * n), ind(v("ts", 0, width), v("lab", 16 + a, n=n)), v("aa", e, s=2, n=16 * n), ALU.is_le)
-        for a, b in ((0, 128), (128, 240)) if cfg["sc"] == 2 else ((0, 240),):
+            lin("SV", v("xt", 0, 64), ind(v("fh"), v("lk")), 2.0)
+        pieces = ((1, 0, 320), (129, 4, 576), (0, 8, 576), (128, 12, 576))
+        for e, a, width in pieces:
+            lin("SV", v("aa", e, s=2, n=64), ind(v("ts", 0, 576 if a == 12 else 320), v("lab", a, n=4)))
+        for e, a, width in pieces:
+            tt(v("gg", e, s=2, n=64), ind(v("ts", 0, width), v("lab", 16 + a, n=4)), v("aa", e, s=2, n=64), ALU.is_le)
+        for a, b in ((0, 128), (128, 240)):
             scan(v("sc", a, b), v("kf", a, b), v("gg", a, b))
-        for a, b in ((0, cfg["runs"]), (cfg["runs"], 9)):
-            if a == b:
-                continue
+        for a, b in ((0, 5), (5, 9)):
             tt(v("ee", 16 * a, 16 * b), ind(v("sc"), v("lm", 0, n=b - a)), v("jc", 16 * a, 16 * b), ALU.is_equal)
             scan(v("st", 16 * a, 16 * b), v("kh", 16 * a, 16 * b), v("ee", 16 * a, 16 * b),
                  first=v("st", 16 * a - 1, n=1) if a else 0.0)
             j = max(a - 1, 0)
             ts(v("oi", j, b - 1), v("st", 16 * j + 31, 16 * b, 16), 16.0, ALU.mult, 7.0225, ALU.add)
-            if cfg["oo"] == 1:
-                if b < 9:
-                    continue
-                a = j = 0
-            ts(v("oo", a, b), v("st", 16 * a + 15, 16 * b, 16), 12582912.0, ALU.add, 12582912.0, ALU.subtract)
-            ts(v("oj", j, b - 1), v("oo", j + 1, b), 16.0, ALU.mult, rep, ALU.add)
-        n = cfg["look"]
-        for j in range(0, 8, n):
-            (act if cfg["gt"][j // 4] == "S" else copy)(v("gt", 16 * j, n=16 * n), ind(tab, v("oi", j, n=n)))
-            scan(v("ms", 16 * j, n=16 * n), v("kd", 0, 16 * n), v("gt", 16 * j, n=16 * n), ALU.add, ALU.min)
-            ts(v("ok", j, n=n), v("ms", 16 * j + 15, s=16, n=n), 16.0, ALU.mult, col[3], ALU.add)
-        n, m = cfg["first"], cfg["z"]
-        for j in range(0, 8, n):
-            for b in range(4):
-                act(v("ab", 128 * b + 16 * j, n=16 * n), ind(plane[b], v("oj", j, n=n)))
-        for j in range(0, 8, m):
-            for b in range(4):
-                tt(v("zt", 64 * j + b, s=4, n=16 * m), ind(plane[b], v("ok", j, n=m)), v("ab", 128 * b + 16 * j, n=16 * m), ALU.add)
-            quant(*(pair(qa, sa, 0, 128) if j + m < 8 else pair(qz, sz, 0, 128)), v("zt"))
-            if j == 0:
-                snd = add("G", "r", h, pair(qa, sa, 0, 64) if m < 8 else pair(qz, sz, 0, 64), [],
-                          cfg["issue"] + (0 if h else cfg["once"]), lat=cfg["lat"],
-                          after=[o["id"] for o in ops if o["eng"] == "G" and h == 0])
+            ts(v("oo", a, b), v("st", 16 * a + 15, 16 * b, 16), 12582912.0, ALU.add, 12582784.0, ALU.subtract)
+            ts(v("oj", j, b - 1), v("oo", j + 1, b), 16.0, ALU.mult, col[2], ALU.add)
         for j in (0, 4):
-            times(cfg["zs"][j // 4], v("zs", 64 * j, n=256), v("zt", 64 * j, n=256), 32.0)
-        for b in range(4):
-            times(cfg["wn"][b], v("wn", 384 * b + 128, n=256), whole[b], 64.0)
-            mm(v("pd", 512 * b, n=128), pair("wq", "wp", 128 * b, 128), pair(qz, sz, 0, 128))
-            tt(v("wn", 384 * b + 64, n=64), v("pd", 512 * b + 64, n=64), v("zs", 256 + b, s=4, n=64), ALU.add)
-        times(cfg["ub"], v("ub", 0, 32, 2), v("sc", 15, 256, 16), 1.0)
-        act(v("ua", 1, 32, 2), v("sc", 15, 256, 16), func=ACT.Relu, scale=64.0, bias=-448.0)
+            lin("SV", v("gt", 16 * j, n=64), ind(tab, v("oi", j, n=4)))
+            scan(v("ms", 16 * j, n=64), v("kd", 0, 64), v("gt", 16 * j, n=64), ALU.add, ALU.min)
+            ts(v("ok", j, n=4), v("ms", 16 * j + 15, s=16, n=4), 16.0, ALU.mult, col[3], ALU.add)
+        for j in (0, 4):
+            for b in range(4):
+                lin("SV", v("ab", 128 * b + 16 * j, n=64), ind(plane[b], v("oj", j, n=4)))
+        for j in (0, 4):
+            for b in range(4):
+                tt(v("zt", 64 * j + b, s=4, n=64), ind(plane[b], v("ok", j, n=4)), v("ab", 128 * b + 16 * j, n=64), ALU.add)
+            quant(*(pair(qz, sz, 0, 128) if j else pair(qa, sa, 0, 128)), v("zt"))
+            if j == 0:
+                snd = add("G", "r", h, pair(qa, sa, 0, 64), [], cfg["issue"] + (0 if h else cfg["once"]), lat=cfg["lat"])
+        for j in (0, 4):
+            lin("SV", v("zs", 64 * j, n=256), v("zt", 64 * j, n=256), 32.0)
+        for b, (bank, a) in enumerate((("ps", 0), ("pt", 0), ("py", 0), ("py", 512))):
+            lin("SV", v("wn", 384 * b + 128, n=256), whole[b], 64.0)
+            mm(v(bank, a, n=128), pair("wq", "wp", 128 * b, 128), pair(qz, sz, 0, 128))
+            tt(v("wn", 384 * b + 64, n=64), v(bank, a + 64, n=64), v("zs", 256 + b, s=4, n=64), ALU.add)
+        lin("GSV", v("ub", 0, 32, 2), v("sc", 15, 256, 16))
+        lin("SV", v("ua", 1, 32, 2), v("sc", 15, 256, 16), 64.0, -448.0)
         scan(v("uc"), v("ua"), v("ub"), ALU.max, ALU.min)
         if not last:
-            for a, b in ((0, P), (P, 15)) if P % 2 else ((0, 15),):
+            for a, b in ((0, P), (P, 15)):
                 ts(v("il", a + a % 2, n=b - a), v("uc", 2 * a + 1, s=2, n=b - a), 16.0, ALU.mult, rep, ALU.add)
         else:
-            act(v("wv", 0, 16), v("uc", 1, 32, 2), scale=16.0, bias=rep)
-            act(v("wv", 16, 32), v("uc", 1, 32, 2), scale=16.0, bias=rep)
+            lin("SV", v("wv", 0, 16), v("uc", 1, 32, 2), 16.0, rep)
+            lin("SV", v("wv", 16, 32), v("uc", 1, 32, 2), 16.0, rep)
             transpose(v("wt"), v("wv"))
-            act(v("wu"), ind(v("wt"), v("lt", 0, 1)))
+            lin("SV", v("wu"), ind(v("wt"), v("lt", 0, 1)))
             copy(v("il"), v("wu"))
         a_, b_, o2_, o3_ = [v("oo", i, n=1) for i in range(4)]
-        slot = lambda buf, k, a=0, n=256: v(buf, w * a + k, s=w, n=n)
-        ts(slot(d1, 0), tab, a_, ALU.not_equal)
-        ts(slot(d1, 1), tab, b_, ALU.not_equal)
-        scan(v("rs", 256, 512), slot(d1, 0), v("kr"))
-        scan(v("rs", 0, 256), slot(d1, 1), v("kr"))
+        slot = lambda buf, k, a=0, n=240: v(buf, w * a + k, s=w, n=n)
+        ts(slot(d1, 1, 0, 256), tab, a_, ALU.not_equal)
+        ts(slot(d1, 2, 0, 256), tab, b_, ALU.not_equal)
+        scan(v("rs", 256, 512), slot(d1, 1, 0, 256), v("kr"))
+        scan(v("rs", 0, 256), slot(d1, 2, 0, 256), v("kr"))
         if h == 0:
-            times(cfg["t0"], slot(d1, w - 1), tab, 1.0)
-        if cfg["rw"] == "S":
-            act(v("rw", 0, 64, 2), ind(v("rs", 0, 512), v("lc")))
-        else:
-            copy(v("rw", 0, 64, 2), ind(v("rs", 0, 512), v("lc")))
+            lin("GSV", slot(d1, 4), v("tb", 0, 240))
+        lin("SV", v("rw", 0, 64, 2), ind(v("rs", 0, 512), v("lm", 28, 30)))
         tt(v("df"), v("rs", 15, 512, 16), v("rs", 31, 528, 16), ALU.subtract)
-        act(v("sb", 0, 1), o2_, scale=-1.0, bias=o3_)
-        act(v("sb", 1, 2), o2_, bias=v("col", 1, 2))
+        lin("SV", v("sb", 0, 1), o2_, -1.0, o3_)
+        lin("SV", v("sb", 1, 2), v("sb", 2, 3), -1.0, o2_)
         ts(v("sb", 3, 4), v("ms", 15, 16), v("sb", 1, 2), ALU.is_equal, v("sb", 0, 1), ALU.mult)
-        ts(v("ne", 3, 256, 8), v("rw", 0, 64, 2), o2_, ALU.subtract, v("sb", 3, 4), ALU.not_equal)
+        if h in cfg["fast"]:
+            for a in (0, 1):
+                ts(v("ne", 3 + 128 * a, s=8, n=16), v("rs", 271 - 256 * a, s=16, n=16), o2_, ALU.subtract, v("sb", 3, 4), ALU.not_equal)
+        else:
+            ts(v("ne", 3, 256, 8), v("rw", 0, 64, 2), o2_, ALU.subtract, v("sb", 3, 4), ALU.not_equal)
         ts(v("ne", 7, 128, 8), v("rw", 1, 32, 2), o2_, ALU.subtract, v("sb", 3, 4), ALU.not_equal)
         z_ = v("rs", 271, 272)
         for s, k in enumerate((3, 1, 2)):
@@ -353,37 +356,49 @@ def build(cfg):
             else:
                 ts(v("ne", 4, 128, 8), v("rw", 1, 32, 2), z_, ALU.subtract, v("ch", 32 * s + 15, n=1), ALU.not_equal)
         scan(v("cs"), v("ne"), v("nk"))
-        tt(v("cc"), v("cs", 135, 256, 8), v("cs", 7, 128, 8), ALU.is_ge)
-        tt(v("rho"), v("rs", 15, 256, 16), v("rs", 271, 512, 16), ALU.subtract)
-        tt(v("dl"), v("cc"), v("rho"), ALU.mult)
-        if cfg["ex"] == "V":
-            tt(v("hy", 0, 256, 16), v("ee", 0, 16), v("ee", 16, 32), ALU.subtract)
-            scan(v("ex"), v("hk"), v("hy"))
-        else:
-            tt(v("ev"), v("ee", 0, 16), v("ee", 16, 32), ALU.subtract)
-        for k in (0, 8):
-            if cfg["ex"] == "S":
-                act(v("ex", 16 * k, n=128), ind(v("ev"), v("lx", k, n=8)))
-            act(slot("dm", 2, 16 * k, 128), ind(v("cc"), v("lx", k, n=8)), scale=v("rho", 15, 16))
-            tt(v("tt", 16 * k, n=128), ind(v("dl"), v("ly", k, n=8)), v("ex", 16 * k, n=128), ALU.mult)
-        for k in (0, 8):
-            act(slot(d1, 3, 16 * k, 128), ind(v("tt"), v("lm", 28 + k, n=8)))
-            times(cfg["cp"][h], slot(d1, 2, 16 * k, 128), v("tt", 16 * k, n=128), 1.0)
-        for k in range(0, 256 * w, 64 * w):
-            scan(v(tn, k, n=64 * w), v("dm", k, n=64 * w), v(d1, k, n=64 * w))
+        rho, ba, cc, ev = v("hy", 0, 256, 16), v("hy", 240, 241), v("hx", 0, 256, 16), v("hz", 0, 256, 16)
+
+        def repeat(k, rows):
+            while rows < 15:
+                n = min(rows, 15 - rows)
+                lin("VGS" if last and k else "GVS", slot(d1, k, 16 * rows, 16 * n), slot(d1, k, 0, 16 * n))
+                rows += n
+
+        def spread(k, src):
+            scan(slot("dm", k, 1), v("hk"), v(src, 0, 240))
+            act(slot("dm", k, 1), ind(v(src), v("lx", 0, 15)))
+            either("VS")
+
+        tt(rho, v("rs", 15, 256, 16), v("rs", 271, 512, 16), ALU.subtract)
+        spread(1, "hy")
+        vec(lambda q: q.reciprocal, v("sm", 0, 1), [ba], [])
+        ops[-1]["cost"] = 190 + 6 * cyc
+        tt(ev, v("ee", 16, 32), v("ee", 0, 16), ALU.subtract)
+        lin("VS", slot(d1, 0, 0, 16), ev, v("sm", 0, 1))
+        repeat(0, 1)
+        lin("SV", v("hz", 1, 240, 16), v("hz", 2, 240, 16), 1.0, ba)
+        scan(slot("dm", 4), v("hq"), v("hz", 0, 240))
+        tt(cc, v("cs", 135, 256, 8), v("cs", 7, 128, 8), ALU.is_ge)
+        spread(3, "hx")
+        tt(v("dl"), cc, rho, ALU.mult)
+        lin("SV", slot(d1, 3, 0, 16 * cfg["dl"][h]), ind(v("dl"), v("ly", 0, n=cfg["dl"][h])), 2.0 ** -12)
+        repeat(3, cfg["dl"][h])
+        n = 240 * w // cfg["parts"]
+        for k in range(0, 240 * w, n):
+            scan(v(tn, k, n=n), v("dm", k + w, n=n), v(d1, k, n=n))
         if last:
-            for k in range(0, 256, 128):
-                times(cfg["otf"][k // 128], v("otf", k, n=128), slot(tn, w - 1, k, 128), 1.0)
-                dma("Y", "so%d" % (k // 128), lambda T, k=k: (T.ot[:, k:k + 128], T.otf[:, k:k + 128]), [v("otf", k, n=128)], [], 64)
+            for k, n in ((0, 120), (120, 136)):
+                lin("VS", v("otf", k, n=120), slot(tn, 4, k, 120), 1.0, -128.0)
+                dma("Y", "so%d" % (k // 120), lambda T, k=k, n=n: (T.ot[:, k:k + n], T.otf[:, k:k + n]), [v("otf", k, n=n)], [], 64)
         else:
-            times(cfg["tb"], tab, slot(tn, w - 1), 1.0)
+            lin("VSG", v("tb", 0, 240), slot(tn, 4))
         add("A", "a", h, [], pair(qz, sz, 128, 64), 0.0, after=[snd["id"]])
         for b in range(4):
             mm(v("pd", 512 * b, n=128), pair("wq", "wp", 128 * b, 128), pair(qz, sz, 64, 128))
             tt(v("wn", 384 * b, n=64), v("pd", 512 * b + 64, n=64), v("zs", b, s=4, n=64), ALU.add)
         for k, e in enumerate(cfg["xlast" if last else "xeng"]):
             b, (p, n) = k % 4, (((0, 8), (8, 8)) if last else ((0, P), (P, 15 - P)))[k // 4]
-            times(e, v("xt", 64 + b + 64 * p, s=4, n=16 * n), ind(v("wn", 384 * b, n=384), v("il", p + p % 2, n=n)), 0.03125)
+            lin(e + "SV".strip(e), v("xt", 64 + b + 64 * p, s=4, n=16 * n), ind(v("wn", 384 * b, n=384), v("il", p + p % 2, n=n)), 0.03125)
 
     for k in range(2):
         quant(*pair("qf", "sf", 128 * k, 128), v("xt", 64 + 512 * k, n=512))
@@ -391,11 +406,11 @@ def build(cfg):
         dma("Y", "sc%d" % k, lambda T, k=k: (T.oc[:, 512 * k:512 * k + 512], T.qf[:, 128 * k:128 * k + 128].bitcast(dt.uint8)),
             [v("qf", 128 * k, n=128)], [], 64)
     for k in range(4):
-        dma("SSYY"[k], "ss%d" % k, lambda T, k=k: (T.osc[4 * k:4 * k + 4, :], T.sf[32 * k:32 * k + 4, :]), [v("sf")], [], 1)
-    act(v("ys", 0, 128), v("py", 0, 128))
-    copy(v("ys", 128, 256), v("py", 512, 640))
+        dma("YS", "ss%d" % k, lambda T, k=k: (T.osc[4 * k:4 * k + 4, :], T.sf[32 * k:32 * k + 4, :]), [v("sf")], [], 1)
+    lin("SV", v("ys", 0, 128), v("py", 0, 128))
+    lin("VS", v("ys", 128, 256), v("py", 512, 640))
     for k in range(2):
-        dma("SY"[k], "sy%d" % k, lambda T, k=k: (T.y[:, 128 * k:128 * k + 128], T.ys[:, 128 * k:128 * k + 128]),
+        dma("SY", "sy%d" % k, lambda T, k=k: (T.y[:, 128 * k:128 * k + 128], T.ys[:, 128 * k:128 * k + 128]),
             [v("ys", 128 * k, n=128)], [], 64)
     return ops
 
@@ -415,7 +430,7 @@ def depend(ops):
             if k in writer:
                 d.add(writer[k])
             if k[0] in PSUM:
-                d.update(r for r in readers.get(k, ()) if ops[r]["eng"] != o["eng"])
+                d.update(r for r in readers.get(k, ()) if ops[r]["eng"] != o["eng"] or "alts" in o or "alts" in ops[r])
         for k in wk:
             if k in writer:
                 d.add(writer[k])
@@ -430,9 +445,7 @@ def depend(ops):
 
 
 def gap(cfg, a, b):
-    if b["kind"] in "at":
-        return a["lat"]
-    return a["lat"] + (cfg["ws"] if a["eng"] == b["eng"] and a["kind"] == "c" else cfg["wx"])
+    return a["lat"] + (0.0 if b["kind"] in "at" else cfg["wake"])
 
 
 def schedule(ops, cfg):
@@ -457,28 +470,22 @@ def schedule(ops, cfg):
 
 
 def span(order, tab):
-    end, free, top = [0.0] * len(tab), {}, 0.0
+    end, start, free, top = [0.0] * len(tab), [0.0] * len(tab), {}, 0.0
     for i in order:
         e, c, ds, lat = tab[i]
-        t = free.get(e, 0.0)
-        for d, gp in ds:
-            x = end[d] + gp
-            if x > t:
-                t = x
-        t += c
-        end[i] = t
-        free[e] = t
-        if t + lat > top:
-            top = t + lat
-    return top
+        start[i] = max([free.get(e, 0.0)] + [end[d] + gp for d, gp in ds])
+        end[i] = free[e] = start[i] + c
+        top = max(top, end[i] + lat)
+    return top, start
 
 
 def tables(ops, cfg):
-    tabs = []
+    tabs, alts = [], []
     for m in COSTS:
         c = dict(cfg)
         c.update(m)
         new = build(c)
+        alts.append([{e: x[1] for e, x in o.get("alts", {}).items()} for o in new])
         tabs.append([(o["eng"], new[o["id"]]["cost"], [(d, gap(c, new[d], new[o["id"]])) for d in o["dep"]],
                       new[o["id"]]["lat"] if o["kind"] == "d" else 0.0) for o in ops])
     reach, out = [0] * len(ops), [[] for t in tabs]
@@ -490,7 +497,7 @@ def tables(ops, cfg):
             reach[i] |= 1 << d
         for t, x in zip(tabs, out):
             x.append((t[i][0], t[i][1], [t[i][2][k] for k in keep], t[i][3]))
-    return out
+    return out, alts
 
 
 QUEUES = "VSPGYAD"
@@ -569,20 +576,39 @@ def trace(w, loc):
     return state, pairs, spans
 
 
+def tails(w, loc):
+    out = []
+    for row, free0, rest, past in loc:
+        back, full, own = list(rest), [0.0] * len(row), [r[4] for r in row]
+        for i in reversed(w):
+            e, c, ds, t, q = row[i]
+            x = own[i]
+            if back[e] > x:
+                x = back[e]
+            x = full[i] = back[e] = x + c
+            for d, gp in ds:
+                if x + gp > own[d]:
+                    own[d] = x + gp
+        out.append((full, own))
+    return out
+
+
 def improve(ops, order, cfg):
-    tabs, n, width, passes = tables(ops, cfg), len(ops), cfg["width"], cfg["passes"]
+    (tabs, alts), n, width, passes = tables(ops, cfg), len(ops), cfg["width"], cfg["passes"]
     succ = [[[] for i in range(n)] for t in tabs]
     for t, s in zip(tabs, succ):
         for i in range(n):
             for d, gp in t[i][2]:
                 s[d].append((i, gp))
     head = len([o for o in ops if o["kind"] == "d" and not o["r"]])
-    base = [span(order, t) for t in tabs]
+    base = [span(order, t)[0] for t in tabs]
     rng = np.random.default_rng(cfg["seed"])
     order = list(order)
-    best, keep = 1e9, list(order)
+    best, keep = 1e9, None
     for ps in range(passes):
         hot = cfg["heat"] * (1 - ps / passes) ** 2
+        start = span(order, tabs[1])[1]
+        order[head:] = sorted(order[head:], key=lambda i: start[i])
         for lo in range(head - int(rng.integers(width // 2)), n - width // 4, width // 2):
             a, b = max(lo, head), min(n, lo + width)
             ids = order[a:b]
@@ -597,17 +623,66 @@ def improve(ops, order, cfg):
                 for d in ds:
                     near[1][d].append(i)
             win, pairs, low = list(range(m)), None, 1e9
+            flex = [k for k, i in enumerate(ids) if len(alts[0][i]) > 1]
+
+            def move(i, e):
+                eng[i] = e
+                for x, al in zip(loc, alts):
+                    x[0][i] = (e, al[ids[i]][QUEUES[e]]) + x[0][i][2:]
+
             for r0, r1, r2, r3 in rng.random((cfg["moves"], 4)).tolist() + [[2.0] * 4]:
                 if pairs is None:
                     state, pairs, spans = trace(win, loc)
                     parts = [x / y for x, y in zip(spans, base)]
-                    cur, pos = sum(parts), [0] * m
+                    cur, pos, tl = sum(parts), [0] * m, None
                     if cur < low:
-                        low, good = cur, win
+                        low, good = cur, (win, list(eng))
                     for k, x in enumerate(win):
                         pos[x] = k
                 if r0 > 1.0:
                     break
+                limit = [cur + hot * r3 - sum(parts[k + 1:]) + 0.004 * len(parts[k + 1:]) for k in range(len(parts))]
+                if r0 < cfg["put"]:
+                    tl = tl or tails(win, loc)
+                    i = pairs[int(r1 * len(pairs))][int(r2 * 2)] if pairs and r0 < cfg["put"] / 2 else win[int(r1 * m)]
+                    first = max([pos[d] for d in near[-1][i]] + [-1])
+                    final = min([pos[d] for d in near[1][i]] + [m])
+                    ready = [max([x[0][i][3]] + [st[0][d] + gp for d, gp in x[0][i][2]]) for x, st in zip(loc, state)]
+                    pick = None
+                    for name in alts[0][ids[i]] or [QUEUES[eng[i]]]:
+                        e = QUEUES.index(name)
+                        line = [None] + [x for x in win if eng[x] == e and x != i] + [None]
+                        cost = [al[ids[i]].get(name, x[0][i][1]) for x, al in zip(loc, alts)]
+                        for p, x in zip(line, line[1:]):
+                            lo2, hi2 = (pos[p] if p is not None else -1), (pos[x] if x is not None else m)
+                            if lo2 >= final or hi2 <= first or (e == eng[i] and lo2 < pos[i] < hi2):
+                                continue
+                            val = hot * 0.3 * ((lo2 * 0.618 + r3 * 7) % 1.0)
+                            for k in range(len(loc)):
+                                t = max(ready[k], state[k][0][p] if p is not None else loc[k][1][e]) + cost[k]
+                                val += (t + max(tl[k][1][i], tl[k][0][x] if x is not None else loc[k][2][e])) / base[k]
+                            if pick is None or val < pick[0]:
+                                pick = (val, e, max(lo2, first))
+                    if pick:
+                        old, k, p = eng[i], pick[2], pos[i]
+                        new = win[:k + 1] + [i] + win[k + 1:p] + win[p + 1:] if k < p else win[:p] + win[p + 1:k + 1] + [i] + win[k + 1:]
+                        if pick[1] != old:
+                            move(i, pick[1])
+                        if fits(new, min(k + 1, p), loc, base, state, limit):
+                            win, pairs = new, None
+                        elif pick[1] != old:
+                            move(i, old)
+                    continue
+                r0 = (r0 - cfg["put"]) / (1.0 - cfg["put"])
+                if flex and r0 > 1.0 - cfg["flip"]:
+                    i = flex[int(r1 * len(flex))]
+                    other, old = [QUEUES.index(e) for e in alts[0][ids[i]] if QUEUES.index(e) != eng[i]], eng[i]
+                    move(i, other[int(r2 * len(other))])
+                    if fits(win, pos[i], loc, base, state, limit):
+                        pairs = None
+                    else:
+                        move(i, old)
+                    continue
                 if pairs and r0 < 0.6:
                     u, w = pairs[int(r1 * len(pairs))]
                     i, way = (w, -1) if r0 < 0.3 else (u, 1)
@@ -630,14 +705,22 @@ def improve(ops, order, cfg):
                 one, two = [x for x in win[s:e] if x in grp], [x for x in win[s:e] if x not in grp]
                 if two:
                     new = win[:s] + (one + two if way < 0 else two + one) + win[e:]
-                    limit = [cur + hot * r3 - sum(parts[k + 1:]) + 0.004 * len(parts[k + 1:]) for k in range(len(parts))]
                     if fits(new, s, loc, base, state, limit):
                         win, pairs = new, None
-            order[a:b] = [ids[k] for k in (win if ps < passes - 1 and cur < low + hot else good)]
-        x = sum(span(order, t) / bs for t, bs in zip(tabs, base))
+            if ps == passes - 1 or cur >= low + hot:
+                win, eng = good
+            order[a:b] = [ids[k] for k in win]
+            for k in flex:
+                for t, al in zip(tabs, alts):
+                    t[ids[k]] = (QUEUES[eng[k]], al[ids[k]][QUEUES[eng[k]]]) + t[ids[k]][2:]
+        spans = [span(order, t)[0] for t in tabs]
+        x = sum(s / bs for s, bs in zip(spans, base))
         if x < best:
-            best, keep = x, list(order)
-    return keep, [round(span(keep, t)) for t in tabs]
+            best, keep = x, (list(order), [r[0] for r in tabs[0]], [round(s) for s in spans])
+    for o, e in zip(ops, keep[1]):
+        if "alts" in o:
+            o["eng"], (o["emit"], o["cost"]) = e, o["alts"][e]
+    return keep[0], keep[2]
 
 
 def waits(ops, order, arrive):
@@ -694,7 +777,7 @@ def rank_program(g, core, T, topo):
     queue = {"V": g.vector, "S": g.scalar, "P": g.tensor, "G": g, "Y": g.sync}
 
     def pass_on(h):
-        qa, sa, qz, sz = [T["%s%d" % (k, h)] for k in (("qa", "sa") if CFG["z"] < 8 else ("qz", "sz")) + ("qz", "sz")]
+        qa, sa, qz, sz = [T["%s%d" % (k, h)] for k in ("qa", "sa", "qz", "sz")]
         arr, (ma, mb) = T.sem["arr%d" % h], [sum(1 << e for e in s) for s in sets[h]]
         g.remote_dma(qz[:, 128:192].bitcast(dt.uint8), qa[:, 0:64].bitcast(dt.uint8), arr, T.sem.sent, pid, rid, ma)
         g.remote_dma(sz[:, 128:192], sa[:, 0:64], arr, T.sem.sent, pid, rid, mb)

@@ -1,29 +1,35 @@
 import numpy as np
-from concourse.mybir import dt, AluOpType as ALU, ActivationFunctionType as ACT
+from concourse.mybir import dt, AluOpType as ALU, ActivationFunctionType as ACT, AxisListType as AX
 
 ROUNDS = 3
-P = 9
-CFG = {"xeng": "SSVVSSSV", "xlast": "SSVVSSVV", "fill": "nk hk hq hx hy hz kr", "dl": (4, 4, 4), "parts": 4, "fast": (2,), "dq": 80.0,
-       "passes": 110, "moves": 400, "width": 44, "heat": 0.016, "seed": 1, "flip": 0.06, "put": 0.6,
+MARKS = [8, 16, 24, 41, 65, 75, 89, 111, 133, 137, 165, 177, 197, 215, 217, 512]
+RUNS = [(0, 1, 3), (3, 3, 3), (8, 2, 3), (4, 1, 2), (7, 4, 2), (13, 1, 2), (15, 1, 1)]
+P = 10
+CFG = {"xeng": "SSVVSSSV", "xlast": "SSVVSSVV", "fill": "nk kr", "runs": ((1, 1, 1), (1, 1, 1), (1, 8, 1)), "parts": 2,
+       "fast": (), "join": (), "rw": 0, "ramp": 1, "oo": False, "aa": (1, 1, 1), "wnf": "SSVV", "dq": 80.0,
+       "passes": 62, "moves": 400, "width": 44, "heat": 0.03, "cool": 0.08, "seed": 1, "flip": 0.1, "put": 0.6,
        "wake": 225.0, "lat": 1900.0, "f": 1.1, "gc": 1.5, "sfix": 60.0, "pe": 0.8, "issue": 150.0, "once": 300.0, "dma": 1500.0, "kb": 4.0}
-COSTS = [{"wake": 230.0, "lat": 1500.0, "issue": 300.0, "once": 800.0, "f": 1.05, "gc": 1.35, "pe": 0.6, "dma": 1200.0, "kb": 3.0},
-         {"wake": 200.0, "lat": 2200.0, "issue": 500.0, "f": 1.2, "gc": 1.8, "sfix": 80.0, "pe": 0.8, "dma": 1600.0, "kb": 4.0},
-         {"wake": 240.0, "lat": 1700.0, "issue": 200.0, "f": 1.45, "gc": 1.6, "pe": 0.7, "dma": 1300.0, "kb": 3.5}]
+RANGES = {"wake": (140, 290), "f": (1.0, 1.5), "gc": (1.04, 2.08), "pe": (0.45, 0.9), "lat": (700, 1800), "issue": (100, 350),
+          "once": (300, 1200), "dma": (800, 1500), "sfix": (30, 90), "kb": (2.5, 4.0)}
+SETS = 7
+COSTS = [dict({k: a + (b - a) * ((i * (1 + j % (SETS - 1)) + 3 * j) % SETS + 0.5) / SETS for j, (k, (a, b)) in enumerate(RANGES.items())},
+              weight=1.0) for i in range(SETS)]
 
 BF, F32, I32, U16, MXC, U8 = "bfloat16", "float32", "int32", "uint16", "float8_e4m3fn_x4", "uint8"
 SB = {}
 for _d, _names in (
-        (BF, "xn1024 ut512 vt512 et516 xt1216 gg256 sc256 fh1024 wn1536 ee144 oo10 gt128 ms128 ab512 zt512 zs512 tb256 "
-             "dm1205 da1280 db1280 rs528 sb8 ch96 ne256 nk256 cs256 dl16 kf240 "
-             "kd64 kr256 jc144 ka16 kb16 kc16 ua32 ub32 uc32 rw64 df32 fl9 hk240 hq240 hx256 hy256 hz256"),
-        (F32, "ts576 aa256 st144 kh144 kg16 den15 rec14 wv32 wt32 wu16 sm2 otf256 ys256 nm17 col16 pc25 pb1 ia30"),
-        (I32, "ti256 ic16 ie16 iw32 ih32"),
-        (U16, "oi8 oj8 ok8 il16 lm30 lab32 lx16 ly16 lt2 lk4"),
+        (BF, "xn1024 ut512 vt512 et516 xt1280 gg384 sc360 fh1024 wn1536 ee80 oo6 gt64 ms64 ab512 zt768 zs512 tb256 "
+             "dm720 da728 db728 na512 rs528 sb8 ch96 ne256 nk256 cs256 dl16 kf384 nm128 "
+             "ph16 pq16 cq128 cp128 dd128 nq512 mt512 rd6 kv128 st80 kh5 "
+             "kd64 kr256 jc80 ka16 ua32 ub32 uc32 rw64 df32 fl5 hx16 hy16 hz16"),
+        (F32, "ts576 aa256 sq5 wv32 wt32 wu16 otf256 ys256 col16 pc25"),
+        (I32, "ti256 ic32 ie32 iw32 ih32 ya66 yb98"),
+        (U16, "oi4 oj8 ok8 il18 lm18 le6 lp8 lf16 lab32 ly16 lt4"),
         (MXC, "wq512 qn256 qu128 qv128 qe512 qf256"), (U8, "wp512 sn256 su128 sv128 se512 sf256")):
     for _n in _names.split():
         SB[_n.rstrip("0123456789")] = (int(_n.lstrip("abcdefghijklmnopqrstuvwxyz")), _d)
 for _h in range(ROUNDS):
-    for _n, _w, _d in (("qx", 304, MXC), ("sx", 304, U8), ("qa", 128, MXC), ("sa", 128, U8), ("qz", 192, MXC), ("sz", 192, U8)):
+    for _n, _w, _d in (("qx", 320, MXC), ("sx", 320, U8), ("qa", 128, MXC), ("sa", 128, U8), ("qz", 192, MXC), ("sz", 192, U8)):
         SB["%s%d" % (_n, _h)] = (_w, _d)
 PSUM = {"ps": 512, "pt": 512, "pd": 2048, "py": 1024}
 SCRATCH = {k: ("sbuf", [128, n], d) for k, (n, d) in SB.items()}
@@ -97,6 +103,9 @@ def build(cfg):
     def scan(out, a, b, op0=ALU.mult, op1=ALU.add, first=0.0):
         vec(lambda q: q.tensor_tensor_scan, out, [a, b], [first, op0, op1])
 
+    def nearest(out, a):
+        vec(lambda q: lambda o, x: q.tensor_reduce(o, x, AX.X, ALU.min, apply_absolute_value=True), out, [a], [])
+
     def transpose(out, a):
         vec(lambda q: q.transpose, out, [a], [])
 
@@ -123,7 +132,7 @@ def build(cfg):
         for e in engs:
             if e == "G":
                 add("G", "c", lambda g, T: g.affine_select(ap(T, out), ap(T, a), [[0, count(a)]], ALU.is_ge, 0.0, 0, 0),
-                    [a], [out], 170 + 2 * count(out) * cyc)
+                    [a], [out], (205 + 2 * count(out)) * cyc)
             elif e == "S":
                 act(out, a, **({"scale": scale} if bias is None else {"scale": scale, "bias": bias}))
             elif bias is not None:
@@ -143,11 +152,11 @@ def build(cfg):
 
     def iota(out, pattern, base, cm):
         kw = {} if SB[out[1]][1] == I32 else {"allow_small_or_imprecise_dtypes": True}
-        add("G", "c", lambda g, T: g.iota(ap(T, out), pattern, base, cm, **kw), [], [out], 130 + 2 * count(out) * cyc)
+        add("G", "c", lambda g, T: g.iota(ap(T, out), pattern, base, cm, **kw), [], [out], (157 + 2 * count(out)) * cyc)
 
     def select(out, pattern, val, base, cm, op=ALU.not_equal):
         add("G", "c", lambda g, T: g.affine_select(ap(T, out), ap(T, out), pattern, op, val, base, cm),
-            [out], [out], 170 + 2 * count(out) * cyc)
+            [out], [out], (205 + 2 * count(out)) * cyc)
 
     def fill(out, c):
         engs = "VG" if count(out) > 64 and out[1] not in cfg["fill"] else "GV"
@@ -176,83 +185,98 @@ def build(cfg):
     dma("Y", "l4", lambda T: (T.wp[:], T.ws[:]), [v("ut")], [v("wp")], 448)
     dma("Y", "l5", lambda T: (T.vt[:], T.v[:]), [v("ut")], [v("vt")], 576)
 
-    memset(v("et"), 0.0)
-    select(v("et", 3, s=4, n=128), [[-1, 128]], 0.5, 0, 1)
+    iota(v("pc"), [[256, 25]], 0, 1)
+    num = lambda a=0, b=16, s=1: v("nm", a, b, s)
+    pc, fl, col = [[v(n, k, n=1) for k in range(SB[n][0])] for n in ("pc", "fl", "col")]
+    for a in (0, 258):
+        fill(v("et", a, n=258), 0)
+    if cfg["ramp"]:
+        memset(v("kf", 0, 384, 3), 1.0)
+        scan(v("nm"), v("kf", 0, 384, 3), v("kf", 0, 384, 3), first=-1.0)
+        ts(v("et", 3, s=4, n=128), v("nm"), pc[0], ALU.is_equal, 0.5, ALU.mult)
+    else:
+        fill(v("kf", 0, 192, 3), 1)
+        iota(v("nm", 0, 16), [[1, 16]], 0, 0)
+        select(v("et", 3, s=4, n=128), [[-1, 128]], 0.5, 0, 1)
     for b in range(4):
         quant(*pair("qe", "se", 128 * b, 128), v("et", 3 - b, n=512))
-    iota(v("pc"), [[256, 25]], 0, 1)
-    iota(v("pb"), [[0, 1]], 197184, 256)
-    iota(v("nm"), [[1, 17]], -1, 0)
-    num = lambda a=0, b=16, s=1: v("nm", a + 1, b + 1, s)
-    pc, fl, col = [[v(n, k, n=1) for k in range(SB[n][0])] for n in ("pc", "fl", "col")]
-    lin("SV", v("fl"), num(0, 9), pc[0], 6128.4)
+    lin("SV", v("fl"), num(0, 5), pc[0], 6128.4)
     rep, low, odd, high = col[12:16]
+
+    def ramp(out, step, base):
+        lin("SV", out, num(0, count(out)), float(step), float(base))
+        iota(out, [[step, count(out)]], base, 0)
+        either("SG")
+
     lin("SV", rep, fl[2], -0.5, pc[12])
     lin("SV", col[2], fl[2], -0.5, pc[4])
     lin("SV", low, fl[4], -0.25, pc[6])
     lin("SV", odd, fl[1], -2.0, fl[2])
     lin("SV", high, fl[2], -2.0, fl[4])
-    lin("SV", col[10], fl[8], -31.96875, v("pb"))
-    lin("SV", col[9], fl[2], -0.125, col[10])
-    lin("SV", col[1], rep, 16.0)
     ts(v("lt", 0, 1), fl[1], -1.0, ALU.mult, pc[24], ALU.add)
-    ts(v("ly"), num(), 0.0, ALU.mult, rep, ALU.add)
-    ts(v("lx"), num(), 16.0, ALU.mult)
-    iota(v("ia"), [[0, 30]], 15, 0)
-    iota(v("ia", 11, 27), [[1, 16]], 0, 0)
-    iota(v("ia", 28, 29), [[0, 1]], 271, 0)
-    ts(v("lm"), v("ia"), col[1], ALU.add)
-    ts(v("sb", 2, 3), rep, 15.0, ALU.is_lt, 16.0, ALU.mult)
-    lin("SV", col[3], v("sb", 2, 3), 16.0, col[2])
-    iota(v("ic"), [[0, 2], [66, 8]], 66, 0)
-    lin("SV", col[11], odd, -1.03125, -6039.0)
-    lin("SV", col[7], odd, -1.03125, -5808.0)
+    for out, step, base, cm in ((v("ya", 0, 18), 1, 255, 16), (v("ya", 18, 26), 0, 0, 16),
+                                (v("ya", 26, 34), 16, 16, 16), (v("ya", 34, 50), 241, 0, 16), (v("ya", 50, 66), 16, 4096, -16)):
+        iota(out, [[step, count(out)]], base, cm)
+    for a, b in ((0, 34), (34, 66)):
+        ts(v("yb", a, b), v("ya", a, b), 255, ALU.bitwise_and)
+    copy(v("lm"), v("yb", 0, 18))
+    ts(v("ly"), v("yb", 18, 34), 0.0625, ALU.mult)
+    lin("SV", col[3], rep, -255.0, 1792.0)
+    if not cfg["rw"]:
+        lin("SV", col[1], rep, 16.0, 271.0)
+        ts(v("lt", 2, 4), num(0, 2), -256.0, ALU.mult, col[1], ALU.add)
+    for a in (0, 1):
+        iota(v("ic", 16 * a, n=16), [[231, 2], [-264, 2], [66, 4]], 99 - 33 * a, 0)
+    lin("SV", col[11], odd, -1.03125, -6270.0)
     ts(col[0], high, odd, ALU.subtract, 1.03125, ALU.mult)
     lin("SV", col[4], low, 33.0, col[11])
-    lin("SV", col[5], low, -33.0, col[11])
-    lin("SV", col[6], low, 512.0)
+    ts(col[6], low, 7.0, ALU.not_equal)
     lin("SV", col[8], odd, 1.0, 6144.0)
-    ts(v("ie"), v("ic"), col[0], ALU.add, col[7], ALU.min)
-    for a, op in ((0, ALU.min), (16, ALU.max)):
-        ts(v("iw", a, n=8), v("ie", 0, 8), col[5], op)
-        ts(v("iw", a + 8, n=8), v("ie", 8, 16), col[4], op, col[6], ALU.min)
+    ts(v("ie"), v("ic"), col[0], ALU.add)
+    for a, op, far in ((0, ALU.min, 7), (8, ALU.min, 0), (16, ALU.max, 8), (24, ALU.max, 1)):
+        ts(v("iw", a, n=8), v("ie", a, n=8), col[4], op, 33.0 * far, ALU.add)
     ts(v("ih"), v("iw"), 0x3C1, ALU.bitwise_and)
-    ts(v("lab"), v("ih"), col[8], ALU.add)
-    memset(v("kf"), 1.0)
-    select(v("kf"), [[-1, 15], [-1, 8], [-1, 2]], -1.0, 8, 0, ALU.is_gt)
-    select(v("kf"), [[-1, 15], [1, 8], [0, 2]], 1.0, 7, 0, ALU.is_gt)
-    for a, b, x, step, base in ((1, 112, 0, 1, -13), (113, 240, 7, -1, 13), (0, 240, 0, 0, 0)):
-        out = v("kf", a, b, 16)
-        lin("SV", out, num(x, x + count(out)), float(step), float(base))
-        iota(out, [[step, count(out)]], base + step * x, 0)
-        either("SG")
-    ts(v("lk"), num(0, 16, 4), col[9], ALU.add)
-    iota(v("jc"), [[1, 9], [0, 16]], 0, 0)
-    iota(v("den"), [[16, 15]], -7, 0)
-    vec(lambda q: q.reciprocal, v("rec"), [v("den", 1, 15)], [])
-    ops[-1]["cost"] = 190 + 84 * cyc
-    tt(v("kg", 1, 15), v("den", 0, 14), v("rec"), ALU.mult)
-    lin("SV", v("kg", 0, 1), num(0, 1), 0.0, -1 / 7)
-    lin("SV", v("kg", 15, 16), num(0, 1), 0.0, 13.5625)
-    lin("SV", v("kh"), ind(v("kg"), v("ly", 0, 9)))
-    ts(v("ka"), num(), rep, ALU.is_equal, 256.0, ALU.mult)
-    ts(v("kb"), v("nm", 0, 16), rep, ALU.is_equal, -16.0, ALU.mult)
-    tt(v("kc"), v("ka"), v("kb"), ALU.add)
-    lin("SV", v("kd"), ind(v("kc"), v("ly", 0, 4)))
+    ts(v("lab"), v("ih"), col[6], ALU.mult, col[8], ALU.add)
+    iota(v("kv"), [[-2, 2], [-2, 8], [2, 8]], 1, 0)
+    ts(v("kf", 2, 360, 3), v("kv", 0, 120), -1.0, ALU.max, 1.0, ALU.min)
+    fill(v("kf", 192, 360, 3), -1)
+    fill(v("kf", 213, 360, 24), 1)
+    lin("GSV", v("kf", 1, 192, 3), v("kf", 2, 192, 3))
+    lin("SV", v("kf", 193, 360, 3), v("kf", 194, 360, 3), -1.0)
+    fill(v("kf", 214, 360, 24), 1)
+    fill(v("kf", 0, 360, 24), 0)
+    fill(v("gg", 2, 384, 3), 1)
+    ramp(v("gg", 2, 384, 24), 1, -18)
+    for a, step, n in RUNS:
+        ramp(v("ph", a, s=step, n=n), MARKS[a + step] - MARKS[a] if n > 1 else 0, MARKS[a])
+    lin("SV", v("pq"), v("ph"), 2.0 ** -9)
+    lin("SV", v("gg", 5, 384, 24), v("ph"), 2.0 ** -9)
+    lq = v("ly", 8, 16)
+    ts(v("lp"), v("yb", 26, 34), rep, ALU.add)
+    lin("SV", v("cq"), ind(v("pq"), v("ly", 0, 8)))
+    tt(v("cp"), ind(v("pq"), lq), v("cq"), ALU.add)
+    ts(v("yb", 66, 82), v("yb", 50, 66), rep, ALU.add)
+    tt(v("yb", 82, 98), v("yb", 34, 50), v("yb", 66, 82), ALU.min)
+    ts(v("lf"), v("yb", 82, 98), 5.0, ALU.mult, 4.0, ALU.add)
+    ts(v("le", 0, 5), v("yb", 18, 23), 0.125, ALU.mult)
+    iota(v("jc"), [[1, 5], [0, 16]], 132, 0)
+    lin("SV", v("kh"), num(0, 5), 0.0, 0.0625)
+    ts(v("ka"), num(), rep, ALU.is_equal)
+    lin("SV", v("kd"), ind(v("ka"), v("ly", 0, 4)), 1040.0, -16.0)
     iota(v("rw", 1, 64, 2), [[0, 2], [1, 16]], 128, 0)
-    iota(v("ub", 1, 30, 2), [[1, 15]], 9, 0)
+    ramp(v("ub", 1, 32, 2), 1, 136)
     w = 5
-    for out, c in ((v("sc", 240, 256), 100), (v("ts", 0, 64, 2), 0), (v("ts", 513, 576, 2), 0), (v("kr"), -1), (v("kr", 15, 256, 16), 143), (v("zt", 256, 512), 0), (v("xt", 1024, 1216), 0),
+    slot = lambda buf, k, a=16, n=128: v(buf, w * a + k, s=w, n=n)
+    for out, c in ((v("ub", 30, 31), 228), (v("ua"), 256), (v("ts", 0, 64, 2), 0), (v("ts", 513, 576, 2), 0), (v("kr"), -1),
+                   (v("kr", 15, 256, 16), 143), (v("zt", 256, 512), 0), (v("xt", 0, 64), 0), (v("xt", 1088, 64 * P + 576), 0),
                    (v("ne", 0, 256, 8), 0), (v("ne", 132, 256, 8), 1), (v("ne", 135, 256, 8), -1), (v("nk"), 0), (v("nk", 0, 256, 8), 1),
-                   (v("nk", 135, 256, 8), 1), (v("rs", 512, 528), 0), (v("ua", 0, 32, 2), 128), (v("ub", 31, 32), 8),
-                   (v("dm", w, 241 * w, w), 0), (v("dm", w + 2, 241 * w, w), -1), (v("dm", 1204, 1205), 0), (v("hk"), 1), (v("hk", 0, 240, 16), 0),
-                   (v("hq"), 1), (v("hq", 0, 240, 16), 0), (v("hq", 1, 240, 16), -4096), (v("hx"), 0), (v("hy"), 0), (v("hz"), 0)):
+                   (v("nk", 135, 256, 8), 1), (v("rs", 512, 528), 0),
+                   (slot("dm", 0), 0), (slot("dm", 2), -1), (v("da", 0, 80), 143), (v("db", 0, 80), 143), (v("da", 720), 0), (v("db", 720), 0)):
         fill(out, c)
 
     quant(v("qu"), v("su"), v("ut"))
     for a in (0, 128):
         lin("VS", v("tb", a, n=128), v("ti", a, n=128), 1.0, 128.0)
-    lin("SV", v("otf", 240, 256), v("ti", 240, 256))
     quant(v("qv"), v("sv"), v("vt"))
     uq = pair("qu", "su", 0, 128)
 
@@ -263,83 +287,89 @@ def build(cfg):
         if h == 0:
             for k in range(2):
                 quant(*pair("qn", "sn", 128 * k, 128), v("xn", 512 * k, n=512))
-            for a, b in ((0, P + 1), (P + 1, 17)):
-                copy(words(v(qx, 16 * a, 16 * b)), ind(words(v("qn")), v("lm", 10 + a, 10 + b)))
-                act(v(sx, 16 * a, 16 * b), ind(v("sn"), v("lm", 10 + a, 10 + b)), func=ACT.Copy)
+            for a, b in ((0, P + 2 - P % 2), (P + 2 - P % 2, P + 8)):
+                copy(words(v(qx, 16 * a, 16 * b)), ind(words(v("qn")), v("lm", a, b)))
+                act(v(sx, 16 * a, 16 * b), ind(v("sn"), v("lm", a, b)), func=ACT.Copy)
         else:
             quant(*pair(qx, sx, 0, 16 * P + 16), v("xt", 0, 64 * P + 64))
             quant(*pair(qx, sx, 16 * P + 16, 128), v("xt", 64 * P + 64, n=512))
         tab = v("tb")
         mm(v("ps", 0, 16 * P + 16), uq, pair(qx, sx, 0, 16 * P + 16))
         mm(v("pt", 0, 128), uq, pair(qx, sx, 16 * P, 128))
-        for a, bank, e, n in ((1, "ps", 0, 160), (64, "ps", 16, 128), (320, "pt", 0, 128), (321, "pt", 16, 96)):
-            transpose(v("ts", a, s=2, n=n), v(bank, e, n=n))
-        whole = [v("fh", 256 * b, n=256) for b in range(4)]
-        plane = [v("fh", 256 * b + 16, n=240) for b in range(4)]
+        for a, e, n in ((1, 0, (P + 1) // 2), (64, 16, P // 2)):
+            transpose(v("ts", a, s=2, n=32 * n), v("ps", e, n=32 * n))
+            transpose(v("ts", a + 64 * n, s=2, n=256 - 32 * n), v("pt", e + 32 * n - 16 * P, n=256 - 32 * n))
+        plane = [v("fh", 256 * b, n=256) for b in range(4)]
         for b in range(4):
-            mm(v("pd", 512 * b, n=256), pair("qe", "se", 128 * b, 128), pair(qx, sx, 0, 256))
-            lin("SV", whole[b], v("pd", 512 * b, n=256))
-        if not last:
-            lin("SV", v("xt", 0, 64), ind(v("fh"), v("lk")), 2.0)
-        pieces = ((1, 0, 320), (129, 4, 576), (0, 8, 576), (128, 12, 576))
-        for e, a, width in pieces:
-            lin("SV", v("aa", e, s=2, n=64), ind(v("ts", 0, 576 if a == 12 else 320), v("lab", a, n=4)))
-        for e, a, width in pieces:
-            tt(v("gg", e, s=2, n=64), ind(v("ts", 0, width), v("lab", 16 + a, n=4)), v("aa", e, s=2, n=64), ALU.is_le)
-        for a, b in ((0, 128), (128, 240)):
+            mm(v("pd", 512 * b, n=256), pair("qe", "se", 128 * b, 128), pair(qx, sx, 16, 256))
+            lin("SV", plane[b], v("pd", 512 * b, n=256))
+        if h == 0:
+            lin("SV", slot(d1, 4), ind(tab, v("lp")))
+        scan(v("dd"), slot(d1, 4), slot(d1, 4, 17), ALU.max, ALU.subtract)
+        pieces = ((1, 12, 4, 320, 320), (0, 4, 8, 320, 576), (193, 0, 4, 576, 576))
+        for e, a, n, lower, higher in pieces if cfg["aa"][h] else ((0, 4, 12, 320, 0), pieces[2]):
+            lin("SV", v("aa", 16 * a, n=16 * n), ind(v("ts", 0, lower), v("lab", a, n=n)))
+        for e, a, n, lower, higher in pieces:
+            tt(v("gg", e, s=3, n=16 * n), ind(v("ts", 0, higher), v("lab", 16 + a, n=n)), v("aa", 16 * a, n=16 * n), ALU.is_le)
+        for a, b in ((0, 192), (192, 360)):
             scan(v("sc", a, b), v("kf", a, b), v("gg", a, b))
-        for a, b in ((0, 5), (5, 9)):
-            tt(v("ee", 16 * a, 16 * b), ind(v("sc"), v("lm", 0, n=b - a)), v("jc", 16 * a, 16 * b), ALU.is_equal)
-            scan(v("st", 16 * a, 16 * b), v("kh", 16 * a, 16 * b), v("ee", 16 * a, 16 * b),
-                 first=v("st", 16 * a - 1, n=1) if a else 0.0)
-            j = max(a - 1, 0)
-            ts(v("oi", j, b - 1), v("st", 16 * j + 31, 16 * b, 16), 16.0, ALU.mult, 7.0225, ALU.add)
-            ts(v("oo", a, b), v("st", 16 * a + 15, 16 * b, 16), 12582912.0, ALU.add, 12582784.0, ALU.subtract)
-            ts(v("oj", j, b - 1), v("oo", j + 1, b), 16.0, ALU.mult, col[2], ALU.add)
-        for j in (0, 4):
-            lin("SV", v("gt", 16 * j, n=64), ind(tab, v("oi", j, n=4)))
-            scan(v("ms", 16 * j, n=64), v("kd", 0, 64), v("gt", 16 * j, n=64), ALU.add, ALU.min)
-            ts(v("ok", j, n=4), v("ms", 16 * j + 15, s=16, n=4), 16.0, ALU.mult, col[3], ALU.add)
-        for j in (0, 4):
+        mark = [v("rd", j, n=1) for j in range(5)]
+        for j in range(5):
+            nearest(mark[j], v("sc", 19 + j, 360, 24))
+        for a, b in ((0, 1), (1, 5)) if cfg["oo"] else ((0, 5),):
+            lin("VS" if a or b > 1 else "SV", v("oo", a, b), v("rd", a, b), 32.0, 128.0)
+        for j in range(4):
+            ts(v("nq", 128 * j, n=128), v("cp"), mark[j], ALU.subtract, mark[j + 1], ALU.not_equal)
+            scan(v("mt", 128 * j, n=128), v("nq", 128 * j, n=128), v("dd"))
+        ts(v("ok", 0, 4), v("mt", 127, 512, 128), 16.0, ALU.mult, col[2], ALU.add)
+        lin("SV", v("ub", 0, 30, 2), v("sc", 20, 360, 24), -1.0, 129.25)
+        tt(v("ee"), ind(v("ub"), v("le", 0, 5)), v("jc"), ALU.not_equal)
+        scan(v("st"), v("ee"), v("kr", 0, 80))
+        scan(v("sq"), v("kh"), v("st", 15, 80, 16), first=2048 / 15)
+        ts(v("oi"), v("sq", 1, 5), 16.0, ALU.mult, -2185.0, ALU.add)
+        lin("SV", v("gt"), ind(tab, v("oi")))
+        scan(v("ms"), v("kd"), v("gt"), ALU.add, ALU.min)
+        ts(v("ok", 4, n=4), v("ms", 15, s=16, n=4), 16.0, ALU.mult, col[3], ALU.add)
+        for j, pts in ((0, v("oo", 1, 5)), (4, v("st", 31, 80, 16))):
+            ts(v("oj", j, n=4), pts, 16.0, ALU.mult, col[2], ALU.add)
             for b in range(4):
                 lin("SV", v("ab", 128 * b + 16 * j, n=64), ind(plane[b], v("oj", j, n=4)))
         for j in (0, 4):
             for b in range(4):
-                tt(v("zt", 64 * j + b, s=4, n=64), ind(plane[b], v("ok", j, n=4)), v("ab", 128 * b + 16 * j, n=64), ALU.add)
-            quant(*(pair(qz, sz, 0, 128) if j else pair(qa, sa, 0, 128)), v("zt"))
+                tt(v("zt", 128 * j + b, s=4, n=64), ind(plane[b], v("ok", j, n=4)), v("ab", 128 * b + 16 * j, n=64), ALU.add)
+            quant(*(pair(qz, sz, 0, 128) if j else pair(qa, sa, 0, 128)), v("zt", 64 * j, n=512))
             if j == 0:
                 snd = add("G", "r", h, pair(qa, sa, 0, 64), [], cfg["issue"] + (0 if h else cfg["once"]), lat=cfg["lat"])
         for j in (0, 4):
-            lin("SV", v("zs", 64 * j, n=256), v("zt", 64 * j, n=256), 32.0)
+            lin("SV", v("zs", 64 * j, n=256), v("zt", 128 * j, n=256), 32.0)
         for b, (bank, a) in enumerate((("ps", 0), ("pt", 0), ("py", 0), ("py", 512))):
-            lin("SV", v("wn", 384 * b + 128, n=256), whole[b], 64.0)
-            mm(v(bank, a, n=128), pair("wq", "wp", 128 * b, 128), pair(qz, sz, 0, 128))
-            tt(v("wn", 384 * b + 64, n=64), v(bank, a + 64, n=64), v("zs", 256 + b, s=4, n=64), ALU.add)
-        lin("GSV", v("ub", 0, 32, 2), v("sc", 15, 256, 16))
-        lin("SV", v("ua", 1, 32, 2), v("sc", 15, 256, 16), 64.0, -448.0)
+            lin(cfg["wnf"][b] + "SV".strip(cfg["wnf"][b]), v("wn", 384 * b + 128, n=256), plane[b], 64.0)
+            if h not in cfg["join"]:
+                mm(v(bank, a, n=128), pair("wq", "wp", 128 * b, 128), pair(qz, sz, 0, 128))
+                tt(v("wn", 384 * b + 64, n=64), v(bank, a + 64, n=64), v("zs", 256 + b, s=4, n=64), ALU.add)
+        lin("SV", v("ua", 1, 30, 2), v("sc", 20, 360, 24), -512.0, -3072.0)
         scan(v("uc"), v("ua"), v("ub"), ALU.max, ALU.min)
         if not last:
-            for a, b in ((0, P), (P, 15)):
-                ts(v("il", a + a % 2, n=b - a), v("uc", 2 * a + 1, s=2, n=b - a), 16.0, ALU.mult, rep, ALU.add)
+            for a, b in ((0, P), (P, 16)) if P % 2 else ((0, 16),):
+                ts(v("il", a + a % 2, n=b - a), v("uc", 2 * a + 1, s=2, n=b - a), 16.0, ALU.mult, col[2], ALU.add)
         else:
-            lin("SV", v("wv", 0, 16), v("uc", 1, 32, 2), 16.0, rep)
-            lin("SV", v("wv", 16, 32), v("uc", 1, 32, 2), 16.0, rep)
+            lin("SV", v("wv", 0, 16), v("uc", 1, 32, 2), 16.0, col[2])
+            lin("SV", v("wv", 16, 32), v("uc", 1, 32, 2), 16.0, col[2])
             transpose(v("wt"), v("wv"))
             lin("SV", v("wu"), ind(v("wt"), v("lt", 0, 1)))
-            copy(v("il"), v("wu"))
+            copy(v("il", 0, 16), v("wu"))
         a_, b_, o2_, o3_ = [v("oo", i, n=1) for i in range(4)]
-        slot = lambda buf, k, a=0, n=240: v(buf, w * a + k, s=w, n=n)
-        ts(slot(d1, 1, 0, 256), tab, a_, ALU.not_equal)
-        ts(slot(d1, 2, 0, 256), tab, b_, ALU.not_equal)
-        scan(v("rs", 256, 512), slot(d1, 1, 0, 256), v("kr"))
-        scan(v("rs", 0, 256), slot(d1, 2, 0, 256), v("kr"))
-        if h == 0:
-            lin("GSV", slot(d1, 4), v("tb", 0, 240))
-        lin("SV", v("rw", 0, 64, 2), ind(v("rs", 0, 512), v("lm", 28, 30)))
+        for k, c in ((1, a_), (0, b_)):
+            ts(v("na", 256 * k, n=256), tab, c, ALU.not_equal, 256.0 - k, ALU.mult)
+            scan(v("rs", 256 * k, n=256), v("na", 256 * k, n=256), v("kr"), ALU.min, first=128.0)
+        if cfg["rw"]:
+            for k in (0, 1):
+                lin("GVS", v("rw", 32 * k, s=2, n=16), v("rs", 271 - 256 * k, s=16, n=16))
+        else:
+            lin("SV", v("rw", 0, 64, 2), ind(v("rs", 0, 512), v("lt", 2, 4)))
         tt(v("df"), v("rs", 15, 512, 16), v("rs", 31, 528, 16), ALU.subtract)
         lin("SV", v("sb", 0, 1), o2_, -1.0, o3_)
-        lin("SV", v("sb", 1, 2), v("sb", 2, 3), -1.0, o2_)
-        ts(v("sb", 3, 4), v("ms", 15, 16), v("sb", 1, 2), ALU.is_equal, v("sb", 0, 1), ALU.mult)
+        ts(v("sb", 3, 4), v("mt", 127, 128), o2_, ALU.is_equal, v("sb", 0, 1), ALU.mult)
         if h in cfg["fast"]:
             for a in (0, 1):
                 ts(v("ne", 3 + 128 * a, s=8, n=16), v("rs", 271 - 256 * a, s=16, n=16), o2_, ALU.subtract, v("sb", 3, 4), ALU.not_equal)
@@ -356,48 +386,47 @@ def build(cfg):
             else:
                 ts(v("ne", 4, 128, 8), v("rw", 1, 32, 2), z_, ALU.subtract, v("ch", 32 * s + 15, n=1), ALU.not_equal)
         scan(v("cs"), v("ne"), v("nk"))
-        rho, ba, cc, ev = v("hy", 0, 256, 16), v("hy", 240, 241), v("hx", 0, 256, 16), v("hz", 0, 256, 16)
+        rho, cc = [v(n) if cfg["runs"][h][k // 2] > 1 else slot("dm", k, 16, 16) for k, n in ((1, "hy"), (3, "hx"))]
+        ev = v("hz")
 
-        def repeat(k, rows):
-            while rows < 15:
-                n = min(rows, 15 - rows)
-                lin("VGS" if last and k else "GVS", slot(d1, k, 16 * rows, 16 * n), slot(d1, k, 0, 16 * n))
-                rows += n
-
-        def spread(k, src):
-            scan(slot("dm", k, 1), v("hk"), v(src, 0, 240))
-            act(slot("dm", k, 1), ind(v(src), v("lx", 0, 15)))
-            either("VS")
+        def repeat(k, src):
+            runs = cfg["runs"][h][k // 2]
+            if runs > 1:
+                lin("SV", slot("dm", k, 16, 16 * runs), ind(src, v("ly", 0, runs)))
+            elif src[1] != "dm":
+                lin("GVS", slot("dm", k, 16, 16), src)
+            while runs < 8:
+                lin("GVS", slot("dm", k, 16 + 16 * runs, 16 * runs), slot("dm", k, 16, 16 * runs))
+                runs *= 2
 
         tt(rho, v("rs", 15, 256, 16), v("rs", 271, 512, 16), ALU.subtract)
-        spread(1, "hy")
-        vec(lambda q: q.reciprocal, v("sm", 0, 1), [ba], [])
-        ops[-1]["cost"] = 190 + 6 * cyc
-        tt(ev, v("ee", 16, 32), v("ee", 0, 16), ALU.subtract)
-        lin("VS", slot(d1, 0, 0, 16), ev, v("sm", 0, 1))
-        repeat(0, 1)
-        lin("SV", v("hz", 1, 240, 16), v("hz", 2, 240, 16), 1.0, ba)
-        scan(slot("dm", 4), v("hq"), v("hz", 0, 240))
+        repeat(1, rho)
+        for k, c in ((1, a_), (2, b_)):
+            ts(slot(d1, k), slot(d1, 4), c, ALU.not_equal, v(rho[1], rho[3] - 1, n=1), ALU.mult)
+        tt(ev, v("na", 15, 256, 16), v("na", 271, 512, 16), ALU.subtract)
+        lin("SV", slot(d1, 0), ind(ev, lq), -2.0 ** -8)
+        repeat(4, ev)
         tt(cc, v("cs", 135, 256, 8), v("cs", 7, 128, 8), ALU.is_ge)
-        spread(3, "hx")
+        repeat(3, cc)
         tt(v("dl"), cc, rho, ALU.mult)
-        lin("SV", slot(d1, 3, 0, 16 * cfg["dl"][h]), ind(v("dl"), v("ly", 0, n=cfg["dl"][h])), 2.0 ** -12)
-        repeat(3, cfg["dl"][h])
-        n = 240 * w // cfg["parts"]
-        for k in range(0, 240 * w, n):
-            scan(v(tn, k, n=n), v("dm", k + w, n=n), v(d1, k, n=n))
-        if last:
-            for k, n in ((0, 120), (120, 136)):
-                lin("VS", v("otf", k, n=120), slot(tn, 4, k, 120), 1.0, -128.0)
-                dma("Y", "so%d" % (k // 120), lambda T, k=k, n=n: (T.ot[:, k:k + n], T.otf[:, k:k + n]), [v("otf", k, n=n)], [], 64)
-        else:
-            lin("VSG", v("tb", 0, 240), slot(tn, 4))
+        lin("SV", slot(d1, 3), ind(v("dl"), lq), 2.0 ** -8)
+        n = 128 * w // cfg["parts"]
+        for k in range(16 * w, 144 * w, n):
+            scan(v(tn, k, n=n), v("dm", k, n=n), v(d1, k, n=n))
+        for k, n in ((0, 8), (8, 7 + last)):
+            if last:
+                lin("SV", v("otf", 16 * k, n=16 * n), ind(v(tn), v("lf", k, n=n)), 1.0, -128.0)
+                dma("Y", "so%d" % (k // 8), lambda T, a=16 * k: (T.ot[:, a:a + 128], T.otf[:, a:a + 128]), [v("otf", 16 * k, n=128)], [], 64)
+            else:
+                lin("SV", v("tb", 16 * k, n=16 * n), ind(v(tn), v("lf", k, n=n)))
         add("A", "a", h, [], pair(qz, sz, 128, 64), 0.0, after=[snd["id"]])
         for b in range(4):
             mm(v("pd", 512 * b, n=128), pair("wq", "wp", 128 * b, 128), pair(qz, sz, 64, 128))
             tt(v("wn", 384 * b, n=64), v("pd", 512 * b + 64, n=64), v("zs", b, s=4, n=64), ALU.add)
+            if h in cfg["join"]:
+                tt(v("wn", 384 * b + 64, n=64), v("pd", 512 * b, n=64), v("zs", 256 + b, s=4, n=64), ALU.add)
         for k, e in enumerate(cfg["xlast" if last else "xeng"]):
-            b, (p, n) = k % 4, (((0, 8), (8, 8)) if last else ((0, P), (P, 15 - P)))[k // 4]
+            b, (p, n) = k % 4, (((0, 8), (8, 8)) if last else ((0, P), (P, 16 - P)))[k // 4]
             lin(e + "SV".strip(e), v("xt", 64 + b + 64 * p, s=4, n=16 * n), ind(v("wn", 384 * b, n=384), v("il", p + p % 2, n=n)), 0.03125)
 
     for k in range(2):
@@ -520,8 +549,9 @@ def window(tab, succ, order, a, b):
 
 def fits(w, s, loc, base, state, limit):
     tot = 0.0
-    for (row, free0, rest, past), bs, (end0, frees, tops), lim in zip(loc, base, state, limit):
+    for (row, free0, rest, past), bs, (end0, frees, tops, mean, prev, ends), lim in zip(loc, base, state, limit):
         free, top, end = list(frees[s]), tops[s], list(end0)
+        cap = (lim - tot) * bs - 0.1 * mean + 10.0
         for i in w[s:]:
             e, c, ds, t, q = row[i]
             x = free[e]
@@ -535,6 +565,8 @@ def fits(w, s, loc, base, state, limit):
             end[i] = free[e] = t
             t += q
             if t > top:
+                if t > cap:
+                    return False
                 top = t
         for x, y in zip(rest, free):
             if x + y > top:
@@ -545,14 +577,23 @@ def fits(w, s, loc, base, state, limit):
     return True
 
 
-def trace(w, loc):
-    state, pairs, spans = [], [], []
-    for row, free0, rest, past in loc:
-        free, top, end = list(free0), past, [0.0] * len(row)
-        frees, tops, last, prev, tail = [], [], [None] * len(free), [None] * len(row), None
-        for i in w:
+def trace(w, loc, s, old):
+    state, pairs, spans, held = [], [], [], [None] * len(QUEUES)
+    for i in w[:s]:
+        held[loc[0][0][i][0]] = i
+    for k, (row, free0, rest, past) in enumerate(loc):
+        if s:
+            end, frees, tops, mean, prev, ends = old[k]
+            free, top, tail = list(frees[s]), tops[s], ends[s]
+            del frees[s:], tops[s:], ends[s:]
+        else:
+            free, top, end = list(free0), past, [0.0] * len(row)
+            frees, tops, ends, prev, tail = [], [], [], [None] * len(row), None
+        last = list(held)
+        for i in w[s:]:
             frees.append(tuple(free))
             tops.append(top)
+            ends.append(tail)
             e, c, ds, t, q = row[i]
             p = None
             if free[e] > t:
@@ -571,8 +612,9 @@ def trace(w, loc):
             if prev[tail][1] and prev[tail][0] is not None:
                 pairs.append((prev[tail][0], tail))
             tail = prev[tail][0]
-        state.append((end, frees, tops))
-        spans.append(top + 0.1 * sum(end) / len(end))
+        mean = sum(end) / len(end)
+        state.append((end, frees, tops, mean, prev, ends))
+        spans.append(top + 0.1 * mean)
     return state, pairs, spans
 
 
@@ -601,12 +643,12 @@ def improve(ops, order, cfg):
             for d, gp in t[i][2]:
                 s[d].append((i, gp))
     head = len([o for o in ops if o["kind"] == "d" and not o["r"]])
-    base = [span(order, t)[0] for t in tabs]
+    base = [span(order, t)[0] / m["weight"] for t, m in zip(tabs, COSTS)]
     rng = np.random.default_rng(cfg["seed"])
     order = list(order)
     best, keep = 1e9, None
     for ps in range(passes):
-        hot = cfg["heat"] * (1 - ps / passes) ** 2
+        hot = cfg["heat"] * cfg["cool"] ** (ps / passes) * (ps < passes - 2)
         start = span(order, tabs[1])[1]
         order[head:] = sorted(order[head:], key=lambda i: start[i])
         for lo in range(head - int(rng.integers(width // 2)), n - width // 4, width // 2):
@@ -622,7 +664,7 @@ def improve(ops, order, cfg):
             for i, ds in enumerate(near[-1]):
                 for d in ds:
                     near[1][d].append(i)
-            win, pairs, low = list(range(m)), None, 1e9
+            win, pairs, low, s, state = list(range(m)), None, 1e9, 0, None
             flex = [k for k, i in enumerate(ids) if len(alts[0][i]) > 1]
 
             def move(i, e):
@@ -632,7 +674,7 @@ def improve(ops, order, cfg):
 
             for r0, r1, r2, r3 in rng.random((cfg["moves"], 4)).tolist() + [[2.0] * 4]:
                 if pairs is None:
-                    state, pairs, spans = trace(win, loc)
+                    state, pairs, spans = trace(win, loc, s, state)
                     parts = [x / y for x, y in zip(spans, base)]
                     cur, pos, tl = sum(parts), [0] * m, None
                     if cur < low:
@@ -668,7 +710,8 @@ def improve(ops, order, cfg):
                         new = win[:k + 1] + [i] + win[k + 1:p] + win[p + 1:] if k < p else win[:p] + win[p + 1:k + 1] + [i] + win[k + 1:]
                         if pick[1] != old:
                             move(i, pick[1])
-                        if fits(new, min(k + 1, p), loc, base, state, limit):
+                        s = min(k + 1, p)
+                        if fits(new, s, loc, base, state, limit):
                             win, pairs = new, None
                         elif pick[1] != old:
                             move(i, old)
@@ -678,7 +721,8 @@ def improve(ops, order, cfg):
                     i = flex[int(r1 * len(flex))]
                     other, old = [QUEUES.index(e) for e in alts[0][ids[i]] if QUEUES.index(e) != eng[i]], eng[i]
                     move(i, other[int(r2 * len(other))])
-                    if fits(win, pos[i], loc, base, state, limit):
+                    s = pos[i]
+                    if fits(win, s, loc, base, state, limit):
                         pairs = None
                     else:
                         move(i, old)

import numpy as np
from concourse.mybir import dt, AluOpType as ALU, ActivationFunctionType as ACT, AxisListType as AX

ROUNDS = 3
MARKS = [8, 16, 24, 41, 65, 75, 89, 111, 133, 137, 165, 177, 197, 215, 217, 512]
RUNS = [(0, 1, 3), (3, 3, 3), (8, 2, 3), (4, 1, 2), (7, 4, 2), (13, 1, 2), (15, 1, 1)]
P = 10
CFG = {"xeng": "SSVVSSSV", "xlast": "SSVVSSVV", "fill": "nk kr", "runs": ((1, 1, 1), (1, 1, 1), (1, 8, 1)), "parts": 2,
       "fast": (), "join": (), "rw": 0, "ramp": 1, "oo": False, "aa": (1, 1, 1), "wnf": "SSVV", "dq": 80.0,
       "passes": 62, "moves": 400, "width": 44, "heat": 0.03, "cool": 0.08, "seed": 1, "flip": 0.1, "put": 0.6,
       "wake": 225.0, "lat": 1900.0, "f": 1.1, "gc": 1.5, "sfix": 60.0, "pe": 0.8, "issue": 150.0, "once": 300.0, "dma": 1500.0, "kb": 4.0}
RANGES = {"wake": (140, 290), "f": (1.0, 1.5), "gc": (1.04, 2.08), "pe": (0.45, 0.9), "lat": (700, 1800), "issue": (100, 350),
          "once": (300, 1200), "dma": (800, 1500), "sfix": (30, 90), "kb": (2.5, 4.0)}
SETS = 7
COSTS = [dict({k: a + (b - a) * ((i * (1 + j % (SETS - 1)) + 3 * j) % SETS + 0.5) / SETS for j, (k, (a, b)) in enumerate(RANGES.items())},
              weight=1.0) for i in range(SETS)]

BF, F32, I32, U16, MXC, U8 = "bfloat16", "float32", "int32", "uint16", "float8_e4m3fn_x4", "uint8"
SB = {}
for _d, _names in (
        (BF, "xn1024 ut512 vt512 et516 xt1280 gg384 sc360 fh1024 wn1536 ee80 oo6 gt64 ms64 ab512 zt768 zs512 tb256 "
             "dm720 da728 db728 na512 rs528 sb8 ch96 ne256 nk256 cs256 dl16 kf384 nm128 "
             "ph16 pq16 cq128 cp128 dd128 nq512 mt512 rd6 kv128 st80 kh5 "
             "kd64 kr256 jc80 ka16 ua32 ub32 uc32 rw64 df32 fl5 hx16 hy16 hz16"),
        (F32, "ts576 aa256 sq5 wv32 wt32 wu16 otf256 ys256 col16 pc25"),
        (I32, "ti256 ic32 ie32 iw32 ih32 ya66 yb98"),
        (U16, "oi4 oj8 ok8 il18 lm18 le6 lp8 lf16 lab32 ly16 lt4"),
        (MXC, "wq512 qn256 qu128 qv128 qe512 qf256"), (U8, "wp512 sn256 su128 sv128 se512 sf256")):
    for _n in _names.split():
        SB[_n.rstrip("0123456789")] = (int(_n.lstrip("abcdefghijklmnopqrstuvwxyz")), _d)
for _h in range(ROUNDS):
    for _n, _w, _d in (("qx", 320, MXC), ("sx", 320, U8), ("qa", 128, MXC), ("sa", 128, U8), ("qz", 192, MXC), ("sz", 192, U8)):
        SB["%s%d" % (_n, _h)] = (_w, _d)
PSUM = {"ps": 512, "pt": 512, "pd": 2048, "py": 1024}
SCRATCH = {k: ("sbuf", [128, n], d) for k, (n, d) in SB.items()}
SCRATCH.update({k: ("psum", [128, n], F32) for k, n in PSUM.items()})
SEMAPHORES = ["cV", "cS", "cP", "cG", "sent", "arr0", "arr1", "arr2", "l0", "l1", "l2", "l3", "l4", "l5", "l6",
              "sc0", "sc1", "ss0", "ss1", "ss2", "ss3", "so0", "so1", "sy0", "sy1"]


def v(name, a=0, b=None, s=1, n=None):
    if n is not None:
        b = a + s * (n - 1) + 1
    if b is None:
        b = SB[name][0] if name in SB else PSUM[name]
    return ("v", name, a, b, s)


def ind(win, off):
    return ("i", win, off)


def words(x):
    return ("w", x)


def count(x):
    return 16 * count(x[2]) if x[0] == "i" else count(x[1]) if x[0] == "w" else len(range(x[2], x[3], x[4]))


def views(x):
    if not isinstance(x, tuple):
        return []
    return views(x[1]) + views(x[2]) if x[0] == "i" else views(x[1]) if x[0] == "w" else [x]


def ap(T, x):
    if not isinstance(x, tuple):
        return x
    if x[0] == "i":
        return ap(T, x[1]).indirect(ap(T, x[2]))
    if x[0] == "w":
        return ap(T, x[1]).bitcast(dt.uint32)
    return T[x[1]][:, x[2]:x[3]] if x[4] == 1 else T[x[1]][:, x[2]:x[3]:x[4]]


def build(cfg):
    ops = []
    cyc = 0.83 * cfg["f"]

    def add(eng, kind, emit, reads, writes, cost, **kw):
        o = {"eng": eng, "kind": kind, "emit": emit, "r": [w for x in reads for w in views(x)],
             "w": [w for x in writes for w in views(x)], "cost": cost, "lat": 0.0, "id": len(ops), "after": []}
        o.update(kw)
        ops.append(o)
        return o

    def vec(call, out, ins, args, per=None):
        if per is None:
            per = 0.5 if all(w[1] in SB and SB[w[1]][1] in (BF, U16) for x in [out] + ins for w in views(x)) else 1
        cost = 50 + count(out) * cfg["gc"] * cyc if ins and ins[0][0] == "i" else max(64, count(out) * per) * cyc
        add("V", "c", lambda g, T: call(g.vector)(*[ap(T, x) for x in [out] + ins + args]), ins + args, [out], cost)

    def copy(out, a):
        vec(lambda q: q.tensor_copy, out, [a], [])

    def tt(out, a, b, op):
        vec(lambda q: q.tensor_tensor, out, [a, b], [op], 1 if a[1] in PSUM else 2)

    def ts(out, a, s1, op0, s2=None, op1=None):
        vec(lambda q: q.tensor_scalar, out, [a], [s1, None, op0] if op1 is None else [s1, s2, op0, op1])

    def scan(out, a, b, op0=ALU.mult, op1=ALU.add, first=0.0):
        vec(lambda q: q.tensor_tensor_scan, out, [a, b], [first, op0, op1])

    def nearest(out, a):
        vec(lambda q: lambda o, x: q.tensor_reduce(o, x, AX.X, ALU.min, apply_absolute_value=True), out, [a], [])

    def transpose(out, a):
        vec(lambda q: q.transpose, out, [a], [])

    def memset(out, c):
        vec(lambda q: q.memset, out, [], [c])

    def quant(q, s, a):
        add("V", "c", lambda g, T: g.vector.quantize_mx(ap(T, q), ap(T, s), ap(T, a)), [a], [q, s],
            (12 + 0.22 * count(a)) * cfg["f"])

    def act(out, a, func=ACT.Identity, **kw):
        n = count(out)
        cost = 65 + n * cfg["gc"] * cyc if a[0] == "i" else cfg["sfix"] + max(64, n) * cyc
        add("S", "c", lambda g, T: g.scalar.activation(ap(T, out), ap(T, a), func, **{k: ap(T, x) for k, x in kw.items()}),
            [a] + list(kw.values()), [out], cost)

    def either(engs):
        forms = ops[-len(engs):]
        del ops[len(ops) - len(engs) + 1:]
        alts = {o["eng"]: (o["emit"], o["cost"]) for o in forms}
        ops[-1].update(alts={**ops[-1].get("alts", {}), **alts}, r=[x for o in forms for x in o["r"]])

    def lin(engs, out, a, scale=1.0, bias=None):
        for e in engs:
            if e == "G":
                add("G", "c", lambda g, T: g.affine_select(ap(T, out), ap(T, a), [[0, count(a)]], ALU.is_ge, 0.0, 0, 0),
                    [a], [out], (205 + 2 * count(out)) * cyc)
            elif e == "S":
                act(out, a, **({"scale": scale} if bias is None else {"scale": scale, "bias": bias}))
            elif bias is not None:
                ts(out, a, scale, ALU.mult, bias, ALU.add)
            elif scale == 1.0:
                copy(out, a)
            else:
                ts(out, a, scale, ALU.mult)
        either(engs)

    def mm(out, l, r):
        add("P", "c", lambda g, T: g.tensor.matmul_mx(*[ap(T, x) for x in [out] + l + r], True, True),
            l + r, [out], (count(r[0]) + 16) * cfg["pe"])

    def pair(q, s, a, n):
        return [v(q, a, n=n), v(s, a, n=n)]

    def iota(out, pattern, base, cm):
        kw = {} if SB[out[1]][1] == I32 else {"allow_small_or_imprecise_dtypes": True}
        add("G", "c", lambda g, T: g.iota(ap(T, out), pattern, base, cm, **kw), [], [out], (157 + 2 * count(out)) * cyc)

    def select(out, pattern, val, base, cm, op=ALU.not_equal):
        add("G", "c", lambda g, T: g.affine_select(ap(T, out), ap(T, out), pattern, op, val, base, cm),
            [out], [out], (205 + 2 * count(out)) * cyc)

    def fill(out, c):
        engs = "VG" if count(out) > 64 and out[1] not in cfg["fill"] else "GV"
        for e in engs:
            if e == "V":
                memset(out, float(c))
            else:
                iota(out, [[0, count(out)]], c, 0)
        either(engs)

    def dma(q, sem, sides, reads, writes, kb):
        for e in q:
            add(e, "d", lambda g, T, e=e: (g.sync if e == "Y" else g.scalar).dma_start(*sides(T)), reads, writes, cfg["dq"],
                sem=sem, lat=cfg["dma"] + (cfg["kb"] * kb if writes else 0.0))
        either(q)
        o = ops[-1]
        if not writes:
            add("D", "t", None, [], [], cfg["kb"] * kb, after=[o["id"]])

    dma("Y", "l1", lambda T: (T.xn[:, 0:512], T.x[:, 0:512]), [], [v("xn", 0, 512)], 192)
    dma("S", "l6", lambda T: (T.xn[:, 512:1024], T.x[:, 512:1024]), [], [v("xn", 512)], 256)
    dma("Y", "l0", lambda T: (T.ut[:], T.u[:]), [], [v("ut")], 384)
    k = len(ops)
    dma("Y", "l2", lambda T: (T.ti[:], T.tri[:]), [v("ut")], [v("ti")], 128)
    dma("Y", "l3", lambda T: (T.wq[:].bitcast(dt.uint8), T.wc[:]), [v("ut")], [v("wq")], 384)
    dma("Y", "l4", lambda T: (T.wp[:], T.ws[:]), [v("ut")], [v("wp")], 448)
    dma("Y", "l5", lambda T: (T.vt[:], T.v[:]), [v("ut")], [v("vt")], 576)

    iota(v("pc"), [[256, 25]], 0, 1)
    num = lambda a=0, b=16, s=1: v("nm", a, b, s)
    pc, fl, col = [[v(n, k, n=1) for k in range(SB[n][0])] for n in ("pc", "fl", "col")]
    for a in (0, 258):
        fill(v("et", a, n=258), 0)
    if cfg["ramp"]:
        memset(v("kf", 0, 384, 3), 1.0)
        scan(v("nm"), v("kf", 0, 384, 3), v("kf", 0, 384, 3), first=-1.0)
        ts(v("et", 3, s=4, n=128), v("nm"), pc[0], ALU.is_equal, 0.5, ALU.mult)
    else:
        fill(v("kf", 0, 192, 3), 1)
        iota(v("nm", 0, 16), [[1, 16]], 0, 0)
        select(v("et", 3, s=4, n=128), [[-1, 128]], 0.5, 0, 1)
    for b in range(4):
        quant(*pair("qe", "se", 128 * b, 128), v("et", 3 - b, n=512))
    lin("SV", v("fl"), num(0, 5), pc[0], 6128.4)
    rep, low, odd, high = col[12:16]

    def ramp(out, step, base):
        lin("SV", out, num(0, count(out)), float(step), float(base))
        iota(out, [[step, count(out)]], base, 0)
        either("SG")

    lin("SV", rep, fl[2], -0.5, pc[12])
    lin("SV", col[2], fl[2], -0.5, pc[4])
    lin("SV", low, fl[4], -0.25, pc[6])
    lin("SV", odd, fl[1], -2.0, fl[2])
    lin("SV", high, fl[2], -2.0, fl[4])
    ts(v("lt", 0, 1), fl[1], -1.0, ALU.mult, pc[24], ALU.add)
    for out, step, base, cm in ((v("ya", 0, 18), 1, 255, 16), (v("ya", 18, 26), 0, 0, 16),
                                (v("ya", 26, 34), 16, 16, 16), (v("ya", 34, 50), 241, 0, 16), (v("ya", 50, 66), 16, 4096, -16)):
        iota(out, [[step, count(out)]], base, cm)
    for a, b in ((0, 34), (34, 66)):
        ts(v("yb", a, b), v("ya", a, b), 255, ALU.bitwise_and)
    copy(v("lm"), v("yb", 0, 18))
    ts(v("ly"), v("yb", 18, 34), 0.0625, ALU.mult)
    lin("SV", col[3], rep, -255.0, 1792.0)
    if not cfg["rw"]:
        lin("SV", col[1], rep, 16.0, 271.0)
        ts(v("lt", 2, 4), num(0, 2), -256.0, ALU.mult, col[1], ALU.add)
    for a in (0, 1):
        iota(v("ic", 16 * a, n=16), [[231, 2], [-264, 2], [66, 4]], 99 - 33 * a, 0)
    lin("SV", col[11], odd, -1.03125, -6270.0)
    ts(col[0], high, odd, ALU.subtract, 1.03125, ALU.mult)
    lin("SV", col[4], low, 33.0, col[11])
    ts(col[6], low, 7.0, ALU.not_equal)
    lin("SV", col[8], odd, 1.0, 6144.0)
    ts(v("ie"), v("ic"), col[0], ALU.add)
    for a, op, far in ((0, ALU.min, 7), (8, ALU.min, 0), (16, ALU.max, 8), (24, ALU.max, 1)):
        ts(v("iw", a, n=8), v("ie", a, n=8), col[4], op, 33.0 * far, ALU.add)
    ts(v("ih"), v("iw"), 0x3C1, ALU.bitwise_and)
    ts(v("lab"), v("ih"), col[6], ALU.mult, col[8], ALU.add)
    iota(v("kv"), [[-2, 2], [-2, 8], [2, 8]], 1, 0)
    ts(v("kf", 2, 360, 3), v("kv", 0, 120), -1.0, ALU.max, 1.0, ALU.min)
    fill(v("kf", 192, 360, 3), -1)
    fill(v("kf", 213, 360, 24), 1)
    lin("GSV", v("kf", 1, 192, 3), v("kf", 2, 192, 3))
    lin("SV", v("kf", 193, 360, 3), v("kf", 194, 360, 3), -1.0)
    fill(v("kf", 214, 360, 24), 1)
    fill(v("kf", 0, 360, 24), 0)
    fill(v("gg", 2, 384, 3), 1)
    ramp(v("gg", 2, 384, 24), 1, -18)
    for a, step, n in RUNS:
        ramp(v("ph", a, s=step, n=n), MARKS[a + step] - MARKS[a] if n > 1 else 0, MARKS[a])
    lin("SV", v("pq"), v("ph"), 2.0 ** -9)
    lin("SV", v("gg", 5, 384, 24), v("ph"), 2.0 ** -9)
    lq = v("ly", 8, 16)
    ts(v("lp"), v("yb", 26, 34), rep, ALU.add)
    lin("SV", v("cq"), ind(v("pq"), v("ly", 0, 8)))
    tt(v("cp"), ind(v("pq"), lq), v("cq"), ALU.add)
    ts(v("yb", 66, 82), v("yb", 50, 66), rep, ALU.add)
    tt(v("yb", 82, 98), v("yb", 34, 50), v("yb", 66, 82), ALU.min)
    ts(v("lf"), v("yb", 82, 98), 5.0, ALU.mult, 4.0, ALU.add)
    ts(v("le", 0, 5), v("yb", 18, 23), 0.125, ALU.mult)
    iota(v("jc"), [[1, 5], [0, 16]], 132, 0)
    lin("SV", v("kh"), num(0, 5), 0.0, 0.0625)
    ts(v("ka"), num(), rep, ALU.is_equal)
    lin("SV", v("kd"), ind(v("ka"), v("ly", 0, 4)), 1040.0, -16.0)
    iota(v("rw", 1, 64, 2), [[0, 2], [1, 16]], 128, 0)
    ramp(v("ub", 1, 32, 2), 1, 136)
    w = 5
    slot = lambda buf, k, a=16, n=128: v(buf, w * a + k, s=w, n=n)
    for out, c in ((v("ub", 30, 31), 228), (v("ua"), 256), (v("ts", 0, 64, 2), 0), (v("ts", 513, 576, 2), 0), (v("kr"), -1),
                   (v("kr", 15, 256, 16), 143), (v("zt", 256, 512), 0), (v("xt", 0, 64), 0), (v("xt", 1088, 64 * P + 576), 0),
                   (v("ne", 0, 256, 8), 0), (v("ne", 132, 256, 8), 1), (v("ne", 135, 256, 8), -1), (v("nk"), 0), (v("nk", 0, 256, 8), 1),
                   (v("nk", 135, 256, 8), 1), (v("rs", 512, 528), 0),
                   (slot("dm", 0), 0), (slot("dm", 2), -1), (v("da", 0, 80), 143), (v("db", 0, 80), 143), (v("da", 720), 0), (v("db", 720), 0)):
        fill(out, c)

    quant(v("qu"), v("su"), v("ut"))
    for a in (0, 128):
        lin("VS", v("tb", a, n=128), v("ti", a, n=128), 1.0, 128.0)
    quant(v("qv"), v("sv"), v("vt"))
    uq = pair("qu", "su", 0, 128)

    for h in range(ROUNDS):
        qx, sx, qa, sa, qz, sz = ["%s%d" % (k, h) for k in ("qx", "sx", "qa", "sa", "qz", "sz")]
        last = h == ROUNDS - 1
        d1, tn = ("da", "db") if h % 2 == 0 else ("db", "da")
        if h == 0:
            for k in range(2):
                quant(*pair("qn", "sn", 128 * k, 128), v("xn", 512 * k, n=512))
            for a, b in ((0, P + 2 - P % 2), (P + 2 - P % 2, P + 8)):
                copy(words(v(qx, 16 * a, 16 * b)), ind(words(v("qn")), v("lm", a, b)))
                act(v(sx, 16 * a, 16 * b), ind(v("sn"), v("lm", a, b)), func=ACT.Copy)
        else:
            quant(*pair(qx, sx, 0, 16 * P + 16), v("xt", 0, 64 * P + 64))
            quant(*pair(qx, sx, 16 * P + 16, 128), v("xt", 64 * P + 64, n=512))
        tab = v("tb")
        mm(v("ps", 0, 16 * P + 16), uq, pair(qx, sx, 0, 16 * P + 16))
        mm(v("pt", 0, 128), uq, pair(qx, sx, 16 * P, 128))
        for a, e, n in ((1, 0, (P + 1) // 2), (64, 16, P // 2)):
            transpose(v("ts", a, s=2, n=32 * n), v("ps", e, n=32 * n))
            transpose(v("ts", a + 64 * n, s=2, n=256 - 32 * n), v("pt", e + 32 * n - 16 * P, n=256 - 32 * n))
        plane = [v("fh", 256 * b, n=256) for b in range(4)]
        for b in range(4):
            mm(v("pd", 512 * b, n=256), pair("qe", "se", 128 * b, 128), pair(qx, sx, 16, 256))
            lin("SV", plane[b], v("pd", 512 * b, n=256))
        if h == 0:
            lin("SV", slot(d1, 4), ind(tab, v("lp")))
        scan(v("dd"), slot(d1, 4), slot(d1, 4, 17), ALU.max, ALU.subtract)
        pieces = ((1, 12, 4, 320, 320), (0, 4, 8, 320, 576), (193, 0, 4, 576, 576))
        for e, a, n, lower, higher in pieces if cfg["aa"][h] else ((0, 4, 12, 320, 0), pieces[2]):
            lin("SV", v("aa", 16 * a, n=16 * n), ind(v("ts", 0, lower), v("lab", a, n=n)))
        for e, a, n, lower, higher in pieces:
            tt(v("gg", e, s=3, n=16 * n), ind(v("ts", 0, higher), v("lab", 16 + a, n=n)), v("aa", 16 * a, n=16 * n), ALU.is_le)
        for a, b in ((0, 192), (192, 360)):
            scan(v("sc", a, b), v("kf", a, b), v("gg", a, b))
        mark = [v("rd", j, n=1) for j in range(5)]
        for j in range(5):
            nearest(mark[j], v("sc", 19 + j, 360, 24))
        for a, b in ((0, 1), (1, 5)) if cfg["oo"] else ((0, 5),):
            lin("VS" if a or b > 1 else "SV", v("oo", a, b), v("rd", a, b), 32.0, 128.0)
        for j in range(4):
            ts(v("nq", 128 * j, n=128), v("cp"), mark[j], ALU.subtract, mark[j + 1], ALU.not_equal)
            scan(v("mt", 128 * j, n=128), v("nq", 128 * j, n=128), v("dd"))
        ts(v("ok", 0, 4), v("mt", 127, 512, 128), 16.0, ALU.mult, col[2], ALU.add)
        lin("SV", v("ub", 0, 30, 2), v("sc", 20, 360, 24), -1.0, 129.25)
        tt(v("ee"), ind(v("ub"), v("le", 0, 5)), v("jc"), ALU.not_equal)
        scan(v("st"), v("ee"), v("kr", 0, 80))
        scan(v("sq"), v("kh"), v("st", 15, 80, 16), first=2048 / 15)
        ts(v("oi"), v("sq", 1, 5), 16.0, ALU.mult, -2185.0, ALU.add)
        lin("SV", v("gt"), ind(tab, v("oi")))
        scan(v("ms"), v("kd"), v("gt"), ALU.add, ALU.min)
        ts(v("ok", 4, n=4), v("ms", 15, s=16, n=4), 16.0, ALU.mult, col[3], ALU.add)
        for j, pts in ((0, v("oo", 1, 5)), (4, v("st", 31, 80, 16))):
            ts(v("oj", j, n=4), pts, 16.0, ALU.mult, col[2], ALU.add)
            for b in range(4):
                lin("SV", v("ab", 128 * b + 16 * j, n=64), ind(plane[b], v("oj", j, n=4)))
        for j in (0, 4):
            for b in range(4):
                tt(v("zt", 128 * j + b, s=4, n=64), ind(plane[b], v("ok", j, n=4)), v("ab", 128 * b + 16 * j, n=64), ALU.add)
            quant(*(pair(qz, sz, 0, 128) if j else pair(qa, sa, 0, 128)), v("zt", 64 * j, n=512))
            if j == 0:
                snd = add("G", "r", h, pair(qa, sa, 0, 64), [], cfg["issue"] + (0 if h else cfg["once"]), lat=cfg["lat"])
        for j in (0, 4):
            lin("SV", v("zs", 64 * j, n=256), v("zt", 128 * j, n=256), 32.0)
        for b, (bank, a) in enumerate((("ps", 0), ("pt", 0), ("py", 0), ("py", 512))):
            lin(cfg["wnf"][b] + "SV".strip(cfg["wnf"][b]), v("wn", 384 * b + 128, n=256), plane[b], 64.0)
            if h not in cfg["join"]:
                mm(v(bank, a, n=128), pair("wq", "wp", 128 * b, 128), pair(qz, sz, 0, 128))
                tt(v("wn", 384 * b + 64, n=64), v(bank, a + 64, n=64), v("zs", 256 + b, s=4, n=64), ALU.add)
        lin("SV", v("ua", 1, 30, 2), v("sc", 20, 360, 24), -512.0, -3072.0)
        scan(v("uc"), v("ua"), v("ub"), ALU.max, ALU.min)
        if not last:
            for a, b in ((0, P), (P, 16)) if P % 2 else ((0, 16),):
                ts(v("il", a + a % 2, n=b - a), v("uc", 2 * a + 1, s=2, n=b - a), 16.0, ALU.mult, col[2], ALU.add)
        else:
            lin("SV", v("wv", 0, 16), v("uc", 1, 32, 2), 16.0, col[2])
            lin("SV", v("wv", 16, 32), v("uc", 1, 32, 2), 16.0, col[2])
            transpose(v("wt"), v("wv"))
            lin("SV", v("wu"), ind(v("wt"), v("lt", 0, 1)))
            copy(v("il", 0, 16), v("wu"))
        a_, b_, o2_, o3_ = [v("oo", i, n=1) for i in range(4)]
        for k, c in ((1, a_), (0, b_)):
            ts(v("na", 256 * k, n=256), tab, c, ALU.not_equal, 256.0 - k, ALU.mult)
            scan(v("rs", 256 * k, n=256), v("na", 256 * k, n=256), v("kr"), ALU.min, first=128.0)
        if cfg["rw"]:
            for k in (0, 1):
                lin("GVS", v("rw", 32 * k, s=2, n=16), v("rs", 271 - 256 * k, s=16, n=16))
        else:
            lin("SV", v("rw", 0, 64, 2), ind(v("rs", 0, 512), v("lt", 2, 4)))
        tt(v("df"), v("rs", 15, 512, 16), v("rs", 31, 528, 16), ALU.subtract)
        lin("SV", v("sb", 0, 1), o2_, -1.0, o3_)
        ts(v("sb", 3, 4), v("mt", 127, 128), o2_, ALU.is_equal, v("sb", 0, 1), ALU.mult)
        if h in cfg["fast"]:
            for a in (0, 1):
                ts(v("ne", 3 + 128 * a, s=8, n=16), v("rs", 271 - 256 * a, s=16, n=16), o2_, ALU.subtract, v("sb", 3, 4), ALU.not_equal)
        else:
            ts(v("ne", 3, 256, 8), v("rw", 0, 64, 2), o2_, ALU.subtract, v("sb", 3, 4), ALU.not_equal)
        ts(v("ne", 7, 128, 8), v("rw", 1, 32, 2), o2_, ALU.subtract, v("sb", 3, 4), ALU.not_equal)
        z_ = v("rs", 271, 272)
        for s, k in enumerate((3, 1, 2)):
            n = 32 if s < 2 else 16
            scan(v("ch", 32 * s, n=n), v("ne", k, s=8, n=n), v("df", 0, n))
            if s < 2:
                ts(v("ne", s + 1, 128, 4), v("rw", 0, 32), z_, ALU.subtract, v("ch", 32 * s + 15, n=1), ALU.not_equal)
                ts(v("ne", 129 + s, 256, 4), v("rw", 32, 64), v("ch", 32 * s + 31, n=1), ALU.not_equal)
            else:
                ts(v("ne", 4, 128, 8), v("rw", 1, 32, 2), z_, ALU.subtract, v("ch", 32 * s + 15, n=1), ALU.not_equal)
        scan(v("cs"), v("ne"), v("nk"))
        rho, cc = [v(n) if cfg["runs"][h][k // 2] > 1 else slot("dm", k, 16, 16) for k, n in ((1, "hy"), (3, "hx"))]
        ev = v("hz")

        def repeat(k, src):
            runs = cfg["runs"][h][k // 2]
            if runs > 1:
                lin("SV", slot("dm", k, 16, 16 * runs), ind(src, v("ly", 0, runs)))
            elif src[1] != "dm":
                lin("GVS", slot("dm", k, 16, 16), src)
            while runs < 8:
                lin("GVS", slot("dm", k, 16 + 16 * runs, 16 * runs), slot("dm", k, 16, 16 * runs))
                runs *= 2

        tt(rho, v("rs", 15, 256, 16), v("rs", 271, 512, 16), ALU.subtract)
        repeat(1, rho)
        for k, c in ((1, a_), (2, b_)):
            ts(slot(d1, k), slot(d1, 4), c, ALU.not_equal, v(rho[1], rho[3] - 1, n=1), ALU.mult)
        tt(ev, v("na", 15, 256, 16), v("na", 271, 512, 16), ALU.subtract)
        lin("SV", slot(d1, 0), ind(ev, lq), -2.0 ** -8)
        repeat(4, ev)
        tt(cc, v("cs", 135, 256, 8), v("cs", 7, 128, 8), ALU.is_ge)
        repeat(3, cc)
        tt(v("dl"), cc, rho, ALU.mult)
        lin("SV", slot(d1, 3), ind(v("dl"), lq), 2.0 ** -8)
        n = 128 * w // cfg["parts"]
        for k in range(16 * w, 144 * w, n):
            scan(v(tn, k, n=n), v("dm", k, n=n), v(d1, k, n=n))
        for k, n in ((0, 8), (8, 7 + last)):
            if last:
                lin("SV", v("otf", 16 * k, n=16 * n), ind(v(tn), v("lf", k, n=n)), 1.0, -128.0)
                dma("Y", "so%d" % (k // 8), lambda T, a=16 * k: (T.ot[:, a:a + 128], T.otf[:, a:a + 128]), [v("otf", 16 * k, n=128)], [], 64)
            else:
                lin("SV", v("tb", 16 * k, n=16 * n), ind(v(tn), v("lf", k, n=n)))
        add("A", "a", h, [], pair(qz, sz, 128, 64), 0.0, after=[snd["id"]])
        for b in range(4):
            mm(v("pd", 512 * b, n=128), pair("wq", "wp", 128 * b, 128), pair(qz, sz, 64, 128))
            tt(v("wn", 384 * b, n=64), v("pd", 512 * b + 64, n=64), v("zs", b, s=4, n=64), ALU.add)
            if h in cfg["join"]:
                tt(v("wn", 384 * b + 64, n=64), v("pd", 512 * b, n=64), v("zs", 256 + b, s=4, n=64), ALU.add)
        for k, e in enumerate(cfg["xlast" if last else "xeng"]):
            b, (p, n) = k % 4, (((0, 8), (8, 8)) if last else ((0, P), (P, 16 - P)))[k // 4]
            lin(e + "SV".strip(e), v("xt", 64 + b + 64 * p, s=4, n=16 * n), ind(v("wn", 384 * b, n=384), v("il", p + p % 2, n=n)), 0.03125)

    for k in range(2):
        quant(*pair("qf", "sf", 128 * k, 128), v("xt", 64 + 512 * k, n=512))
        mm(v("py", 512 * k, n=128), pair("qv", "sv", 0, 128), pair("qf", "sf", 128 * k, 128))
        dma("Y", "sc%d" % k, lambda T, k=k: (T.oc[:, 512 * k:512 * k + 512], T.qf[:, 128 * k:128 * k + 128].bitcast(dt.uint8)),
            [v("qf", 128 * k, n=128)], [], 64)
    for k in range(4):
        dma("YS", "ss%d" % k, lambda T, k=k: (T.osc[4 * k:4 * k + 4, :], T.sf[32 * k:32 * k + 4, :]), [v("sf")], [], 1)
    lin("SV", v("ys", 0, 128), v("py", 0, 128))
    lin("VS", v("ys", 128, 256), v("py", 512, 640))
    for k in range(2):
        dma("SY", "sy%d" % k, lambda T, k=k: (T.y[:, 128 * k:128 * k + 128], T.ys[:, 128 * k:128 * k + 128]),
            [v("ys", 128 * k, n=128)], [], 64)
    return ops


def depend(ops):
    writer, readers = {}, {}
    for o in ops:
        d = set(o["after"])
        rk, wk = set(), set()
        for ws, ks in ((o["r"], rk), (o["w"], wk)):
            for x in ws:
                if x[1] in PSUM:
                    ks.update((x[1], c) for c in range(x[2] // 512, (x[3] - 1) // 512 + 1))
                else:
                    ks.update((x[1], c) for c in range(x[2], x[3], x[4]))
        for k in rk:
            if k in writer:
                d.add(writer[k])
            if k[0] in PSUM:
                d.update(r for r in readers.get(k, ()) if ops[r]["eng"] != o["eng"] or "alts" in o or "alts" in ops[r])
        for k in wk:
            if k in writer:
                d.add(writer[k])
            d.update(readers.get(k, ()))
        for k in rk:
            readers.setdefault(k, []).append(o["id"])
        for k in wk:
            writer[k] = o["id"]
            readers[k] = []
        d.discard(o["id"])
        o["dep"] = sorted(d)


def gap(cfg, a, b):
    return a["lat"] + (0.0 if b["kind"] in "at" else cfg["wake"])


def schedule(ops, cfg):
    rank = [o["cost"] + o["lat"] for o in ops]
    for o in reversed(ops):
        for d in o["dep"]:
            rank[d] = max(rank[d], ops[d]["cost"] + gap(cfg, ops[d], o) + rank[o["id"]])
    busy = {}
    loads = [o["id"] for o in ops if o["kind"] == "d" and not o["r"]]
    for i in loads + sorted((i for i in range(len(ops)) if i not in loads), key=lambda i: (-rank[i], i)):
        o = ops[i]
        t = max([ops[d]["end"] + gap(cfg, ops[d], o) for d in o["dep"]] + [0.0])
        line = busy.setdefault(o["eng"], [])
        for s, e in line:
            if t + o["cost"] <= s:
                break
            t = max(t, e)
        o["start"], o["end"] = t, t + o["cost"]
        line.append((o["start"], o["end"]))
        line.sort()
    return [o["id"] for o in sorted(ops, key=lambda o: (o["start"], o["id"]))]


def span(order, tab):
    end, start, free, top = [0.0] * len(tab), [0.0] * len(tab), {}, 0.0
    for i in order:
        e, c, ds, lat = tab[i]
        start[i] = max([free.get(e, 0.0)] + [end[d] + gp for d, gp in ds])
        end[i] = free[e] = start[i] + c
        top = max(top, end[i] + lat)
    return top, start


def tables(ops, cfg):
    tabs, alts = [], []
    for m in COSTS:
        c = dict(cfg)
        c.update(m)
        new = build(c)
        alts.append([{e: x[1] for e, x in o.get("alts", {}).items()} for o in new])
        tabs.append([(o["eng"], new[o["id"]]["cost"], [(d, gap(c, new[d], new[o["id"]])) for d in o["dep"]],
                      new[o["id"]]["lat"] if o["kind"] == "d" else 0.0) for o in ops])
    reach, out = [0] * len(ops), [[] for t in tabs]
    for i, o in enumerate(ops):
        for d in o["dep"]:
            reach[i] |= reach[d]
        keep = [k for k, d in enumerate(o["dep"]) if not (reach[i] >> d) & 1 or ops[d]["lat"] > 0]
        for d in o["dep"]:
            reach[i] |= 1 << d
        for t, x in zip(tabs, out):
            x.append((t[i][0], t[i][1], [t[i][2][k] for k in keep], t[i][3]))
    return out, alts


QUEUES = "VSPGYAD"


def window(tab, succ, order, a, b):
    end, free, rest, q = {}, {}, {}, {}
    for i in order[:a]:
        e, c, ds, lat = tab[i]
        end[i] = free[e] = max([free.get(e, 0.0)] + [end[d] + gp for d, gp in ds]) + c
    for i in reversed(order[b:]):
        e, c, ds, lat = tab[i]
        q[i] = rest[e] = max([rest.get(e, 0.0), lat] + [q[d] + gp for d, gp in succ[i]]) + c
    past = max([end[i] + tab[i][3] for i in end] + [end[i] + gp + q[d] for i in end for d, gp in succ[i] if d in q] + [0.0])
    row = {i: (tab[i][0], tab[i][1], [(d, gp) for d, gp in tab[i][2] if d not in end],
               max([end[d] + gp for d, gp in tab[i][2] if d in end] + [0.0]),
               max([q[d] + gp for d, gp in succ[i] if d in q] + [tab[i][3]])) for i in order[a:b]}
    return row, free, rest, past


def fits(w, s, loc, base, state, limit):
    tot = 0.0
    for (row, free0, rest, past), bs, (end0, frees, tops, mean, prev, ends), lim in zip(loc, base, state, limit):
        free, top, end = list(frees[s]), tops[s], list(end0)
        cap = (lim - tot) * bs - 0.1 * mean + 10.0
        for i in w[s:]:
            e, c, ds, t, q = row[i]
            x = free[e]
            if x > t:
                t = x
            for d, gp in ds:
                x = end[d] + gp
                if x > t:
                    t = x
            t += c
            end[i] = free[e] = t
            t += q
            if t > top:
                if t > cap:
                    return False
                top = t
        for x, y in zip(rest, free):
            if x + y > top:
                top = x + y
        tot += (top + 0.1 * sum(end) / len(end)) / bs
        if tot > lim:
            return False
    return True


def trace(w, loc, s, old):
    state, pairs, spans, held = [], [], [], [None] * len(QUEUES)
    for i in w[:s]:
        held[loc[0][0][i][0]] = i
    for k, (row, free0, rest, past) in enumerate(loc):
        if s:
            end, frees, tops, mean, prev, ends = old[k]
            free, top, tail = list(frees[s]), tops[s], ends[s]
            del frees[s:], tops[s:], ends[s:]
        else:
            free, top, end = list(free0), past, [0.0] * len(row)
            frees, tops, ends, prev, tail = [], [], [], [None] * len(row), None
        last = list(held)
        for i in w[s:]:
            frees.append(tuple(free))
            tops.append(top)
            ends.append(tail)
            e, c, ds, t, q = row[i]
            p = None
            if free[e] > t:
                t, p = free[e], (last[e], True)
            for d, gp in ds:
                if end[d] + gp > t:
                    t, p = end[d] + gp, (d, False)
            end[i] = free[e] = t + c
            last[e], prev[i] = i, p
            if t + c + q > top:
                top, tail = t + c + q, i
        for e in range(len(free)):
            if free[e] + rest[e] > top:
                top, tail = free[e] + rest[e], last[e]
        while tail is not None and prev[tail] is not None:
            if prev[tail][1] and prev[tail][0] is not None:
                pairs.append((prev[tail][0], tail))
            tail = prev[tail][0]
        mean = sum(end) / len(end)
        state.append((end, frees, tops, mean, prev, ends))
        spans.append(top + 0.1 * mean)
    return state, pairs, spans


def tails(w, loc):
    out = []
    for row, free0, rest, past in loc:
        back, full, own = list(rest), [0.0] * len(row), [r[4] for r in row]
        for i in reversed(w):
            e, c, ds, t, q = row[i]
            x = own[i]
            if back[e] > x:
                x = back[e]
            x = full[i] = back[e] = x + c
            for d, gp in ds:
                if x + gp > own[d]:
                    own[d] = x + gp
        out.append((full, own))
    return out


def improve(ops, order, cfg):
    (tabs, alts), n, width, passes = tables(ops, cfg), len(ops), cfg["width"], cfg["passes"]
    succ = [[[] for i in range(n)] for t in tabs]
    for t, s in zip(tabs, succ):
        for i in range(n):
            for d, gp in t[i][2]:
                s[d].append((i, gp))
    head = len([o for o in ops if o["kind"] == "d" and not o["r"]])
    base = [span(order, t)[0] / m["weight"] for t, m in zip(tabs, COSTS)]
    rng = np.random.default_rng(cfg["seed"])
    order = list(order)
    best, keep = 1e9, None
    for ps in range(passes):
        hot = cfg["heat"] * cfg["cool"] ** (ps / passes) * (ps < passes - 2)
        start = span(order, tabs[1])[1]
        order[head:] = sorted(order[head:], key=lambda i: start[i])
        for lo in range(head - int(rng.integers(width // 2)), n - width // 4, width // 2):
            a, b = max(lo, head), min(n, lo + width)
            ids = order[a:b]
            m, at, loc = len(ids), {x: k for k, x in enumerate(ids)}, []
            for t, s in zip(tabs, succ):
                row, free, rest, past = window(t, s, order, a, b)
                loc.append(([(QUEUES.index(row[i][0]), row[i][1], [(at[d], g) for d, g in row[i][2]]) + row[i][3:] for i in ids],
                            [free.get(e, 0.0) for e in QUEUES], [rest.get(e, -1e9) for e in QUEUES], past))
            eng = [r[0] for r in loc[0][0]]
            near = {-1: [[d for d, g in r[2]] for r in loc[0][0]], 1: [[] for i in ids]}
            for i, ds in enumerate(near[-1]):
                for d in ds:
                    near[1][d].append(i)
            win, pairs, low, s, state = list(range(m)), None, 1e9, 0, None
            flex = [k for k, i in enumerate(ids) if len(alts[0][i]) > 1]

            def move(i, e):
                eng[i] = e
                for x, al in zip(loc, alts):
                    x[0][i] = (e, al[ids[i]][QUEUES[e]]) + x[0][i][2:]

            for r0, r1, r2, r3 in rng.random((cfg["moves"], 4)).tolist() + [[2.0] * 4]:
                if pairs is None:
                    state, pairs, spans = trace(win, loc, s, state)
                    parts = [x / y for x, y in zip(spans, base)]
                    cur, pos, tl = sum(parts), [0] * m, None
                    if cur < low:
                        low, good = cur, (win, list(eng))
                    for k, x in enumerate(win):
                        pos[x] = k
                if r0 > 1.0:
                    break
                limit = [cur + hot * r3 - sum(parts[k + 1:]) + 0.004 * len(parts[k + 1:]) for k in range(len(parts))]
                if r0 < cfg["put"]:
                    tl = tl or tails(win, loc)
                    i = pairs[int(r1 * len(pairs))][int(r2 * 2)] if pairs and r0 < cfg["put"] / 2 else win[int(r1 * m)]
                    first = max([pos[d] for d in near[-1][i]] + [-1])
                    final = min([pos[d] for d in near[1][i]] + [m])
                    ready = [max([x[0][i][3]] + [st[0][d] + gp for d, gp in x[0][i][2]]) for x, st in zip(loc, state)]
                    pick = None
                    for name in alts[0][ids[i]] or [QUEUES[eng[i]]]:
                        e = QUEUES.index(name)
                        line = [None] + [x for x in win if eng[x] == e and x != i] + [None]
                        cost = [al[ids[i]].get(name, x[0][i][1]) for x, al in zip(loc, alts)]
                        for p, x in zip(line, line[1:]):
                            lo2, hi2 = (pos[p] if p is not None else -1), (pos[x] if x is not None else m)
                            if lo2 >= final or hi2 <= first or (e == eng[i] and lo2 < pos[i] < hi2):
                                continue
                            val = hot * 0.3 * ((lo2 * 0.618 + r3 * 7) % 1.0)
                            for k in range(len(loc)):
                                t = max(ready[k], state[k][0][p] if p is not None else loc[k][1][e]) + cost[k]
                                val += (t + max(tl[k][1][i], tl[k][0][x] if x is not None else loc[k][2][e])) / base[k]
                            if pick is None or val < pick[0]:
                                pick = (val, e, max(lo2, first))
                    if pick:
                        old, k, p = eng[i], pick[2], pos[i]
                        new = win[:k + 1] + [i] + win[k + 1:p] + win[p + 1:] if k < p else win[:p] + win[p + 1:k + 1] + [i] + win[k + 1:]
                        if pick[1] != old:
                            move(i, pick[1])
                        s = min(k + 1, p)
                        if fits(new, s, loc, base, state, limit):
                            win, pairs = new, None
                        elif pick[1] != old:
                            move(i, old)
                    continue
                r0 = (r0 - cfg["put"]) / (1.0 - cfg["put"])
                if flex and r0 > 1.0 - cfg["flip"]:
                    i = flex[int(r1 * len(flex))]
                    other, old = [QUEUES.index(e) for e in alts[0][ids[i]] if QUEUES.index(e) != eng[i]], eng[i]
                    move(i, other[int(r2 * len(other))])
                    s = pos[i]
                    if fits(win, s, loc, base, state, limit):
                        pairs = None
                    else:
                        move(i, old)
                    continue
                if pairs and r0 < 0.6:
                    u, w = pairs[int(r1 * len(pairs))]
                    i, way = (w, -1) if r0 < 0.3 else (u, 1)
                    k, hops = (pos[u] if way < 0 else pos[w]), int(r2 * r2 * 6)
                else:
                    i, way = win[int(r1 * m)], (-1 if r0 < 0.8 else 1)
                    k, hops = pos[i], 1 + int(r2 * r2 * 8)
                j, p = k, pos[i]
                while hops and 0 <= j + way < m:
                    j += way
                    if eng[win[j]] == eng[i]:
                        k, hops = j, hops - 1
                grp, stack = {i}, [i]
                while stack:
                    for y in near[way][stack.pop()]:
                        if y not in grp and (pos[y] - k) * way <= 0:
                            grp.add(y)
                            stack.append(y)
                s, e = min(k, p), max(k, p) + 1
                one, two = [x for x in win[s:e] if x in grp], [x for x in win[s:e] if x not in grp]
                if two:
                    new = win[:s] + (one + two if way < 0 else two + one) + win[e:]
                    if fits(new, s, loc, base, state, limit):
                        win, pairs = new, None
            if ps == passes - 1 or cur >= low + hot:
                win, eng = good
            order[a:b] = [ids[k] for k in win]
            for k in flex:
                for t, al in zip(tabs, alts):
                    t[ids[k]] = (QUEUES[eng[k]], al[ids[k]][QUEUES[eng[k]]]) + t[ids[k]][2:]
        spans = [span(order, t)[0] for t in tabs]
        x = sum(s / bs for s, bs in zip(spans, base))
        if x < best:
            best, keep = x, (list(order), [r[0] for r in tabs[0]], [round(s) for s in spans])
    for o, e in zip(ops, keep[1]):
        if "alts" in o:
            o["eng"], (o["emit"], o["cost"]) = e, o["alts"][e]
    return keep[0], keep[2]


def waits(ops, order, arrive):
    done, known, pos = {}, {}, {x: k for k, x in enumerate(order)}
    for i in order:
        o = ops[i]
        if o["kind"] == "t":
            continue
        if o["kind"] == "c":
            done[o["eng"]] = done.get(o["eng"], 0) + 1
            o["mark"] = ("c" + o["eng"], done[o["eng"]])
        elif o["kind"] == "d":
            o["mark"] = (o["sem"], 16)
        elif o["kind"] == "a":
            o["mark"] = ("arr%d" % o["emit"], arrive[o["emit"]])
            o["know"] = {}
            continue
        kn = known.setdefault(o["eng"], {})
        o["wait"] = []
        for d in sorted(o["dep"], key=lambda d: -pos[d]):
            s, n = ops[d]["mark"]
            if kn.get(s, 0) < n:
                o["wait"].append((s, n))
                kn[s] = n
                for s2, n2 in ops[d]["know"].items():
                    kn[s2] = max(kn.get(s2, 0), n2)
        o["know"] = dict(kn)


PLAN = {}


def plan(arrive):
    if arrive not in PLAN:
        ops = build(CFG)
        depend(ops)
        order = improve(ops, schedule(ops, CFG), CFG)[0]
        waits(ops, order, arrive)
        PLAN[arrive] = (ops, order)
    return PLAN[arrive]


def rank_program(g, core, T, topo):
    rank = T.rank_of(core)
    if rank is None:
        return
    nxt = T.cores[(rank + 1) % len(T.cores)]
    rid, pid = topo.addr(nxt)[:2]
    engines = topo.engines(core, nxt)
    n = len(engines) // 2
    sets = [(engines[:n], engines[n:])] + [(engines, engines)] * (ROUNDS - 1)
    arrive = tuple(len(a) + len(b) for a, b in sets)
    ops, order = plan(arrive)
    queue = {"V": g.vector, "S": g.scalar, "P": g.tensor, "G": g, "Y": g.sync}

    def pass_on(h):
        qa, sa, qz, sz = [T["%s%d" % (k, h)] for k in ("qa", "sa", "qz", "sz")]
        arr, (ma, mb) = T.sem["arr%d" % h], [sum(1 << e for e in s) for s in sets[h]]
        g.remote_dma(qz[:, 128:192].bitcast(dt.uint8), qa[:, 0:64].bitcast(dt.uint8), arr, T.sem.sent, pid, rid, ma)
        g.remote_dma(sz[:, 128:192], sa[:, 0:64], arr, T.sem.sent, pid, rid, mb)

    for i in order:
        o = ops[i]
        if o["kind"] in "at":
            continue
        q = queue[o["eng"]]
        for s, k in o["wait"]:
            q.wait_ge(T.sem[s], k)
        if o["kind"] == "r":
            pass_on(o["emit"])
        else:
            o["emit"](g, T).then_inc(T.sem[o["mark"][0]], 1 if o["kind"] == "c" else 16)
    total = {"sent": sum(arrive)}
    for o in ops:
        if o["kind"] in "cd":
            total[o["mark"][0]] = max(total.get(o["mark"][0], 0), o["mark"][1])
    for s, k in total.items():
        g.wait_ge(T.sem[s], k)
